import numpy as np, ml_dtypes
CORES = [1,5,17,21,33,37,49,53]
N = 8
BF = ml_dtypes.bfloat16
def gentries(a):
    return np.ascontiguousarray(a.reshape(8, 16, -1).transpose(0, 2, 1)).reshape(8, -1)
def gtable(e):
    e = np.asarray(e); return np.ascontiguousarray(e.reshape(8, -1, 16).transpose(0, 2, 1)).reshape(128, -1).astype(np.int32)
F, STEP, CAPP, V, R, D = 6144, 256, 128, 2048, 2, 2
def aim(rng, s):
    p = rng.integers(1, 64, F); o = rng.permutation(F); k = s - int(np.sum(p)); room = (63 - p if k > 0 else p - 1)[o]
    p[o] += np.sign(k) * np.clip(abs(k) - (np.add.accumulate(room) - room), 0, room)
    return p
def rise(rng):
    top = N * CAPP * STEP + int(rng.integers(62, STEP + 1)); lo, hi, best = F, N * CAPP * STEP, -1
    for k in range(20):
        s = (lo + hi) // 2 if k else F; v = aim(rng, s); z = v.copy()
        for a in range(R - 1):
            z[np.flatnonzero(np.diff(np.add.accumulate(z) // STEP, prepend=0))] = 63
        u = int(np.sum(z))
        if u >= top: hi = s
        else:
            lo = s
            if u > best: best, p, last = u, v, z
    total = np.concatenate([np.zeros(1, np.int64), np.add.accumulate(last)]) + 63 * (F - np.arange(F + 1))
    p[np.flatnonzero(total < top)[0]:] = 63
    return p
def links(rng):
    lab = rng.integers(0, rng.integers(8, 257), F); o = np.argsort(lab, kind="stable"); b, c = o[:-1], o[1:]
    on = (lab[b] == lab[c]) & (rng.random(F - 1) > 0.05); v = np.stack([np.arange(F), np.arange(F)])
    v[0, c[on]] = b[on]; v[1, b[on]] = c[on]
    return v
def whole(rng, m, *shape):
    return rng.integers(-m, m + 1, shape).astype(np.float32).astype(BF)
def draw(rng, lo, hi):
    v = np.stack([np.stack([links(rng) for g in range(8)]) for r in range(N)]).astype(np.int32)
    return {"x": whole(rng, 8, N, 128, F), "prv": np.ascontiguousarray(v[:, :, 0]), "nxt": np.ascontiguousarray(v[:, :, 1]), "key": rng.integers(0, V, (N, 8, F)).astype(np.int32), "rw": rng.integers(-255, 256, (N, 8, F)).astype(np.int32),
            "pri": np.stack([gtable(np.stack([aim(rng, int(rng.integers(lo * F, hi * F))) for g in range(8)])) for r in range(N)]), "w": whole(rng, 4, N, 128, 2 * D + 1), "val": whole(rng, 8, N, 128, V)}
def put(d, r, g, p):
    e = gentries(d["pri"][r]); e[g] = p; d["pri"][r] = gtable(e)
def setup_inputs(rng):
    return draw(rng, 24, 34)
def setup_inputs_full(rng):
    d = draw(rng, 24, 34); o = rng.permutation(N); late = rng.random((N, 8)) < 0.2; late[o[1], rng.permutation(8)[:4]] = True; late[o[0]] = False
    m = rng.random((N, 8)) < 0.3; m[o[0]] = True; m = m & ~late
    for r, g in np.argwhere(m):
        put(d, r, g, aim(rng, N * CAPP * STEP + int(rng.integers(0, STEP))))
        d["x"][r, 16 * g:16 * g + 16] = whole(rng, 1, 16, F); d["rw"][r, g] = rng.integers(-60, 61, F)
    for r, g in np.argwhere(late):
        put(d, r, g, rise(rng))
        d["x"][r, 16 * g:16 * g + 16] = 0; d["rw"][r, g] = 340; d["rw"][r, g, 0] = 0
    return d
def setup_inputs_even(rng):
    d = draw(rng, 24, 34)
    for r in range(N):
        d["pri"][r] = gtable(np.repeat(rng.permutation(np.array([16, 16, 16, 32, 32, 32, 32, 32]))[:, None], F, 1))
    return d
def setup_inputs_few(rng):
    d = draw(rng, 24, 34)
    for r in range(N):
        o = rng.permutation(8)[:4]
        for g in o[1:]: d["x"][r, 16 * g:16 * g + 16] = 0
        for g in o[:2]: put(d, r, g, np.ones(F, np.int64))
        for g in o[2:]: put(d, r, g, aim(rng, int(rng.integers(12 * F, 17 * F))))
        d["rw"][r, o[1]] = 0; d["rw"][r, o[2]] = rng.choice(np.array([0, 8, -8, 16, -16, 5, -5]), F); d["rw"][r, o[3]] = rng.choice(np.array([-336, -342, 336, 341, 335, 330]), F)
    return d
def setup_inputs_loose(rng):
    d = draw(rng, 8, 17); d["prv"] = rng.integers(0, F, (N, 8, F)).astype(np.int32); d["nxt"] = rng.integers(0, F, (N, 8, F)).astype(np.int32)
    for n, m in (("x", 8), ("w", 4), ("val", 8)):
        d[n] = (m * (2 * rng.integers(0, 2, d[n].shape) - 1)).astype(np.float32).astype(BF)
    d["rw"] = (1023 * rng.integers(-1, 2, (N, 8, F))).astype(np.int32)
    for r in range(N):
        o = rng.permutation(8)
        d["prv"][r, o[0]] = 0; d["nxt"][r, o[0]] = F - 1; d["prv"][r, o[1]] = np.arange(F); d["nxt"][r, o[1]] = np.arange(F)
        d["prv"][r, o[2]] = (np.arange(F) - 1) % F; d["nxt"][r, o[2]] = (np.arange(F) + 1) % F
        d["key"][r, o[3]] = V - 1; d["key"][r, o[4]] = rng.choice(np.array([0, V - 1]), F)
        d["x"][r, 16 * o[5]:16 * o[5] + 16] = 8
    q = rng.integers(0, N); d["w"][q] = 4; d["val"][q] = 8
    return d
def setup_inputs_spread(rng):
    d = draw(rng, 8, 17)
    for n, m in (("x", F), ("val", V)):
        s = np.left_shift(1, rng.integers(0, 4, (N, 1, m))) * (rng.random((N, 1, m)) > 0.0625)
        d[n] = (rng.integers(-1, 2, (N, 128, m)) * s).astype(np.float32).astype(BF)
    d["w"] = (rng.integers(-4, 5, (N, 128, 2 * D + 1)) * (rng.random((N, 128, 1)) > 0.4)).astype(np.float32).astype(BF)
    d["key"] = np.minimum(rng.random((N, 8, F)) ** 3 * V, V - 1).astype(np.int32)
    d["rw"] = np.right_shift(rng.integers(-1023, 1024, (N, 8, F)), rng.integers(0, 11, (N, 8, F))).astype(np.int32)
    return d
def play(x, prv, nxt, key, rw, pri, w, val):
    X = x.astype(np.float32).reshape(N, 8, 16, F); W = w.astype(np.float32).reshape(N, 8, 16, 2 * D + 1); A = val.astype(np.float32).reshape(N, 8, 16, V)
    P = np.stack([gentries(pri[r]) for r in range(N)]).astype(np.int64); most = 0
    for a in range(R):
        for r in range(N):
            for g in range(8):
                t = np.flatnonzero(np.diff(np.add.accumulate(P[r, g]) // STEP, prepend=0)); most = max(most, len(t))
                q = np.arange(len(t)) % N
                pt = {0: t}
                for k in range(1, D + 1):
                    pt[k] = nxt[r, g][pt[k - 1]]; pt[-k] = prv[r, g][pt[1 - k]]
                h = np.zeros((len(t), 16), np.float32)
                for k in range(-D, D + 1):
                    h += W[q, g, :, D + k] * X[r, g][:, pt[k]].T
                e = np.sum(A[q, g, :, key[r, g][t]] * h, axis=1) + (rw[r, g][pt[0]] + rw[r, g][pt[1]] + rw[r, g][pt[2]])
                P[r, g, t] = np.minimum(np.maximum(np.abs(e).astype(np.int64) >> 4, 1), 63)
    return P, most
def check_inputs(d):
    bad = []
    for n, lo, hi in (("x", -8, 8), ("prv", 0, F - 1), ("nxt", 0, F - 1), ("key", 0, V - 1), ("rw", -1023, 1023), ("pri", 1, 63), ("w", -4, 4), ("val", -8, 8)):
        v = np.asarray(d[n]).astype(np.float32)
        if not (np.isfinite(v).all() and (v == np.floor(v)).all() and v.min() >= lo and v.max() <= hi): bad.append(n)
    if not bad and play(**d)[1] > N * CAPP: bad.append("CAPP")
    return bad
def reference(x, prv, nxt, key, rw, pri, w, val):
    P, most = play(x, prv, nxt, key, rw, pri, w, val)
    y = np.stack([gtable(P[r]) for r in range(N)])
    return {"y": y.astype(np.float32)}

@@ -1,0 +1,448 @@
+from concourse.bass import DstId, RemoteDMATransfer
+from concourse.mybir import AluOpType as A, ActivationFunctionType as AF
+
+N, F, C, K, V, NSIM = 8, 6144, 384, 1024, 2048, 64
+SCRATCH = {}
+for _dt, _bufs in (
+    ("bfloat16", dict(XS=F, TB=F, VA=N * V, HS=1024, HB=3072, DG=8 * C, WL=40, DI=40 * 128, CA=C, CB=C, CT=C, B15=144,
+                      EF=3 * 144, ET=160, ES=6 * 128, Ib=128, LR=128, LC=128, ZS=C, W0=2848, W1=2848,
+                      G0=K, GN1=K, GP1=K, GN2=K, X0=K, X1=K, X2=K, X3=K, X4=K, VG=K)),
+    ("float16", dict(ON=128, TG=128, TR=128, EK=144, L1=136, L2=136, LZ=136, Ih=128, SH=128, Dm=128, Dn=128,
+                     PH=C, YH=C, RH=C, GE=4 * C, PR=K, GG=4 * C)),
+    ("float32", dict(WF=40, cf=8, cm=8, XF=192, OB=128, D2i=24, D2=24, OH=16, M4=4, MT=4, Mle=4, Mgt=4,
+                     ua=24, ub=24, uc=24, ud=24, AE=1032, YO=C)),
+    ("int32", dict(TI=4 * C, PI=C, ci=8, NI=C)),
+    ("uint16", dict(US=24, UR=96, oT=64, oN1=64, oP1=64, oN2=64, oP2=64, oK=64)),
+):
+    for _n, _w in _bufs.items():
+        SCRATCH[_n] = ("sbuf", [128, _w], _dt)
+SCRATCH["KH"] = ("sbuf", [128, 25, 16], "float16")
+for _k in range(8):
+    SCRATCH["B%d" % _k] = ("psum", [128, 512], "float32")
+SEMAPHORES = ["cV", "cS", "cP", "cG", "dP", "dW", "dT0", "dT1", "dT2", "dT3", "dX", "dV", "dR", "dY",
+              "loc", "aw", "av", "ah", "a0", "a1", "a2"]
+
+
+def blk(t, k, n, m=1):
+    return t[:, n * k:n * (k + m)]
+
+
+def plan(T, topo):
+    cores, out = list(T.cores), []
+    chips = sorted(set(topo.chip(c) for c in cores))
+    for r, c in enumerate(cores):
+        mate = [k for k in range(NSIM) if topo.mates(topo.chip(c), topo.chip(k)) and topo.die(k) == topo.die(c)]
+        here = [k for k in topo.cores_of(c) if topo.die(k) == topo.die(c) and k != c]
+        own = [k for k in here if topo.may_write(k, mate[0])]
+        i = chips.index(topo.chip(c))
+        sets = [[q for q in range(N) if topo.chip(cores[q]) == chips[(i + k) % len(chips)]] for k in range(len(chips))]
+        out.append(dict(core=c, E=[k for k in here if k not in own][0], O=own[0], F=own[1],
+                        M=[k for k in mate if topo.may_write(k, c)], pair=sets[0], far=sets[1:],
+                        sib=[q for q in sets[0] if q != r][0],
+                        to=[[q for q in s if topo.die(cores[q]) == topo.die(c)][0] for s in sets[1:]]))
+    return out
+
+
+def sender(g, core, T, topo):
+    total = [0]
+
+    def send(trs):
+        out = []
+        for s, ds, cs, es, sm in trs:
+            ids = [DstId(rid=topo.addr(c)[0], pnc=topo.addr(c)[1]) for c in cs]
+            out.append(RemoteDMATransfer(dst_ids=ids, dma_engine_mask=sum(1 << e for e in es), remote_sem=T.sem[sm],
+                                         srcs=[s], dsts=ds))
+            total[0] += len(es)
+        g.remote_dma_fused(out, local_sem=T.sem.loc)
+    return send, total
+
+
+def helper_program(g, core, T, topo, pl):
+    send, total = sender(g, core, T, topo)
+    for r, p in enumerate(pl):
+        e_on = topo.engines(core, [k for k in topo.cores_of(core) if k != core][0])
+        e_off = topo.engines(core, pl[p["to"][0]]["core"])
+        e_rest, hf = [e for e in e_on if e not in e_off], len(e_off) // 2
+        both = [pl[q]["core"] for q in p["pair"]]
+        src = [[q for q in range(N) if pl[q]["to"][j] == r][0] for j in range(3)]
+        if core in (p["E"], p["O"], p["F"]):
+            w = blk(T.WL, r, 5)
+            g.wait_ge(T.sem.aw, len(e_on))
+            send([(w, [w, w], [pl[q]["core"] for q in p["far"][(p["E"], p["O"], p["F"]).index(core)]], e_off, "aw")])
+        if core in (p["E"], p["O"]):
+            h = int(core == p["O"])
+            g.wait_ge(T.sem.ah, len(e_on) // 2)
+            for j, q in enumerate(p["to"]):
+                if h == 0:
+                    trs = [(T.HS[:], [blk(T.HB, j, 1024)], [pl[q]["F"]], e_off, "a%d" % j)]
+                else:
+                    trs = [(blk(T.HS, m, 512), [blk(T.HB, j, 512)], [pl[q]["M"][m]], e_off[hf * m:hf * m + hf], "a%d" % j)
+                           for m in range(2)]
+                send(trs)
+                if j == 0:
+                    send([(T.HS[:], [blk(T.VA, 2 * r + h, 1024)], [pl[p["sib"]]["core"]], e_rest, "av")])
+        if core == p["F"]:
+            for j in range(3):
+                g.wait_ge(T.sem["a%d" % j], len(e_off))
+                d = blk(T.VA, 2 * src[j], 1024)
+                send([(blk(T.HB, j, 1024), [d, d], both, e_on, "av")])
+        if core in p["M"]:
+            for j in range(3):
+                g.wait_ge(T.sem["a%d" % j], hf)
+                d = blk(T.VA, 4 * src[j] + 2 + p["M"].index(core), 512)
+                send([(blk(T.HB, j, 512), [d, d], both, e_off, "av")])
+    if total[0]:
+        g.wait_ge(T.sem.loc, total[0])
+
+
+def rank_program(g, core, T, topo):
+    me, pl = T.rank_of(core), plan(T, topo)
+    if me is None:
+        return helper_program(g, core, T, topo, pl)
+    Q = {"V": g.vector, "S": g.scalar, "P": g.tensor, "G": g, "Y": g.sync}
+    cnt = {"V": 0, "S": 0, "P": 0, "G": 0}
+    waited = {e: {} for e in Q}
+    lastw, readers, bank = {}, {}, {}
+    vec, act = g.vector, g.scalar
+
+    def wait(e, s, v):
+        if waited[e].get(s, 0) < v:
+            Q[e].wait_ge(T.sem[s], v)
+            waited[e][s] = v
+
+    def before(e, r, w):
+        r, w, need, toks = r.split(), w.split(), {}, []
+        for k in r + w:
+            if k in lastw:
+                toks.append(lastw[k])
+            toks.extend(t for f, t in bank.get(k, {}).items() if f != e)
+        for k in w:
+            toks.extend(readers.get(k, []))
+        for s, v in toks:
+            if not (e == "P" and s == "cP"):
+                need[s] = max(need.get(s, 0), v)
+        for s, v in need.items():
+            wait(e, s, v)
+
+    def after(e, tok, r, w):
+        r, w = r.split(), w.split()
+        for k in r:
+            readers.setdefault(k, []).append(tok)
+        for k in w:
+            lastw[k] = tok
+            readers[k] = []
+        for k in r + w:
+            if k[0] == "B" and len(k) == 2:
+                bank.setdefault(k, {})[e] = tok
+
+    def op(e, fn, r, w):
+        before(e, r, w)
+        cnt[e] += 1
+        fn().then_inc(T.sem["c" + e], 1)
+        after(e, ("c" + e, cnt[e]), r, w)
+
+    def dma(out, in_, sem, val, r, w):
+        before("Y", r, w)
+        g.sync.dma_start(out, in_).then_inc(T.sem[sem], 16)
+        after("Y", (sem, val), r, w)
+
+    def mm(items, r, w):
+        def fn():
+            for it in items[:-1]:
+                g.tensor.matmul(*it)
+            return g.tensor.matmul(*items[-1])
+        op("P", fn, r, w)
+
+    def group(out, pairs):
+        return [(out, l, x, i == 0, i == len(pairs) - 1) for i, (l, x) in enumerate(pairs)]
+
+    def ts(out, in0, s1, o0, r, w, s2=None, o1=None):
+        if o1 is None:
+            op("V", lambda: vec.tensor_scalar(out, in0, s1, None, o0), r, w)
+        else:
+            op("V", lambda: vec.tensor_scalar(out, in0, s1, s2, o0, o1), r, w)
+
+    def tt(out, a, b, o, r, w):
+        op("V", lambda: vec.tensor_tensor(out, a, b, o), r, w)
+
+    def cp(out, a, r, w):
+        op("V", lambda: vec.tensor_copy(out, a), r, w)
+
+    def ms(out, c, w):
+        op("V", lambda: vec.memset(out, c), "", w)
+
+    def sc(out, a, r, w, scale=1.0, func=AF.Copy):
+        op("S", lambda: act.activation(out, a, func, scale=scale), r, w)
+
+    def iota(out, pat, base, cm, w):
+        op("G", lambda: g.iota(out, pat, base, cm, allow_small_or_imprecise_dtypes=True), "", w)
+
+    def bk(k):
+        return T["B%d" % k]
+
+    p = pl[me]
+    send, total = sender(g, core, T, topo)
+    e_on = topo.engines(core, p["E"])
+    n_on, n_off = len(e_on), len(topo.engines(core, pl[p["to"][0]]["core"]))
+
+    wme = blk(T.WL, me, 5)
+    dma(wme, T.w[:], "dW", 16, "", "wme")
+    dma(T.PI[:], T.pri[:], "dP", 16, "", "PI")
+    dma(blk(T.VA, me, V), T.val[:], "dV", 16, "", "Vme")
+    for k, tab in enumerate([T.key, T.nxt, T.prv, T.rw]):
+        dma(blk(T.TI, k, C), tab[:], "dT%d" % k, 16, "", "TI%d" % k)
+
+    pc = T.ci[:, 5:6]
+    iota(pc, [[0, 1]], 0, 1, "ci5")
+    iota(T.OB[:], [[16, 8], [0, 16]], 0, 0, "OB")
+    iota(T.XF[:], [[1, 192]], -32, 0, "XF")
+    iota(T.CA[:], [[256, 24], [0, 16]], 0, 0, "CA")
+    before("G", "wme", "")
+    send([(wme, [wme] * 4, [p["E"], p["O"], p["F"], pl[p["sib"]]["core"]], e_on, "aw")])
+    lastw["WL"] = ("aw", n_on + 6 * n_off)
+    iota(T.D2i[:], [[16, 24]], 512, 0, "D2i")
+    before("G", "Vme", "")
+    send([(blk(T.VA, 2 * me + h, 1024), [T.HS[:]], [p["EO"[h]]], e_on[n_on // 2 * h:n_on // 2 * (h + 1)], "ah")
+          for h in range(2)])
+    lastw["VA"] = ("av", 2 * (n_on - n_off) + 6 * n_on + 12 * n_off)
+    iota(T.CB[:], [[0, 24], [16, 16]], 0, 0, "CB")
+    iota(T.W0[:, 0:1040], [[0, 1040]], 0, 0, "W0")
+    iota(T.AE[:, K:1032], [[0, 8]], 0, 0, "AEp")
+    iota(T.W1[:, 0:1040], [[0, 1040]], 0, 0, "W1")
+
+    ms(T.TB[:, 0:1536], 0.0, "TBa")
+    sc(T.TB[:, 1536:3072], T.TB[:, 0:1536], "TBa", "TBb")
+    sc(T.TB[:, 3072:F], T.TB[:, 0:3072], "TBa TBb", "TBc")
+    ts(T.ci[:, 0:1], pc, 15, A.bitwise_and, "ci5", "ci0")
+    ts(T.ci[:, 1:2], pc, 15, A.bitwise_and, "ci5", "ci1", 1, A.logical_shift_right)
+    ts(T.ci[:, 2:3], pc, 3, A.bitwise_and, "ci5", "ci2")
+    ts(T.ci[:, 3:4], pc, 15, A.bitwise_and, "ci5", "ci3", 2, A.logical_shift_right)
+    ts(T.ci[:, 4:5], pc, 112, A.bitwise_and, "ci5", "ci4")
+    ts(T.ci[:, 6:7], pc, 7, A.bitwise_and, "ci5", "ci6")
+    cp(T.cf[:, 0:7], T.ci[:, 0:7], "ci0 ci1 ci2 ci3 ci4 ci5 ci6", "cf")
+    ca, ca2, cr, cty, cgb, cpp, cq = [T.cf[:, k:k + 1] for k in range(7)]
+    x4, x128, oh0, oh15 = T.XF[:, 32:36], T.XF[:, 32:160], T.OH[:, 0:1], T.OH[:, 15:16]
+    ts(T.ON[:], T.OB[:], cgb, A.is_equal, "OB cf", "ON", 1.0 / 256, A.mult)
+    ts(T.TG[:], x128, cpp, A.is_ge, "XF cf", "TG")
+    ts(T.OH[:], T.XF[:, 32:48], ca, A.is_equal, "XF cf", "OH")
+    ts(T.B15[:], T.XF[:, 17:161], cgb, A.is_equal, "XF cf", "B15")
+    tt(T.TR[:], T.TG[:], T.ON[:], A.mult, "TG ON", "TR")
+    ts(T.EK[:], T.B15[:], oh0, A.mult, "B15 OH", "EK")
+    ms(T.B2[:, 0:400], -2048.0, "B2")
+
+    def mid_constants():
+        ts(T.cm[:, 0:1], oh15, 16.0, A.mult, "OH", "cm0", -1.0, A.add)
+        tt(T.L1[:, 0:132], T.B15[:, 8:140], T.B15[:, 4:136], A.add, "B15", "L1")
+        tt(T.cm[:, 1:2], cgb, cr, A.add, "cf", "cm1")
+        ts(T.L2[:, 0:132], T.B15[:, 12:144], T.cm[:, 0:1], A.mult, "B15 cm0", "L2")
+        ts(T.L1[:, 0:132], T.L1[:, 0:132], oh15, A.mult, "L1 OH", "L1")
+        ts(T.ET[:], T.XF[:, 17:177], T.cm[:, 1:2], A.is_equal, "XF cm1", "ET")
+        ts(T.MT[:], x4, cty, A.is_equal, "XF cf", "MT")
+        tt(T.LZ[:, 0:132], T.L1[:, 0:132], T.L2[:, 0:132], A.add, "L1 L2", "LZ")
+        ts(T.M4[:], x4, ca2, A.is_equal, "XF cf", "M4")
+        ts(T.Mle[:], x4, cr, A.is_ge, "XF cf", "Mle")
+        ts(T.Mgt[:], x4, cr, A.is_lt, "XF cf", "Mgt")
+        ts(T.Ib[:], x128, cpp, A.is_equal, "XF cf", "Ib")
+
+    def last_constants():
+        ts(T.cm[:, 3:4], cq, float(V), A.mult, "cf", "cm3")
+        ts(T.cm[:, 2:3], oh15, 0.0, A.is_equal, "OH", "cm2")
+        ts(T.Ih[:], x128, cpp, A.is_equal, "XF cf", "Ih")
+        ts(T.SH[:], T.XF[:, 31:159], cpp, A.is_equal, "XF cf cm2", "SH", T.cm[:, 2:3], A.mult)
+        ts(T.LR[:], T.ON[:], T.M4[:, 3:4], A.mult, "ON M4", "LR")
+        tt(T.Dm[:], T.Ih[:], T.SH[:], A.subtract, "Ih SH", "Dm")
+        ts(T.LC[:], T.ON[:], oh0, A.mult, "ON OH", "LC", -120.0, A.mult)
+        ts(T.Dn[:], T.Dm[:], -64.0, A.mult, "Dm", "Dn")
+
+    def pick_matrices():
+        op("S", lambda: act.activation(T.CA[:], T.CA[:], AF.Identity, bias=T.MT[:, 0:1], scale=T.MT[:, 1:2]), "CA MT", "CA")
+        sc(T.CB[:], T.CB[:], "CB MT", "CB", T.MT[:, 2:3])
+        for s in range(3):
+            sc(blk(T.ES, 2 * s, 128), T.ET[:, s:s + 128], "ET Mle", "ESm%d" % s, T.Mle[:, s:s + 1])
+            sc(blk(T.ES, 2 * s + 1, 128), T.ET[:, 16 + s:144 + s], "ET Mgt", "ESc%d" % s, T.Mgt[:, s:s + 1])
+        for k in range(3):
+            sc(blk(T.EF, k, 144), T.B15[:], "B15 M4", "EF%d" % k, T.M4[:, k:k + 1])
+
+    def diags(e, d, qs=range(N)):
+        for q in qs:
+            o, col, w = blk(T.DI, 8 * d + q, 128), T.WF[:, 5 * q + d:5 * q + d + 1], "DI%d" % (8 * d + q)
+            if e == "S":
+                sc(o, T.Ib[:], "Ib WF", w, col)
+            else:
+                ts(o, T.Ib[:], col, A.mult, "Ib WF", w)
+
+    def tab_float(k):
+        b = "B%d" % (4 + k)
+        cp(bk(4 + k)[:, 0:C], blk(T.TI, k, C), "TI%d" % k, b)
+        sc(blk(T.DG, 2 * k, C), bk(4 + k)[:, 0:C], b, "DG%d" % (2 * k))
+
+    def tab_digits(k):
+        tt(blk(T.DG, 2 * k + 1, C), bk(4 + k)[:, 0:C], blk(T.DG, 2 * k, C), A.subtract,
+           "B%d DG%d" % (4 + k, 2 * k), "DG%d" % (2 * k + 1))
+        for a in (2 * k, 2 * k + 1):
+            dma(T.TB[a:128:16, :], blk(T.DG, a, C), "dR", 128, "DG%d TBa TBb TBc" % a, "TBr%d" % a)
+
+    def pick(b, lo, pairs, r):
+        mm(group(bk(b)[:, lo:lo + 64], pairs), r, "B%d" % b)
+
+    def fam(b, lo, k, src):
+        pick(b, lo, [(T.EF[:, 144 * k + 15 - u:144 * k + 143 - u], T[src][:, u:K:16]) for u in range(16)],
+             "%sa %sb EF%d" % (src, src, k))
+
+    def take(b, lo, name):
+        cp(T[name][:], bk(b)[:, lo:lo + 64], "B%d" % b, name)
+
+    src_of = {"G0": "TB oT", "GN1": "TB oN1", "GP1": "TB oP1", "GN2": "TB oN2", "X0": "XS oP2", "X1": "XS oP1",
+              "X2": "XS oT", "X3": "XS oN1", "X4": "XS oN2", "VG": "VA oK"}
+    also = {"TB": "TBr0", "XS": "XS", "VA": "VA Vme"}
+    nx = [0, 0]
+
+    def hsum(name, h):
+        d, first, last = int(name[1]), nx[h] % 5 == 0, nx[h] % 5 == 4
+        nx[h] += 1
+        mm([(bk(4 + h)[:, q:512:8], blk(T.DI, 8 * d + q, 128), T[name][:, 512 * h + q:512 * h + 512:8], first and q == 0,
+             last and q == 7) for q in range(N)],
+           name + "ab"[h] + " " + " ".join("DI%d" % (8 * d + q) for q in range(N)), "B%d" % (4 + h))
+
+    def ga(e, name, h, now=True):
+        win, off = src_of[name].split()
+        (cp if e == "V" else sc)(blk(T[name], h, 512), T[win][:].indirect(blk(T[off], h, 32)), also[win] + " " + off,
+                                 name + "ab"[h])
+        if win == "XS" and now:
+            hsum(name, h)
+
+    def rw(name, h):
+        mm([(bk(6 + h)[:], T.LR[:], blk(T[name], h, 512), name == "G0", False)], name + "ab"[h] + " LR", "B%d" % (6 + h))
+
+    def errors(h):
+        tt(blk(T.PR, h, 512), bk(4 + h)[:], blk(T.VG, h, 512), A.mult, "B%d VG%s" % (4 + h, "ab"[h]), "PR%d" % h)
+        mm([(bk(6 + h)[:], T.ON[:], blk(T.PR, h, 512), False, True)], "ON PR%d" % h, "B%d" % (6 + h))
+
+    def absolute(h):
+        sc(blk(T.AE, h, 512), bk(6 + h)[:], "B%d" % (6 + h), "AE%d" % h, 16.0, AF.Abs)
+
+    b0, b1, b3 = T.B0[:, 0:C], T.B1[:, 0:C], T.B3[:, 0:C]
+    kex, kin = T.B0[:, 0:48:2], T.B0[:, 1:48:2]
+    cp(T.PH[:], T.PI[:], "PI", "PH")
+    for rd in range(2):
+        W, wk = T["W%d" % rd], "W%d" % rd
+        mm([(b0, T.ON[:], T.PH[:], True, True)], "ON PH", "B0")
+        mm([(b1, T.TR[:], T.PH[:], True, True)], "TR PH", "B1")
+        if rd == 0:
+            mid_constants()
+        op("V", lambda: vec.tensor_tensor_scan(T.B2[:, 1:C + 1], b0, T.PH[:], -2048.0, A.add, A.min), "B0 PH", "B2")
+        ts(T.KH[:], T.B2[:, 0:400], -0.498046875, A.add, "B2", "KH")
+        mm([(T.B0[:, 0:48], T.EK[:, 15 - u:143 - u], T.KH[:, 0:24, u:u + 2], u == 0, False) for u in range(15)] +
+           [(kex, T.EK[:, 0:128], T.KH[:, 0:24, 15], False, False), (kin, T.EK[:, 0:128], T.KH[:, 1:25, 0], False, True)],
+           "EK KH", "B0")
+        if rd == 0:
+            tab_float(0)
+            tab_float(1)
+        tt(T.YH[:], T.B2[:, 0:C], T.KH[:, 0:24, :], A.subtract, "B2 KH", "YH")
+        if rd == 0:
+            tab_digits(0)
+            tab_float(2)
+            tab_digits(1)
+            tab_float(3)
+        tt(T.RH[:], b1, T.YH[:], A.add, "B1 YH", "RH")
+        if rd == 0:
+            tab_digits(2)
+            tab_digits(3)
+            dma(T.XS[:], T.x[:], "dX", 16, "", "XS")
+            pick_matrices()
+        for r in range(4):
+            ts(blk(T.GE, r, C), T.RH[:], float(r + 1), A.is_ge, "RH", "GE%d" % r)
+            mm([(b3, T.LZ[:, 3 - r:131 - r], blk(T.GE, r, C), r == 0, r == 3)], "LZ GE%d" % r, "B3")
+        sc(T.ZS[:], b3, "B3", "ZS")
+        if rd == 0:
+            ts(T.D2[:], T.D2i[:], ca, A.add, "D2i cf", "D2", 2.0, A.mult)
+        ts(T.ua[:], kin, -0.75, A.add, "B0", "ua")
+        tt(T.ub[:], T.ua[:], kex, A.is_lt, "ua B0", "ub")
+        tt(T.uc[:], T.ub[:], T.D2[:], A.mult, "ub D2", "uc")
+        tt(T.ud[:], T.uc[:], kex, A.add, "uc B0", "ud")
+        ts(T.US[:], T.ud[:], 2064.0, A.add, "ud", "US")
+        if rd == 0:
+            tt(T.CT[:], T.CA[:], T.CB[:], A.add, "CA CB", "CT")
+        tt(W[:].indirect(T.US[:]), T.ZS[:], T.CT[:], A.mult, "ZS CT US", wk)
+        pairs = [(T.ET[:, 15 - u:143 - u], W[:, 16 + u:1040:16]) for u in range(13)]
+        for s in range(3):
+            pairs.append((blk(T.ES, 2 * s, 128), W[:, 31 - s:1040:16]))
+            pairs.append((blk(T.ES, 2 * s + 1, 128), W[:, 15 - s:1024:16]))
+        pick(3, 0, pairs, "ET ESm0 ESm1 ESm2 ESc0 ESc1 ESc2 " + wk)
+        if rd == 0:
+            sc(T.WF[:], T.WL[:], "WL wme", "WF")
+            diags("S", 2)
+            diags("S", 3, range(4))
+        for r in range(4):
+            ts(blk(T.UR, r, 24), kex, 2048.0 + r, A.add, "B0", "UR%d" % r)
+        take(3, 0, "oT")
+        ga("V", "G0", 0)
+        ga("S", "G0", 1)
+        fam(2, 448, 1, "G0")
+        fam(3, 0, 2, "G0")
+        if rd == 0:
+            last_constants()
+            diags("S", 4)
+        else:
+            ga("V", "X2", 0, False)
+            ga("S", "X2", 1, False)
+        take(2, 448, "oN1")
+        take(3, 0, "oP1")
+        fam(2, 448, 0, "G0")
+        ga("V", "GN1", 0)
+        ga("S", "GP1", 0)
+        mm([(b1, T.Ih[:], T.PH[:], True, False)] + [(b1, T.Dn[:], blk(T.GE, r, C), False, r == 3) for r in range(4)],
+           "Ih Dn PH GE0 GE1 GE2 GE3", "B1")
+        ga("V", "GN1", 1)
+        ga("S", "GP1", 1)
+        ts(T.oK[:], T.B2[:, 448:512], T.cm[:, 3:4], A.add, "B2 cm3", "oK")
+        fam(3, 0, 1, "GN1")
+        fam(2, 448, 2, "GP1")
+        if rd == 0:
+            diags("V", 3, range(4, 8))
+            diags("V", 1)
+        else:
+            ga("V", "X1", 0, False)
+            ga("S", "X3", 0, False)
+        take(3, 0, "oN2")
+        if rd == 1:
+            ga("V", "VG", 0)
+        take(2, 448, "oP2")
+        if rd == 0:
+            diags("V", 0)
+            order = "SGN20 SGN21 r0 r1 C VX20 SX30 VX10 SX00 VX40 R0 SX21 VX11 SX31 VX41 R1 SX01 VVG0 SVG1 E0 A0"
+        else:
+            order = "HX20 HX10 HX30 r0 SGN20 SX00 VX40 R0 HX21 SX31 VX11 E0 r1 C SVG1 VX41 SGN21 R1 A0 VX01"
+        for it in order.split():
+            if it[0] in "EA":
+                (errors if it[0] == "E" else absolute)(0)
+            elif it[0] == "r":
+                rw("G0", int(it[1]))
+                rw("GN1", int(it[1]))
+            elif it[0] == "R":
+                rw("GN2", int(it[1]))
+            elif it[0] == "H":
+                hsum(it[1:3], int(it[3]))
+            elif it[0] == "C":
+                mm([(T.B3[:, 0:128], T.LC[:], T.CT[:, 0:128], True, False)], "LC CT", "B3")
+                mm([(T.B0[:, 128:C], T.LC[:], T.CT[:, 128:C], True, False)], "LC CT", "B0")
+            else:
+                ga(it[0], it[1:-1], int(it[-1]))
+        errors(1)
+        absolute(1)
+        parts = ((3, 0, 128, T.AE[:, 0:512], "AE0"), (0, 128, C, T.AE[:], "AE0 AE1 AEp"))
+        for b, lo, hi, win, keys in parts:
+            for r in range(4):
+                gg, key = T.GG[:, C * r + lo:C * r + hi], "GG%d%d" % (b, r)
+                tt(gg, win.indirect(T.UR[:, 24 * r + lo // 16:24 * r + hi // 16]), T.GE[:, C * r + lo:C * r + hi], A.mult,
+                   keys + " UR%d GE%d" % (r, r), key)
+                mm([(bk(b)[:, lo:hi], T.Dm[:], gg, False, r == 3)], "Dm " + key, "B%d" % b)
+        for b, lo, hi, win, keys in parts:
+            ts(T.NI[:, lo:hi], bk(b)[:, lo:hi], 1.0, A.max, "B%d" % b, "NI%d" % b, 63.0, A.min)
+            out = ("PH", "YO")[rd]
+            tt(T[out][:, lo:hi], T.NI[:, lo:hi], T.B1[:, lo:hi], A.max, "NI%d B1" % b, out)
+    dma(T.y[:], T.YO[:], "dY", 16, "YO", "y")
+    wait("G", "loc", total[0])
+    for e in "VSPG":
+        wait("Y", "c" + e, cnt[e])
+    wait("Y", "dY", 16)

@@ -2,25 +2,34 @@ from concourse.bass import DstId, RemoteDMATransfer
 from concourse.mybir import AluOpType as A, ActivationFunctionType as AF
 
 N, F, C, K, V, NSIM = 8, 6144, 384, 1024, 2048, 64
+ZONE, GAP = 1040, 1152
+CHUNKS = ((0, 512), (512, 1024))
+CUT = 128
+AHEAD, DUP, FILL, POS = 2, False, 9, (0, 0, 0, 0)
+LIFT = (0.0, 9216.0, 0.0, 3072.0)
 SCRATCH = {}
 for _dt, _bufs in (
-    ("bfloat16", dict(XS=F, TB=F, VA=N * V, HS=1024, HB=3072, DG=8 * C, WL=40, DI=40 * 128, CA=C, CB=C, CT=C, B15=144,
-                      EF=3 * 144, ET=160, ES=6 * 128, Ib=128, LR=128, LC=128, ZS=C, W0=2848, W1=2848,
-                      G0=K, GN1=K, GP1=K, GN2=K, X0=K, X1=K, X2=K, X3=K, X4=K, VG=K)),
-    ("float16", dict(ON=128, TG=128, TR=128, EK=144, L1=136, L2=136, LZ=136, Ih=128, SH=128, Dm=128, Dn=128,
-                     PH=C, YH=C, RH=C, GE=4 * C, PR=K, GG=4 * C)),
-    ("float32", dict(WF=40, cf=8, cm=8, XF=192, OB=128, D2i=24, D2=24, OH=16, M4=4, MT=4, Mle=4, Mgt=4,
-                     ua=24, ub=24, uc=24, ud=24, AE=1032, YO=C)),
-    ("int32", dict(TI=4 * C, PI=C, ci=8, NI=C)),
-    ("uint16", dict(US=24, UR=96, oT=64, oN1=64, oP1=64, oN2=64, oP2=64, oK=64)),
+    ("bfloat16", dict(XS=F, TB=F, VA=N * V, HS=1024, HB=3072, DG=8 * C, WL=40, DI=40 * 128, CR=C, CT=C, B15=144,
+                      EF=3 * 144, EZ=144, ET=160, ES=6 * 128, NI=128, LC=128, L8=128, LS=128, TRa=128, TRb=128,
+                      BM=128, TG=128, NEG=C, RAMP=C, CC=C, T1=C, CAP=C, Z1=C, ZO=C, PH=16 + C, W=2 * ZONE + 17 * GAP,
+                      cf=8, XF=192, OB=128, D4=128, SM=128, ZZ=ZONE // 2,
+                      G0=K, GP1=K, X0=K, X1=K, X2=K, X3=K, X4=K, VG=K)),
+    ("float16", dict(EK=144, LE=5 * 128, QM=128, SH=128, LE2=128, LE3=128, LQ=128, I64=128, S64=128, Dp=128, D15=128,
+                     BH=128, PR=K + 16, GG=C, GN1=K, GN2=K + 16, LR=5 * 128, EN=144)),
+    ("float32", dict(OH=16, WF=40, cm=16, cs=8, M4=4, Mle=4, Mgt=4, AE=520, YO=C)),
+    ("int32", dict(TI=4 * C, PI=C, ci=8)),
+    ("uint16", dict(OF=48, oT=64, oN1=64, oP1=64, oN2=64, oP2=64, oK=64)),
 ):
     for _n, _w in _bufs.items():
         SCRATCH[_n] = ("sbuf", [128, _w], _dt)
-SCRATCH["KH"] = ("sbuf", [128, 25, 16], "float16")
+SCRATCH["KK"] = ("sbuf", [128, 2, 16 + C], "float16")
+for _n in ("R15", "LA1", "LA2"):
+    SCRATCH[_n] = ("sbuf", [128, 8, 16], "float16")
+SCRATCH["LB"] = ("sbuf", [128, 8, 16], "bfloat16")
 for _k in range(8):
     SCRATCH["B%d" % _k] = ("psum", [128, 512], "float32")
-SEMAPHORES = ["cV", "cS", "cP", "cG", "dP", "dW", "dT0", "dT1", "dT2", "dT3", "dX", "dV", "dR", "dY",
-              "loc", "aw", "av", "ah", "a0", "a1", "a2"]
+SEMAPHORES = ["cV", "cS", "cP", "cG", "dP", "dW", "dT0", "dT1", "dT2", "dT3", "dX", "dV0", "dV1", "dR", "dY",
+              "loc", "out", "aw", "av", "ah0", "ah1", "a0", "a1", "a2", "a3", "a4", "a5"]
 
 
 def blk(t, k, n, m=1):
@@ -62,7 +71,7 @@ def helper_program(g, core, T, topo, pl):
     for r, p in enumerate(pl):
         e_on = topo.engines(core, [k for k in topo.cores_of(core) if k != core][0])
         e_off = topo.engines(core, pl[p["to"][0]]["core"])
-        e_rest, hf = [e for e in e_on if e not in e_off], len(e_off) // 2
+        e_rest = [e for e in e_on if e not in e_off]
         both = [pl[q]["core"] for q in p["pair"]]
         src = [[q for q in range(N) if pl[q]["to"][j] == r][0] for j in range(3)]
         if core in (p["E"], p["O"], p["F"]):
@@ -71,28 +80,113 @@ def helper_program(g, core, T, topo, pl):
             send([(w, [w, w], [pl[q]["core"] for q in p["far"][(p["E"], p["O"], p["F"]).index(core)]], e_off, "aw")])
         if core in (p["E"], p["O"]):
             h = int(core == p["O"])
-            g.wait_ge(T.sem.ah, len(e_on) // 2)
-            for j, q in enumerate(p["to"]):
-                if h == 0:
-                    trs = [(T.HS[:], [blk(T.HB, j, 1024)], [pl[q]["F"]], e_off, "a%d" % j)]
-                else:
-                    trs = [(blk(T.HS, m, 512), [blk(T.HB, j, 512)], [pl[q]["M"][m]], e_off[hf * m:hf * m + hf], "a%d" % j)
-                           for m in range(2)]
-                send(trs)
-                if j == 0:
-                    send([(T.HS[:], [blk(T.VA, 2 * r + h, 1024)], [pl[p["sib"]]["core"]], e_rest, "av")])
-        if core == p["F"]:
-            for j in range(3):
-                g.wait_ge(T.sem["a%d" % j], len(e_off))
-                d = blk(T.VA, 2 * src[j], 1024)
-                send([(blk(T.HB, j, 1024), [d, d], both, e_on, "av")])
+            for i in range(2):
+                s = blk(T.HS, i, 512)
+                g.wait_ge(T.sem["ah%d" % i], len(e_on) // 2)
+                for j, q in enumerate(p["to"]):
+                    trs = [(s, [blk(T.HB, 3 * i + j, 512)], [pl[q]["M"][i] if h else pl[q]["F"]], e_off, "a%d" % (3 * i + j))]
+                    if j == 0:
+                        trs.append((s, [blk(T.VA, 4 * r + 2 * i + h, 512)], [pl[p["sib"]]["core"]], e_rest, "av"))
+                    send(trs)
         if core in p["M"]:
+            i = p["M"].index(core)
             for j in range(3):
-                g.wait_ge(T.sem["a%d" % j], hf)
-                d = blk(T.VA, 4 * src[j] + 2 + p["M"].index(core), 512)
-                send([(blk(T.HB, j, 512), [d, d], both, e_off, "av")])
+                g.wait_ge(T.sem["a%d" % (3 * i + j)], len(e_off))
+                send([(blk(T.HB, 3 * i + j, 512), [blk(T.HB, j, 512)], [p["EO"[i]]], e_off, "a%d" % j)])
+        if core in (p["E"], p["O"], p["F"]):
+            h = int(core != p["F"])
+            for k in range(3 if h else 6):
+                i, j = int(core == p["O"]) if h else k // 3, k % 3
+                g.wait_ge(T.sem["a%d" % k], len(e_off))
+                d = blk(T.VA, 4 * src[j] + 2 * i + h, 512)
+                send([(blk(T.HB, k, 512), [d, d], both, e_rest if h else e_on, "av")])
     if total[0]:
         g.wait_ge(T.sem.loc, total[0])
+
+
+HOP, CYC, PEC, GAT, SCA = 70, 0.83, 0.45, 1.5, 3.5
+
+
+def issue(steps, Q, T):
+    wrote, pieces, read = {}, {}, {}
+    last_dma = None
+    for i, s in enumerate(steps):
+        pre = set()
+        for k in s["r"]:
+            pre.update(wrote.get(k, []))
+        for k in s["w"]:
+            n = k.lstrip("+")
+            if k[0] == "+" and n in pieces and not read.get(n):
+                pre.update(pieces[n])
+            else:
+                old = wrote.get(n, []) + read.get(n, [])
+                pre.update(old)
+                wrote[n], read[n] = [], []
+                pieces.pop(n, None)
+                if k[0] == "+":
+                    pieces[n] = old
+            wrote[n].append(i)
+        for k in s["r"]:
+            read.setdefault(k, []).append(i)
+        pre.discard(i)
+        s["pre"], s["post"], s["behind"] = pre, [], last_dma if s["alt"][0][0] == "Y" else None
+        if s["alt"][0][0] == "Y":
+            last_dma = i
+    for i, s in enumerate(steps):
+        for j in s["pre"]:
+            steps[j]["post"].append(i)
+    for i in reversed(range(len(steps))):
+        s = steps[i]
+        s["chain"] = max([-i if s["early"] else -len(steps)] + [steps[j]["chain"] + 0.01 for j in s["post"]])
+    free, done, order, pipe = {e: 0.0 for e in Q}, {}, [], [0.0]
+    todo = set(range(len(steps)))
+
+    def start(i, e):
+        s = steps[i]
+        return max([free[e]] + [done[j][0] + (0 if e == "P" == done[j][1] else HOP) for j in s["pre"]])
+    while todo:
+        cand = []
+        for i in todo:
+            s = steps[i]
+            if all(j in done for j in s["pre"]) and (s["behind"] is None or s["behind"] in done):
+                t, e, c, fn = min(((start(i, a[0]) + a[2], a[0], a[2], a[1]) for a in s["alt"]), key=lambda x: x[0])
+                cand.append((t - c, -s["chain"], i, e, c, fn))
+        cand.sort(key=lambda x: x[:3])
+        for x in cand:
+            if all(y[3] != x[3] or y[1] >= x[1] or y[0] >= x[0] + x[4] - HOP for y in cand):
+                break
+        else:
+            x = min((y for y in cand if y[3] == cand[0][3]), key=lambda y: y[1])
+        t, _, i, e, c, fn = x
+        free[e] = t + c
+        end = t + c + steps[i]["lat"]
+        if e == "Y":
+            pipe[0] = max(pipe[0], t + 600) + steps[i]["lat"]
+            end = pipe[0] + 600
+        done[i] = (end, e)
+        order.append((t, i, e, fn))
+        todo.remove(i)
+    cnt, tok, waited = {e: 0 for e in "VSPG"}, {}, {e: {} for e in Q}
+
+    def wait(e, sem, v):
+        if waited[e].get(sem, 0) < v:
+            Q[e].wait_ge(T.sem[sem], v)
+            waited[e][sem] = v
+    for t, i, e, fn in order:
+        need = {}
+        for j in steps[i]["pre"]:
+            if not e == "P" == done[j][1]:
+                need[tok[j][0]] = max(need.get(tok[j][0], 0), tok[j][1])
+        for sem, v in need.items():
+            wait(e, sem, v)
+        ins, tok[i] = fn(), steps[i]["tok"]
+        if e == "Y":
+            ins.then_inc(T.sem[tok[i][0]], 16)
+        elif tok[i] is None:
+            cnt[e] += 1
+            ins.then_inc(T.sem["c" + e], 1)
+            tok[i] = ("c" + e, cnt[e])
+    return cnt, wait
 
 
 def rank_program(g, core, T, topo):
@@ -100,82 +194,67 @@ def rank_program(g, core, T, topo):
     if me is None:
         return helper_program(g, core, T, topo, pl)
     Q = {"V": g.vector, "S": g.scalar, "P": g.tensor, "G": g, "Y": g.sync}
-    cnt = {"V": 0, "S": 0, "P": 0, "G": 0}
-    waited = {e: {} for e in Q}
-    lastw, readers, bank = {}, {}, {}
     vec, act = g.vector, g.scalar
+    steps, early = [], [0]
 
-    def wait(e, s, v):
-        if waited[e].get(s, 0) < v:
-            Q[e].wait_ge(T.sem[s], v)
-            waited[e][s] = v
-
-    def before(e, r, w):
-        r, w, need, toks = r.split(), w.split(), {}, []
-        for k in r + w:
-            if k in lastw:
-                toks.append(lastw[k])
-            toks.extend(t for f, t in bank.get(k, {}).items() if f != e)
-        for k in w:
-            toks.extend(readers.get(k, []))
-        for s, v in toks:
-            if not (e == "P" and s == "cP"):
-                need[s] = max(need.get(s, 0), v)
-        for s, v in need.items():
-            wait(e, s, v)
-
-    def after(e, tok, r, w):
+    def step(alt, r, w, lat=0, tok=None):
         r, w = r.split(), w.split()
-        for k in r:
-            readers.setdefault(k, []).append(tok)
-        for k in w:
-            lastw[k] = tok
-            readers[k] = []
-        for k in r + w:
-            if k[0] == "B" and len(k) == 2:
-                bank.setdefault(k, {})[e] = tok
+        banks = [k for k in r if len(k) == 2 and k[0] == "B" and k[1] in "01234567"]
+        steps.append(dict(alt=alt, r=[k for k in r if k not in banks], w=w + banks, lat=lat, tok=tok, early=early[0]))
 
-    def op(e, fn, r, w):
-        before(e, r, w)
-        cnt[e] += 1
-        fn().then_inc(T.sem["c" + e], 1)
-        after(e, ("c" + e, cnt[e]), r, w)
+    def cost(n):
+        return 30 + CYC * max(64, n)
 
-    def dma(out, in_, sem, val, r, w):
-        before("Y", r, w)
-        g.sync.dma_start(out, in_).then_inc(T.sem[sem], 16)
-        after("Y", (sem, val), r, w)
+    def dma(out, in_, sem, val, r, w, kb):
+        step([("Y", lambda: g.sync.dma_start(out, in_), 60)], r, w, 1.6 * kb, (sem, val))
 
-    def mm(items, r, w):
+    def mm(items, r, w, n):
         def fn():
-            for it in items[:-1]:
+            its = items if isinstance(items, list) else items()
+            for it in its[:-1]:
                 g.tensor.matmul(*it)
-            return g.tensor.matmul(*items[-1])
-        op("P", fn, r, w)
+            return g.tensor.matmul(*its[-1])
+        step([("P", fn, PEC * n)], r, w)
 
-    def group(out, pairs):
-        return [(out, l, x, i == 0, i == len(pairs) - 1) for i, (l, x) in enumerate(pairs)]
+    def group(out, pairs, first=True, last=True):
+        return [(out, l, x, first and i == 0, last and i == len(pairs) - 1) for i, (l, x) in enumerate(pairs)]
 
-    def ts(out, in0, s1, o0, r, w, s2=None, o1=None):
+    def ts_alt(out, in0, s1, o0, s2=None, o1=None, n=64):
         if o1 is None:
-            op("V", lambda: vec.tensor_scalar(out, in0, s1, None, o0), r, w)
-        else:
-            op("V", lambda: vec.tensor_scalar(out, in0, s1, s2, o0, o1), r, w)
+            return ("V", lambda: vec.tensor_scalar(out, in0, s1, None, o0), cost(n))
+        return ("V", lambda: vec.tensor_scalar(out, in0, s1, s2, o0, o1), cost(n))
 
-    def tt(out, a, b, o, r, w):
-        op("V", lambda: vec.tensor_tensor(out, a, b, o), r, w)
+    def sc_alt(out, a, scale=1.0, func=AF.Copy, bias=None, n=64):
+        if bias is None:
+            return ("S", lambda: act.activation(out, a, func, scale=scale), cost(n))
+        return ("S", lambda: act.activation(out, a, func, bias=bias, scale=scale), cost(n))
 
-    def cp(out, a, r, w):
-        op("V", lambda: vec.tensor_copy(out, a), r, w)
+    def ts(out, in0, s1, o0, r, w, s2=None, o1=None, n=64):
+        step([ts_alt(out, in0, s1, o0, s2, o1, n)], r, w)
 
-    def ms(out, c, w):
-        op("V", lambda: vec.memset(out, c), "", w)
+    def tt(out, a, b, o, r, w, n=64):
+        step([("V", lambda: vec.tensor_tensor(out, a, b, o), cost(n))], r, w)
 
-    def sc(out, a, r, w, scale=1.0, func=AF.Copy):
-        op("S", lambda: act.activation(out, a, func, scale=scale), r, w)
+    def cp(out, a, r, w, n=64):
+        step([("V", lambda: vec.tensor_copy(out, a), cost(n))], r, w)
 
-    def iota(out, pat, base, cm, w):
-        op("G", lambda: g.iota(out, pat, base, cm, allow_small_or_imprecise_dtypes=True), "", w)
+    def ms(out, c, w, n=64):
+        step([("V", lambda: vec.memset(out, c), cost(n))], "", w)
+
+    def sc(out, a, r, w, scale=1.0, func=AF.Copy, bias=None, n=64):
+        step([sc_alt(out, a, scale, func, bias, n)], r, w)
+
+    def scaled(out, a, col, r, w, n=128):
+        step([ts_alt(out, a, col, A.mult, n=n // 2), sc_alt(out, a, col, n=n)], r, w)
+
+    def line(out, a, mul, add, r, w):
+        step([ts_alt(out, a, mul, A.mult, add, A.add), sc_alt(out, a, mul, AF.Identity, add)], r, w)
+
+    def iota(out, pat, base, cm, w, n):
+        step([("G", lambda: g.iota(out, pat, base, cm, allow_small_or_imprecise_dtypes=True), 130 + 2 * CYC * n)], "", w)
+
+    def select(out, a, pat, o, fill, base, cm, r, w, n=128):
+        step([("G", lambda: g.affine_select(out, a, pat, o, fill, base, cm), 170 + 2 * CYC * n)], r, w)
 
     def bk(k):
         return T["B%d" % k]
@@ -186,263 +265,284 @@ def rank_program(g, core, T, topo):
     n_on, n_off = len(e_on), len(topo.engines(core, pl[p["to"][0]]["core"]))
 
     wme = blk(T.WL, me, 5)
-    dma(wme, T.w[:], "dW", 16, "", "wme")
-    dma(T.PI[:], T.pri[:], "dP", 16, "", "PI")
-    dma(blk(T.VA, me, V), T.val[:], "dV", 16, "", "Vme")
-    for k, tab in enumerate([T.key, T.nxt, T.prv, T.rw]):
-        dma(blk(T.TI, k, C), tab[:], "dT%d" % k, 16, "", "TI%d" % k)
+    dma(wme, T.w[:], "dW", 16, "", "wme", 20)
+    dma(blk(T.VA, 2 * me, 1024), blk(T.val, 0, 1024), "dV0", 16, "", "Vme0", 256)
+    dma(T.PI[:], T.pri[:], "dP", 16, "", "PI", 192)
+    dma(blk(T.VA, 2 * me + 1, 1024), blk(T.val, 1, 1024), "dV1", 16, "", "Vme1", 256)
 
-    pc = T.ci[:, 5:6]
-    iota(pc, [[0, 1]], 0, 1, "ci5")
-    iota(T.OB[:], [[16, 8], [0, 16]], 0, 0, "OB")
-    iota(T.XF[:], [[1, 192]], -32, 0, "XF")
-    iota(T.CA[:], [[256, 24], [0, 16]], 0, 0, "CA")
-    before("G", "wme", "")
-    send([(wme, [wme] * 4, [p["E"], p["O"], p["F"], pl[p["sib"]]["core"]], e_on, "aw")])
-    lastw["WL"] = ("aw", n_on + 6 * n_off)
-    iota(T.D2i[:], [[16, 24]], 512, 0, "D2i")
-    before("G", "Vme", "")
-    send([(blk(T.VA, 2 * me + h, 1024), [T.HS[:]], [p["EO"[h]]], e_on[n_on // 2 * h:n_on // 2 * (h + 1)], "ah")
-          for h in range(2)])
-    lastw["VA"] = ("av", 2 * (n_on - n_off) + 6 * n_on + 12 * n_off)
-    iota(T.CB[:], [[0, 24], [16, 16]], 0, 0, "CB")
-    iota(T.W0[:, 0:1040], [[0, 1040]], 0, 0, "W0")
-    iota(T.AE[:, K:1032], [[0, 8]], 0, 0, "AEp")
-    iota(T.W1[:, 0:1040], [[0, 1040]], 0, 0, "W1")
+    def table(k, r):
+        dma(blk(T.TI, k, C), [T.key, T.nxt, T.prv, T.rw][k][:], "dT%d" % k, 16, r, "TI%d" % k, 192)
+    for k in (1, 2, 3, 0)[:AHEAD]:
+        table(k, "")
+    pc = T.ci[:, 7:8]
+    early[0] = True
+    iota(pc, [[0, 1]], 0, 1, "pc", 1)
+    iota(T.OB[:], [[16, 8], [0, 16]], 0, 0, "OB", 128)
+    iota(T.XF[:], [[1, 192]], -32, 0, "XF", 192)
+    iota(T.cf[:, 6:7], [[1, 1]], 0, 1, "cp", 1)
+    iota(T.D4[:], [[4, 32], [0, 4]], 0, 0, "D4", 128)
+    step([("G", lambda: send([(wme, [wme] * 4, [p["E"], p["O"], p["F"], pl[p["sib"]]["core"]], e_on, "aw")]), 1300)],
+         "wme", "WL", 4500, ("aw", n_on + 6 * n_off))
 
-    ms(T.TB[:, 0:1536], 0.0, "TBa")
-    sc(T.TB[:, 1536:3072], T.TB[:, 0:1536], "TBa", "TBb")
-    sc(T.TB[:, 3072:F], T.TB[:, 0:3072], "TBa TBb", "TBc")
-    ts(T.ci[:, 0:1], pc, 15, A.bitwise_and, "ci5", "ci0")
-    ts(T.ci[:, 1:2], pc, 15, A.bitwise_and, "ci5", "ci1", 1, A.logical_shift_right)
-    ts(T.ci[:, 2:3], pc, 3, A.bitwise_and, "ci5", "ci2")
-    ts(T.ci[:, 3:4], pc, 15, A.bitwise_and, "ci5", "ci3", 2, A.logical_shift_right)
-    ts(T.ci[:, 4:5], pc, 112, A.bitwise_and, "ci5", "ci4")
-    ts(T.ci[:, 6:7], pc, 7, A.bitwise_and, "ci5", "ci6")
-    cp(T.cf[:, 0:7], T.ci[:, 0:7], "ci0 ci1 ci2 ci3 ci4 ci5 ci6", "cf")
-    ca, ca2, cr, cty, cgb, cpp, cq = [T.cf[:, k:k + 1] for k in range(7)]
-    x4, x128, oh0, oh15 = T.XF[:, 32:36], T.XF[:, 32:160], T.OH[:, 0:1], T.OH[:, 15:16]
-    ts(T.ON[:], T.OB[:], cgb, A.is_equal, "OB cf", "ON", 1.0 / 256, A.mult)
-    ts(T.TG[:], x128, cpp, A.is_ge, "XF cf", "TG")
+    def hand_on(i):
+        send([(blk(T.VA, 4 * me + 2 * i + h, 512), [blk(T.HS, i, 512)], [p["EO"[h]]],
+               e_on[n_on // 2 * h:n_on // 2 * (h + 1)], "ah%d" % i) for h in range(2)])
+    step([("G", lambda: hand_on(0), 300)], "Vme0", "gone", 1500, ("loc", 3 * n_on))
+    step([("G", lambda: hand_on(1), 300)], "Vme1", "VA ord", 16000, ("av", 16 * (n_on - n_off) + 12 * n_on))
+    step([("G", lambda: g.sem_inc(T.sem.out, 1), 10)], "Vme0 Vme1 wme", "issued", 0, ("out", 1))
+    early[0] = False
+    for k in (1, 2, 3, 0)[AHEAD:]:
+        table(k, "issued")
+    dma(blk(T.XS, 0, F // 2), blk(T.x, 0, F // 2), "dX", 32, "gone", "+XS", 768)
+
+    iota(T.LB[0:1, :, :], [[0, 32], [5, 4]], 0, 0, "LB", 128)
+    iota(T.LB[0:1, :, 1:4], [[0, 8], [4, 3]], 4, 0, "+LB", 24)
+    iota(T.LB[0:1, :, 6:8], [[0, 16]], 0, 0, "+LB", 16)
+    iota(T.RAMP[0:1, :], [[0, 24], [GAP, 16]], GAP, 0, "RAMP", C)
+    iota(T.CR[:], [[4, C]], 4 - 768, 0, "CR", C)
+    iota(T.SM[:], [[16, 8], [0, 4], [1, 4]], 0, 0, "SM", 128)
+    iota(T.SM[:, 7:128:16], [[16, 8]], 4, 0, "SM", 8)
+    for k, (m, s) in enumerate(((112, 0), (15, 0), (124, 0), (3, 0), (14, 1), (7, 0))):
+        ts(T.ci[:, k:k + 1], pc, m, A.bitwise_and, "pc", "ci%d" % k, s, A.logical_shift_right)
+    cp(T.cf[:, 0:1], T.ci[:, 0:1], "ci0", "cg")
+    cp(T.cf[:, 1:6], T.ci[:, 1:6], "ci1 ci2 ci3 ci4 ci5 cg", "cf")
+    cgb, ca, cq4, cr, ca2, cq, cpp, cp1 = [T.cf[:, k:k + 1] for k in range(8)]
+    x4, x128 = T.XF[:, 32:36], T.XF[:, 32:160]
+    oh = [T.OH[:, k:k + 1] for k in range(16)]
+    cm = [T.cm[:, k:k + 1] for k in range(16)]
     ts(T.OH[:], T.XF[:, 32:48], ca, A.is_equal, "XF cf", "OH")
-    ts(T.B15[:], T.XF[:, 17:161], cgb, A.is_equal, "XF cf", "B15")
-    tt(T.TR[:], T.TG[:], T.ON[:], A.mult, "TG ON", "TR")
-    ts(T.EK[:], T.B15[:], oh0, A.mult, "B15 OH", "EK")
-    ms(T.B2[:, 0:400], -2048.0, "B2")
+    line(cm[0], oh[15], -1.0, 1.0, "OH", "cm0")
+    ms(T.NEG[:], -1024.0, "NEG", 192)
 
-    def mid_constants():
-        ts(T.cm[:, 0:1], oh15, 16.0, A.mult, "OH", "cm0", -1.0, A.add)
-        tt(T.L1[:, 0:132], T.B15[:, 8:140], T.B15[:, 4:136], A.add, "B15", "L1")
-        tt(T.cm[:, 1:2], cgb, cr, A.add, "cf", "cm1")
-        ts(T.L2[:, 0:132], T.B15[:, 12:144], T.cm[:, 0:1], A.mult, "B15 cm0", "L2")
-        ts(T.L1[:, 0:132], T.L1[:, 0:132], oh15, A.mult, "L1 OH", "L1")
-        ts(T.ET[:], T.XF[:, 17:177], T.cm[:, 1:2], A.is_equal, "XF cm1", "ET")
-        ts(T.MT[:], x4, cty, A.is_equal, "XF cf", "MT")
-        tt(T.LZ[:, 0:132], T.L1[:, 0:132], T.L2[:, 0:132], A.add, "L1 L2", "LZ")
-        ts(T.M4[:], x4, ca2, A.is_equal, "XF cf", "M4")
-        ts(T.Mle[:], x4, cr, A.is_ge, "XF cf", "Mle")
-        ts(T.Mgt[:], x4, cr, A.is_lt, "XF cf", "Mgt")
-        ts(T.Ib[:], x128, cpp, A.is_equal, "XF cf", "Ib")
+    early[0] = True
+    ms(T.ZZ[:], 0.0, "ZZ", ZONE // 4)
+    for k in range(0 if DUP else FILL):
+        sc(blk(T.TB, k, 512), T.ZZ[:, 0:512], "ZZ", "+TBb", n=512)
+    early[0] = False
+    for k in range(12 if DUP else FILL, 12):
+        ms(blk(T.TB, k, 512), 0.0, "+TBb", 256)
 
-    def last_constants():
-        ts(T.cm[:, 3:4], cq, float(V), A.mult, "cf", "cm3")
-        ts(T.cm[:, 2:3], oh15, 0.0, A.is_equal, "OH", "cm2")
-        ts(T.Ih[:], x128, cpp, A.is_equal, "XF cf", "Ih")
-        ts(T.SH[:], T.XF[:, 31:159], cpp, A.is_equal, "XF cf cm2", "SH", T.cm[:, 2:3], A.mult)
-        ts(T.LR[:], T.ON[:], T.M4[:, 3:4], A.mult, "ON M4", "LR")
-        tt(T.Dm[:], T.Ih[:], T.SH[:], A.subtract, "Ih SH", "Dm")
-        ts(T.LC[:], T.ON[:], oh0, A.mult, "ON OH", "LC", -120.0, A.mult)
-        ts(T.Dn[:], T.Dm[:], -64.0, A.mult, "Dm", "Dn")
+    def zero(out, n, w):
+        step([("V", lambda: vec.memset(out, 0.0), cost(n // 2)), sc_alt(out, T.ZZ[:, 0:n], n=n)], "ZZ", w)
 
-    def pick_matrices():
-        op("S", lambda: act.activation(T.CA[:], T.CA[:], AF.Identity, bias=T.MT[:, 0:1], scale=T.MT[:, 1:2]), "CA MT", "CA")
-        sc(T.CB[:], T.CB[:], "CB MT", "CB", T.MT[:, 2:3])
-        for s in range(3):
-            sc(blk(T.ES, 2 * s, 128), T.ET[:, s:s + 128], "ET Mle", "ESm%d" % s, T.Mle[:, s:s + 1])
-            sc(blk(T.ES, 2 * s + 1, 128), T.ET[:, 16 + s:144 + s], "ET Mgt", "ESc%d" % s, T.Mgt[:, s:s + 1])
-        for k in range(3):
-            sc(blk(T.EF, k, 144), T.B15[:], "B15 M4", "EF%d" % k, T.M4[:, k:k + 1])
-
-    def diags(e, d, qs=range(N)):
-        for q in qs:
-            o, col, w = blk(T.DI, 8 * d + q, 128), T.WF[:, 5 * q + d:5 * q + d + 1], "DI%d" % (8 * d + q)
-            if e == "S":
-                sc(o, T.Ib[:], "Ib WF", w, col)
-            else:
-                ts(o, T.Ib[:], col, A.mult, "Ib WF", w)
-
-    def tab_float(k):
-        b = "B%d" % (4 + k)
-        cp(bk(4 + k)[:, 0:C], blk(T.TI, k, C), "TI%d" % k, b)
-        sc(blk(T.DG, 2 * k, C), bk(4 + k)[:, 0:C], b, "DG%d" % (2 * k))
-
-    def tab_digits(k):
-        tt(blk(T.DG, 2 * k + 1, C), bk(4 + k)[:, 0:C], blk(T.DG, 2 * k, C), A.subtract,
-           "B%d DG%d" % (4 + k, 2 * k), "DG%d" % (2 * k + 1))
+    def digits(k):
+        b = k % 2
+        ts(bk(b)[:, 0:C], blk(T.TI, k, C), LIFT[k], A.add, "TI%d" % k, "B%d" % b, n=C)
+        sc(blk(T.DG, 2 * k, C), bk(b)[:, 0:C], "B%d" % b, "DG%d" % (2 * k), n=C)
+        tt(blk(T.DG, 2 * k + 1, C), bk(b)[:, 0:C], blk(T.DG, 2 * k, C), A.subtract,
+           "B%d DG%d" % (b, 2 * k), "DG%d" % (2 * k + 1), C)
         for a in (2 * k, 2 * k + 1):
-            dma(T.TB[a:128:16, :], blk(T.DG, a, C), "dR", 128, "DG%d TBa TBb TBc" % a, "TBr%d" % a)
+            for at in (a, a + 8) if DUP else (a,):
+                dma(T.TB[at:128:16, :], blk(T.DG, a, C), "dR", 256 if DUP else 128, "DG%d TBb" % a, "+TBr", 96)
 
-    def pick(b, lo, pairs, r):
-        mm(group(bk(b)[:, lo:lo + 64], pairs), r, "B%d" % b)
+    ms(T.PH[:, 0:16], 128.0, "PHp")
+    ms(T.L8[0:1, :], 1.0 / 128, "L8")
+    ts(T.BM[:], T.OB[:], cgb, A.is_equal, "OB cg", "BM0", 1.0 / 256, A.mult)
+    ts(T.BH[:], T.OB[:], cgb, A.is_equal, "OB cg", "BH")
+    ts(T.TG[:], x128, cpp, A.is_ge, "XF cp", "TG")
+    tt(T.TRa[:], T.TG[:], T.BM[:], A.mult, "TG BM0", "TRa", 256)
+    tt(T.TRb[:], T.BM[:], T.TRa[:], A.subtract, "TRa BM0", "TRb", 256)
+    ts(T.PH[:, 16:], T.PI[:], 128.0, A.add, "PI", "PHa PHb", n=C)
 
-    def fam(b, lo, k, src):
-        pick(b, lo, [(T.EF[:, 144 * k + 15 - u:144 * k + 143 - u], T[src][:, u:K:16]) for u in range(16)],
-             "%sa %sb EF%d" % (src, src, k))
+    scaled(T.KK[:, :, 0:16], T.NEG[:, 0:32], 2.0, "NEG", "KKp", 64)
+    scaled(T.R15[:], T.BH[:], oh[15], "BH OH", "R15")
+    scaled(T.LB[0:1, :, :], T.LB[0:1, :, :], 1.0 / 1024, "LB", "LB")
+    ms(T.LS[0:1, :], 0.0, "LS")
+    ms(T.LS[0:1, 7:128:16], 1.0, "LS")
+    scaled(T.LA2[:], T.R15[:], -5.0, "R15", "LA2")
+    ts(T.B15[:], T.XF[:, 17:161], cgb, A.is_equal, "XF cg", "B15", n=72)
+    line(cm[9], cpp, 1.0, 1.0, "cp", "cm9")
+    ts(T.SH[:], T.D4[:], cm[9], A.is_equal, "D4 cm9 cm0", "SH", cm[0], A.mult)
+    ts(T.QM[:], T.D4[:], cq4, A.is_equal, "D4 cf", "QM")
+    tt(T.LA1[:], T.QM[:], T.SH[:], A.add, "QM SH", "LA1", 256)
+    for lo, hi, a1, a2 in ((1, 4, 4.0, None), (0, 4, None, -4.0), (6, 7, 4.0, -4.0), (7, 8, -32768.0, 32768.0)):
+        for t, a in (("LA1", a1), ("LA2", a2)):
+            if a is not None:
+                scaled(T[t][:, :, lo:hi], T.R15[:, :, lo:hi], a, "R15", "+" + t, 64)
+    scaled(T.EK[:], T.B15[:], oh[15], "B15 OH", "EK", 144)
+    scaled(T.EZ[:], T.B15[:], oh[7], "B15 OH", "EZ", 144)
+    line(cm[1], oh[7], 32768.0, 4.0, "OH", "cm1")
+    ts(cm[6], ca, 3.5, A.is_lt, "cf OH", "cm6", oh[0], A.subtract)
+    line(cm[2], oh[6], 1.0, cm[6], "cm6 OH", "cm2")
+    line(cm[3], oh[6], -2.0, cr, "OH cf", "cm3")
+    ts(cm[4], cm[2], oh[7], A.add, "cm2 OH", "cm4", -1.0, A.add)
+    line(cm[5], cm[3], 1.0, cgb, "cm3 cf", "cm5")
+    for k in range(4):
+        zero(blk(T.W, k, ZONE // 2), ZONE // 2, "+W" if k > 1 else "+Wz")
+    sc(T.CT[:], T.CR[:], "CR cm2 cm4", "CT", cm[2], AF.Identity, cm[4], C)
 
-    def take(b, lo, name):
-        cp(T[name][:], bk(b)[:, lo:lo + 64], "B%d" % b, name)
+    ts(T.Mle[:], x4, cm[3], A.is_ge, "XF cm3", "Mle")
+    ts(T.Mgt[:], x4, cm[3], A.is_lt, "XF cm3", "Mgt")
+    ts(T.ET[:], T.XF[:, 17:177], cm[5], A.is_equal, "XF cm5", "ET", n=80)
+    ts(T.M4[:], x4, ca2, A.is_equal, "XF cf", "M4")
+    for s in range(3):
+        scaled(blk(T.ES, 2 * s, 128), T.ET[:, s:s + 128], T.Mle[:, s:s + 1], "ET Mle", "+ES")
+        scaled(blk(T.ES, 2 * s + 1, 128), T.ET[:, 16 + s:144 + s], T.Mgt[:, s:s + 1], "ET Mgt", "+ES")
+    for k in (1, 2):
+        scaled(blk(T.EF, k, 144), T.B15[:], T.M4[:, k:k + 1], "B15 M4", "EF%d" % k, 144)
+    ts(blk(T.EF, 0, 144), T.B15[:], T.M4[:, 0:1], A.mult, "B15 M4", "EF0", 1.0 / V, A.mult, 72)
+
+    line(cm[7], oh[7], 8.0, cq4, "OH cf", "cm7")
+    ts(cm[8], oh[7], cr, A.add, "OH cf", "cm8", 2048.0, A.add)
+    line(T.cs[:, 0:5], T.XF[:, 32:37], 1.0, cgb, "XF cf", "cs")
+    scaled(T.SH[:, 7:128:16], T.BH[:, 7:128:16], oh[11], "BH OH", "SH", 64)
+    ts(T.LE2[:], T.D4[:], T.cs[:, 0:1], A.is_equal, "D4 cs OH", "LE2", oh[15], A.mult)
+    scaled(T.LE3[:], T.R15[:], -2.0, "R15", "LE3")
+    scaled(T.I64[:], T.BH[:], -64.0, "BH", "I64")
+    select(T.S64[:], T.I64[:], [[1, 128]], A.is_equal, 0.0, -1, -1, "I64", "S64")
+    select(T.Dp[:], T.S64[:], [[1, 128]], A.not_equal, 64.0, 0, -1, "S64", "Dp")
+    select(T.D15[:], T.I64[:], [[1, 128]], A.is_equal, 0.0, 15, -1, "I64", "D15")
+    ts(T.NI[:], x128, cpp, A.is_equal, "XF cp", "NI", -1.0, A.mult)
+    ts(T.LQ[:], T.D4[:], cm[7], A.is_equal, "D4 cm7", "LQ")
+    ms(T.LC[0:32, :], -2.0 ** -9, "+LC")
+    ms(T.LC[32:64, :], 15 * 2.0 ** -20, "+LC")
+    for s in range(5):
+        ts(blk(T.LE, s, 128), T.SM[:], T.cs[:, s:s + 1], A.is_equal, "SM cs", "LE%d" % s)
+        scaled(blk(T.LR, s, 128), blk(T.LE, s, 128), T.M4[:, 3:4], "LE%d M4" % s, "+LR")
+    for t in ("GN2", "PR"):
+        scaled(T[t][:, K:], T.ZZ[:, 0:16], 1.0, "ZZ", t + "p", 64)
+    scaled(T.EN[:], blk(T.EF, 1, 144), -1.0, "EF1", "EN", 144)
+    zero(T.AE[:, 512:], 8, "AEp")
+    sc(T.WF[:], T.WL[:], "WL wme", "WF", -1.0)
+    for d in (2, 3, 1, 4, 0):
+        for q in range(N):
+            o, j = blk(T.DI, 8 * d + q, 128), 5 * q + d
+            step([ts_alt(o, T.NI[:], T.WL[:, j:j + 1], A.mult, -1.0, A.mult), sc_alt(o, T.NI[:], T.WF[:, j:j + 1], n=128)],
+                 "NI WF WL wme", "+DI%d" % d)
 
     src_of = {"G0": "TB oT", "GN1": "TB oN1", "GP1": "TB oP1", "GN2": "TB oN2", "X0": "XS oP2", "X1": "XS oP1",
               "X2": "XS oT", "X3": "XS oN1", "X4": "XS oN2", "VG": "VA oK"}
-    also = {"TB": "TBr0", "XS": "XS", "VA": "VA Vme"}
-    nx = [0, 0]
+    also = {"TB": "TBr", "XS": "XS", "VA": "VA Vme0 Vme1"}
+    nch = len(CHUNKS)
+    hbank, ebank = (4, 5, 2)[:nch], (6, 7, 3)[:nch]
+    ecut = [0] + [hi // 2 - 2 for lo, hi in CHUNKS[:-1]] + [512]
+    parts = ((0, CUT), (CUT, C))
+    seen = {}
 
-    def hsum(name, h):
-        d, first, last = int(name[1]), nx[h] % 5 == 0, nx[h] % 5 == 4
-        nx[h] += 1
-        mm([(bk(4 + h)[:, q:512:8], blk(T.DI, 8 * d + q, 128), T[name][:, 512 * h + q:512 * h + 512:8], first and q == 0,
-             last and q == 7) for q in range(N)],
-           name + "ab"[h] + " " + " ".join("DI%d" % (8 * d + q) for q in range(N)), "B%d" % (4 + h))
+    def turn(k, n):
+        seen[k] = seen.get(k, 0) + 1
+        return seen[k] % n == 1, seen[k] % n == 0
 
-    def ga(e, name, h, now=True):
+    def upto(name, h):
+        return " ".join(name + str(j) for j in range(h + 1))
+
+    def listed(b, k, src, name):
+        terms = [("EF", 144 * k, "EF%d" % k, "G0"), ("EN", 0, "EN", src)] if src == "GN1" else [("EF", 144 * k, "EF%d" % k, src)]
+        for j, (m, at, mk, x) in enumerate(terms):
+            mm(group(bk(b)[:, 0:64], [(T[m][:, at + 15 - u:at + 143 - u], T[x][:, u:K:16]) for u in range(16)],
+                     j == 0, j == len(terms) - 1), upto(x, nch - 1) + " " + mk, "B%d" % b, 1024)
+        if k:
+            ts(T[name][:], bk(b)[:, 0:64], -1.0 if src == "GN1" else 1.0, A.mult, "B%d" % b, name, -LIFT[k], A.add)
+        else:
+            ts(T[name][:], bk(b)[:, 0:64], cq, A.add, "B%d cf" % b, name, float(V), A.mult)
+
+    def gather(name, h):
+        lo, hi = CHUNKS[h]
         win, off = src_of[name].split()
-        (cp if e == "V" else sc)(blk(T[name], h, 512), T[win][:].indirect(blk(T[off], h, 32)), also[win] + " " + off,
-                                 name + "ab"[h])
-        if win == "XS" and now:
-            hsum(name, h)
+        o, a, c = T[name][:, lo:hi], T[win][:].indirect(T[off][:, lo // 16:hi // 16]), GAT * CYC * (hi - lo)
+        if name in ("GN1", "GN2"):
+            old = {"GN1": "G0", "GN2": "GN1"}[name]
+            return tt(o, a, T[old][:, lo:hi], A.add, also[win] + " " + off + " " + old + str(h), name + str(h), c / CYC + 25)
+        step([("V", lambda: vec.tensor_copy(o, a), 50 + c), ("S", lambda: act.activation(o, a, AF.Copy), 65 + c)],
+             also[win] + " " + off, name + str(h))
+        if win == "XS":
+            d, b = int(name[1]), hbank[h]
 
-    def rw(name, h):
-        mm([(bk(6 + h)[:], T.LR[:], blk(T[name], h, 512), name == "G0", False)], name + "ab"[h] + " LR", "B%d" % (6 + h))
+            def items():
+                first, last = turn(b, 5)
+                return [(bk(b)[:, q:hi - lo:8], blk(T.DI, 8 * d + q, 128), T[name][:, lo + q:hi:8], first and q == 0,
+                         last and q == 7) for q in range(N)]
+            mm(items, name + str(h) + " DI%d" % d, "+B%d" % b, 512)
 
-    def errors(h):
-        tt(blk(T.PR, h, 512), bk(4 + h)[:], blk(T.VG, h, 512), A.mult, "B%d VG%s" % (4 + h, "ab"[h]), "PR%d" % h)
-        mm([(bk(6 + h)[:], T.ON[:], blk(T.PR, h, 512), False, True)], "ON PR%d" % h, "B%d" % (6 + h))
+    def esum(name, h):
+        lo, hi, b, m = ecut[h], ecut[h + 1], ebank[h], "LE" if name == "PR" else "LR"
+        mm(lambda: group(bk(b)[:, 0:hi - lo], [(blk(T[m], s, 128), T[name][:, 2 * lo + s:2 * hi + s:2]) for s in range(5)],
+                         *turn(b + 10, 2)),
+           (upto(m, 4) if name == "PR" else m) + " " + upto(name, h) + " " + name + "p", "+B%d" % b, 5 * (hi - lo))
 
-    def absolute(h):
-        sc(blk(T.AE, h, 512), bk(6 + h)[:], "B%d" % (6 + h), "AE%d" % h, 16.0, AF.Abs)
-
-    b0, b1, b3 = T.B0[:, 0:C], T.B1[:, 0:C], T.B3[:, 0:C]
-    kex, kin = T.B0[:, 0:48:2], T.B0[:, 1:48:2]
-    cp(T.PH[:], T.PI[:], "PI", "PH")
+    kf, kb, hb = T.KK[:, 0, 16:], T.KK[:, 0, 15:15 + C], T.KK[:, 1, 15:15 + C]
     for rd in range(2):
-        W, wk = T["W%d" % rd], "W%d" % rd
-        mm([(b0, T.ON[:], T.PH[:], True, True)], "ON PH", "B0")
-        mm([(b1, T.TR[:], T.PH[:], True, True)], "TR PH", "B1")
+        base = 16 + ZONE * (1 - rd)
+        early[0] = True
+        mm([(T.B4[:, 0:C], T.L8[0:1, :], T.NEG[0:1, :], True, False)], "L8 NEG", "B4", C)
+        mm(group(T.B4[:, 0:C], [(T.TRa[:], T.PH[:, 16:]), (T.TRb[:], T.PH[:, 15:15 + C])], False, True),
+           "TRa TRb PHa PHb PHp", "B4", 2 * C)
+        def lay(at):
+            for k, a in zip((1, 2, 3, 0), POS):
+                if rd == 0 and a == at:
+                    digits(k)
+        lay(0)
+        mm(group(T.B5[:, 0:C], [(T.LB[0:1, :, :], T.NEG[0:1, :]), (T.LS[0:1, :], T.RAMP[0:1, :])], True, False),
+           "LB LS NEG RAMP", "B5", 2 * C)
+        step([("V", lambda: vec.tensor_tensor_scan(kf, T.B4[:, 0:C], T.NEG[:], -2048.498046875, A.add, A.min), cost(C))],
+             "B4 NEG", "KF")
+        lay(1)
+        mm(group(T.B5[:, 0:C], [(T.LA1[:], kf), (T.LA2[:], kb)], False, True), "LA1 LA2 KF KKp", "B5", 2 * C)
+        ts(T.KK[:, 1, 16:], kf, 0.5, A.mult, "KF", "KH", -1024.25, A.add, C // 2)
+        mm(group(T.B2[:, 0:48], [(T.EK[:, 15 - u:143 - u], T.KK[:, :, 15 + u:15 + C:16]) for u in range(16)], True, False),
+           "EK KF KH KKp", "B2", 1024)
+        ts(T.CC[:], T.B5[:, 0:C], 0.0, A.max, "B5 cm1", "CC", cm[1], A.min, C)
+        lay(2)
+        mm(group(T.B2[:, 0:24], [(T.EZ[:, 15 - u:143 - u], T.CC[:, u:C:16]) for u in range(16)], False, True),
+           "EZ CC", "B2", 1024)
+        ts(T.OF[:], T.B2[:, 0:48], 2048.0, A.add, "B2", "OF")
+        tt(T.W[:, base:].indirect(T.OF[:, 0:24]), T.CC[:], T.CT[:], A.mult, "CC CT OF Wz" if rd else "CC CT OF", "W", SCA * C)
+        lay(3)
         if rd == 0:
-            mid_constants()
-        op("V", lambda: vec.tensor_tensor_scan(T.B2[:, 1:C + 1], b0, T.PH[:], -2048.0, A.add, A.min), "B0 PH", "B2")
-        ts(T.KH[:], T.B2[:, 0:400], -0.498046875, A.add, "B2", "KH")
-        mm([(T.B0[:, 0:48], T.EK[:, 15 - u:143 - u], T.KH[:, 0:24, u:u + 2], u == 0, False) for u in range(15)] +
-           [(kex, T.EK[:, 0:128], T.KH[:, 0:24, 15], False, False), (kin, T.EK[:, 0:128], T.KH[:, 1:25, 0], False, True)],
-           "EK KH", "B0")
-        if rd == 0:
-            tab_float(0)
-            tab_float(1)
-        tt(T.YH[:], T.B2[:, 0:C], T.KH[:, 0:24, :], A.subtract, "B2 KH", "YH")
-        if rd == 0:
-            tab_digits(0)
-            tab_float(2)
-            tab_digits(1)
-            tab_float(3)
-        tt(T.RH[:], b1, T.YH[:], A.add, "B1 YH", "RH")
-        if rd == 0:
-            tab_digits(2)
-            tab_digits(3)
-            dma(T.XS[:], T.x[:], "dX", 16, "", "XS")
-            pick_matrices()
-        for r in range(4):
-            ts(blk(T.GE, r, C), T.RH[:], float(r + 1), A.is_ge, "RH", "GE%d" % r)
-            mm([(b3, T.LZ[:, 3 - r:131 - r], blk(T.GE, r, C), r == 0, r == 3)], "LZ GE%d" % r, "B3")
-        sc(T.ZS[:], b3, "B3", "ZS")
-        if rd == 0:
-            ts(T.D2[:], T.D2i[:], ca, A.add, "D2i cf", "D2", 2.0, A.mult)
-        ts(T.ua[:], kin, -0.75, A.add, "B0", "ua")
-        tt(T.ub[:], T.ua[:], kex, A.is_lt, "ua B0", "ub")
-        tt(T.uc[:], T.ub[:], T.D2[:], A.mult, "ub D2", "uc")
-        tt(T.ud[:], T.uc[:], kex, A.add, "uc B0", "ud")
-        ts(T.US[:], T.ud[:], 2064.0, A.add, "ud", "US")
-        if rd == 0:
-            tt(T.CT[:], T.CA[:], T.CB[:], A.add, "CA CB", "CT")
-        tt(W[:].indirect(T.US[:]), T.ZS[:], T.CT[:], A.mult, "ZS CT US", wk)
-        pairs = [(T.ET[:, 15 - u:143 - u], W[:, 16 + u:1040:16]) for u in range(13)]
+            dma(blk(T.XS, 1, F // 2), blk(T.x, 1, F // 2), "dX", 32, "", "+XS", 768)
+        pairs = [(T.ET[:, 15 - u:143 - u], T.W[:, base + u:base + K:16]) for u in range(13)]
         for s in range(3):
-            pairs.append((blk(T.ES, 2 * s, 128), W[:, 31 - s:1040:16]))
-            pairs.append((blk(T.ES, 2 * s + 1, 128), W[:, 15 - s:1024:16]))
-        pick(3, 0, pairs, "ET ESm0 ESm1 ESm2 ESc0 ESc1 ESc2 " + wk)
-        if rd == 0:
-            sc(T.WF[:], T.WL[:], "WL wme", "WF")
-            diags("S", 2)
-            diags("S", 3, range(4))
-        for r in range(4):
-            ts(blk(T.UR, r, 24), kex, 2048.0 + r, A.add, "B0", "UR%d" % r)
-        take(3, 0, "oT")
-        ga("V", "G0", 0)
-        ga("S", "G0", 1)
-        fam(2, 448, 1, "G0")
-        fam(3, 0, 2, "G0")
-        if rd == 0:
-            last_constants()
-            diags("S", 4)
-        else:
-            ga("V", "X2", 0, False)
-            ga("S", "X2", 1, False)
-        take(2, 448, "oN1")
-        take(3, 0, "oP1")
-        fam(2, 448, 0, "G0")
-        ga("V", "GN1", 0)
-        ga("S", "GP1", 0)
-        mm([(b1, T.Ih[:], T.PH[:], True, False)] + [(b1, T.Dn[:], blk(T.GE, r, C), False, r == 3) for r in range(4)],
-           "Ih Dn PH GE0 GE1 GE2 GE3", "B1")
-        ga("V", "GN1", 1)
-        ga("S", "GP1", 1)
-        ts(T.oK[:], T.B2[:, 448:512], T.cm[:, 3:4], A.add, "B2 cm3", "oK")
-        fam(3, 0, 1, "GN1")
-        fam(2, 448, 2, "GP1")
-        if rd == 0:
-            diags("V", 3, range(4, 8))
-            diags("V", 1)
-        else:
-            ga("V", "X1", 0, False)
-            ga("S", "X3", 0, False)
-        take(3, 0, "oN2")
-        if rd == 1:
-            ga("V", "VG", 0)
-        take(2, 448, "oP2")
-        if rd == 0:
-            diags("V", 0)
-            order = "SGN20 SGN21 r0 r1 C VX20 SX30 VX10 SX00 VX40 R0 SX21 VX11 SX31 VX41 R1 SX01 VVG0 SVG1 E0 A0"
-        else:
-            order = "HX20 HX10 HX30 r0 SGN20 SX00 VX40 R0 HX21 SX31 VX11 E0 r1 C SVG1 VX41 SGN21 R1 A0 VX01"
-        for it in order.split():
-            if it[0] in "EA":
-                (errors if it[0] == "E" else absolute)(0)
-            elif it[0] == "r":
-                rw("G0", int(it[1]))
-                rw("GN1", int(it[1]))
-            elif it[0] == "R":
-                rw("GN2", int(it[1]))
-            elif it[0] == "H":
-                hsum(it[1:3], int(it[3]))
-            elif it[0] == "C":
-                mm([(T.B3[:, 0:128], T.LC[:], T.CT[:, 0:128], True, False)], "LC CT", "B3")
-                mm([(T.B0[:, 128:C], T.LC[:], T.CT[:, 128:C], True, False)], "LC CT", "B0")
-            else:
-                ga(it[0], it[1:-1], int(it[-1]))
-        errors(1)
-        absolute(1)
-        parts = ((3, 0, 128, T.AE[:, 0:512], "AE0"), (0, 128, C, T.AE[:], "AE0 AE1 AEp"))
-        for b, lo, hi, win, keys in parts:
-            for r in range(4):
-                gg, key = T.GG[:, C * r + lo:C * r + hi], "GG%d%d" % (b, r)
-                tt(gg, win.indirect(T.UR[:, 24 * r + lo // 16:24 * r + hi // 16]), T.GE[:, C * r + lo:C * r + hi], A.mult,
-                   keys + " UR%d GE%d" % (r, r), key)
-                mm([(bk(b)[:, lo:hi], T.Dm[:], gg, False, r == 3)], "Dm " + key, "B%d" % b)
-        for b, lo, hi, win, keys in parts:
-            ts(T.NI[:, lo:hi], bk(b)[:, lo:hi], 1.0, A.max, "B%d" % b, "NI%d" % b, 63.0, A.min)
-            out = ("PH", "YO")[rd]
-            tt(T[out][:, lo:hi], T.NI[:, lo:hi], T.B1[:, lo:hi], A.max, "NI%d B1" % b, out)
-    dma(T.y[:], T.YO[:], "dY", 16, "YO", "y")
+            pairs.append((blk(T.ES, 2 * s, 128), T.W[:, base + 15 - s:base + K:16]))
+            pairs.append((blk(T.ES, 2 * s + 1, 128), T.W[:, base - 1 - s:base + K - 16:16]))
+        mm(group(T.B3[:, 0:64], pairs), "ET ES W", "B3", 19 * 64)
+        ts(T.oT[:], T.B3[:, 0:64], 3072.0, A.add, "B3", "oT")
+        for src, lists in (("G0", ((2, 1, "oN1"), (3, 2, "oP1"))), ("GN1", ((2, 1, "oN2"),)), ("GP1", ((3, 2, "oP2"),))):
+            for h in range(nch):
+                gather(src, h)
+            for b, k, name in lists:
+                listed(b, k, src, name)
+        listed(2, 0, "G0", "oK")
+        mm(group(T.B6[:, 0:C], [(T.SH[:], kf), (T.LE2[:], kb), (T.LE3[:], hb)]), "SH LE2 LE3 KF KH KKp", "B6", 3 * C)
+        sc(T.T1[:], T.B6[:, 0:C], "B6 cm8", "T1", -1.0, AF.Abs, cm[8], C)
+        mm(group(T.B7[:, 0:C], [(T.NI[:], T.PH[:, 16:]), (T.Dp[:], kf), (T.D15[:], kb)]), "NI Dp D15 PHa PHb KF KKp", "B7",
+           3 * C)
+        sc(T.Z1[:], T.B7[:, 0:C], "B7", "Z1", -1.0, AF.Relu, -129.0, C)
+        sc(T.CAP[:], T.T1[:], "T1", "CAP", -63.0, AF.Relu, 63.0, C)
+        step([ts_alt(T.ZO[:], T.Z1[:], 129.0, A.add, n=C // 2), sc_alt(T.ZO[:], T.Z1[:], 1.0, AF.Identity, 129.0, C)],
+             "Z1", "ZO")
+        for h, (lo, hi) in enumerate(parts):
+            mm(group(bk(h)[:, 0:hi - lo], [(T.LC[0:64, :], T.NEG[0:64, lo:hi]), (T.Dp[:], T.KK[:, 0, 16 + lo:16 + hi]),
+                                           (T.D15[:], T.KK[:, 0, 15 + lo:15 + hi])], True, False),
+               "LC NEG Dp D15 KF KKp", "B%d" % h, 3 * (hi - lo))
+        for c in range(nch if rd == 0 else 0):
+            for name in ("X2", "X3", "X1", "GN2", "X4", "X0"):
+                gather(name, c)
+            esum("GN2", c)
+        for c, (lo, hi) in enumerate(CHUNKS):
+            for name in ("VG",) if rd == 0 else ("X2", "X3", "X1", "GN2", "VG", "X4", "X0"):
+                gather(name, c)
+            if rd == 1:
+                esum("GN2", c)
+            tt(T.PR[:, lo:hi], bk(hbank[c])[:, 0:hi - lo], T.VG[:, lo:hi], A.mult, "B%d VG%d" % (hbank[c], c), "PR%d" % c,
+               hi - lo)
+            esum("PR", c)
+            n = ecut[c + 1] - ecut[c]
+            sc(T.AE[:, ecut[c]:ecut[c + 1]], bk(ebank[c])[:, 0:n], "B%d" % ebank[c], "AE%d" % c, 1.0 / 16, AF.Abs,
+               -3 * LIFT[3] / 16, n)
+            h = c - nch + 2
+            if h < 0:
+                continue
+            lo, hi = parts[h]
+            ab, win = "ab"[h], T.AE[:] if h else T.AE[:, 0:ecut[-2]]
+            tt(T.GG[:, lo:hi], win.indirect(T.OF[:, 24 + lo // 16:24 + hi // 16]), T.CAP[:, lo:hi], A.min,
+               upto("AE", c) + " OF CAP" + " AEp" * h, "GG" + ab, GAT * (hi - lo))
+            mm([(bk(h)[:, 0:hi - lo], T.LQ[:], T.GG[:, lo:hi], False, True)], "LQ GG" + ab, "B%d" % h, hi - lo)
+            tt(T.PH[:, 16 + lo:16 + hi], bk(h)[:, 0:hi - lo], T.ZO[:, lo:hi], A.max, "B%d ZO" % h, "PH" + ab, hi - lo)
+            if rd == 1:
+                sc(T.YO[:, lo:hi], T.PH[:, 16 + lo:16 + hi], "PH" + ab, "YO" + ab, 1.0, AF.Identity, -128.0, hi - lo)
+                dma(T.y[:, lo:hi], T.YO[:, lo:hi], "dY", 32, "YO" + ab, "y" + ab, 100)
+    cnt, wait = issue(steps, Q, T)
     wait("G", "loc", total[0])
     for e in "VSPG":
         wait("Y", "c" + e, cnt[e])
-    wait("Y", "dY", 16)
+    wait("Y", "dY", 32)

@@ -3,9 +3,16 @@ from concourse.mybir import AluOpType as A, ActivationFunctionType as AF
 
 N, F, C, K, V, NSIM = 8, 6144, 384, 1024, 2048, 64
 ZONE, GAP = 1040, 1152
-CHUNKS = ((0, 512), (512, 1024))
-CUT = 128
-AHEAD, DUP, FILL, POS = 2, False, 9, (0, 0, 0, 0)
+GCH = ((0, 512, 1024), (0, 512, 768, 1024))
+ECH = ((0, 512, 768, 1024), (0, 512, 768, 1024))
+CUT, SPLIT, TOL, LAM, HOLD = 192, False, 70, 0, 2
+AHEAD, DUP, FILL, POS = 2, False, 10, (1, 1, 2, 2)
+PELO, XA, AFTER = (), True, "TI1"
+ORDER = ("-G0a -G0b fN1 fP1 tN1 -GN1a tP1 -GN1b -GP1a -GP1b fK fN2 tK tN2 fP2 tP2 M -X2a -X3a -X1a -GN2a -X4a -X0a E0 "
+         "-X2b -X3b -X1b -GN2b -X4b -X0b E1 E2 -VGa P0 A0 -VGc P1 A1 -VGd P2 A2 Ng0 Ng1 Nn0 Nn1",
+         "M VG0a SG0b fN1 fP1 VX2a SX2b tN1 SX3a VGN1a tP1 fK SGP1a VGN1b fN2 tK SGP1b VX3b fP2 tN2 SX1a VVGa tP2 SX4a "
+         "VGN2a E0 SX1b VX0a SX4b VGN2b SX0b P0 E1 E2 SVGc VVGd P1 A0 P2 A1 A2 Ng0 Ng1 Nn0 Nn1")
+PIN = (False, True)
 LIFT = (0.0, 9216.0, 0.0, 3072.0)
 SCRATCH = {}
 for _dt, _bufs in (
@@ -16,9 +23,9 @@ for _dt, _bufs in (
                       G0=K, GP1=K, X0=K, X1=K, X2=K, X3=K, X4=K, VG=K)),
     ("float16", dict(EK=144, LE=5 * 128, QM=128, SH=128, LE2=128, LE3=128, LQ=128, I64=128, S64=128, Dp=128, D15=128,
                      BH=128, PR=K + 16, GG=C, GN1=K, GN2=K + 16, LR=5 * 128, EN=144)),
-    ("float32", dict(OH=16, WF=40, cm=16, cs=8, M4=4, Mle=4, Mgt=4, AE=520, YO=C)),
+    ("float32", dict(OH=16, TF=4 * C, I32=128, WF=40, cm=16, cs=8, M4=4, Mle=4, Mgt=4, AE=520, YO=C, SF=C)),
     ("int32", dict(TI=4 * C, PI=C, ci=8)),
-    ("uint16", dict(OF=48, oT=64, oN1=64, oP1=64, oN2=64, oP2=64, oK=64)),
+    ("uint16", dict(OF=96, oT=64, oN1=64, oP1=64, oN2=64, oP2=64, oK=64)),
 ):
     for _n, _w in _bufs.items():
         SCRATCH[_n] = ("sbuf", [128, _w], _dt)
@@ -109,7 +116,7 @@ HOP, CYC, PEC, GAT, SCA = 70, 0.83, 0.45, 1.5, 3.5
 
 def issue(steps, Q, T):
     wrote, pieces, read = {}, {}, {}
-    last_dma = None
+    last = {}
     for i, s in enumerate(steps):
         pre = set()
         for k in s["r"]:
@@ -129,9 +136,9 @@ def issue(steps, Q, T):
         for k in s["r"]:
             read.setdefault(k, []).append(i)
         pre.discard(i)
-        s["pre"], s["post"], s["behind"] = pre, [], last_dma if s["alt"][0][0] == "Y" else None
-        if s["alt"][0][0] == "Y":
-            last_dma = i
+        s["pre"], s["post"], s["behind"] = pre, [], last.get(s["row"])
+        if s["row"]:
+            last[s["row"]] = i
     for i, s in enumerate(steps):
         for j in s["pre"]:
             steps[j]["post"].append(i)
@@ -149,11 +156,11 @@ def issue(steps, Q, T):
         for i in todo:
             s = steps[i]
             if all(j in done for j in s["pre"]) and (s["behind"] is None or s["behind"] in done):
-                t, e, c, fn = min(((start(i, a[0]) + a[2], a[0], a[2], a[1]) for a in s["alt"]), key=lambda x: x[0])
+                t, e, c, fn = min(((start(i, a[0]) + a[2], a[0], a[2], a[1]) for a in s["alt"]), key=lambda x: x[0] + LAM * x[2])
                 cand.append((t - c, -s["chain"], i, e, c, fn))
         cand.sort(key=lambda x: x[:3])
         for x in cand:
-            if all(y[3] != x[3] or y[1] >= x[1] or y[0] >= x[0] + x[4] - HOP for y in cand):
+            if all(y[3] != x[3] or y[1] >= x[1] or y[0] >= x[0] + x[4] - TOL for y in cand):
                 break
         else:
             x = min((y for y in cand if y[3] == cand[0][3]), key=lambda y: y[1])
@@ -195,12 +202,13 @@ def rank_program(g, core, T, topo):
         return helper_program(g, core, T, topo, pl)
     Q = {"V": g.vector, "S": g.scalar, "P": g.tensor, "G": g, "Y": g.sync}
     vec, act = g.vector, g.scalar
-    steps, early = [], [0]
+    steps, early, pin = [], [0], [None]
 
     def step(alt, r, w, lat=0, tok=None):
         r, w = r.split(), w.split()
         banks = [k for k in r if len(k) == 2 and k[0] == "B" and k[1] in "01234567"]
-        steps.append(dict(alt=alt, r=[k for k in r if k not in banks], w=w + banks, lat=lat, tok=tok, early=early[0]))
+        alt = [a for a in alt if a[0] == pin[0]] or alt
+        steps.append(dict(alt=alt, row=alt[0][0] if alt[0][0] in ("Y", pin[0]) else None, r=[k for k in r if k not in banks], w=w + banks, lat=lat, tok=tok, early=early[0]))
 
     def cost(n):
         return 30 + CYC * max(64, n)
@@ -293,7 +301,8 @@ def rank_program(g, core, T, topo):
     early[0] = False
     for k in (1, 2, 3, 0)[AHEAD:]:
         table(k, "issued")
-    dma(blk(T.XS, 0, F // 2), blk(T.x, 0, F // 2), "dX", 32, "gone", "+XS", 768)
+    if XA:
+        dma(blk(T.XS, 0, F // 2), blk(T.x, 0, F // 2), "dX", 32, "gone", "+XS", 768)
 
     iota(T.LB[0:1, :, :], [[0, 32], [5, 4]], 0, 0, "LB", 128)
     iota(T.LB[0:1, :, 1:4], [[0, 8], [4, 3]], 4, 0, "+LB", 24)
@@ -320,20 +329,34 @@ def rank_program(g, core, T, topo):
         sc(blk(T.TB, k, 512), T.ZZ[:, 0:512], "ZZ", "+TBb", n=512)
     early[0] = False
     for k in range(12 if DUP else FILL, 12):
-        ms(blk(T.TB, k, 512), 0.0, "+TBb", 256)
+        step([("V", lambda k=k: vec.memset(blk(T.TB, k, 512), 0.0), cost(256))], AFTER, "+TBb")
 
     def zero(out, n, w):
         step([("V", lambda: vec.memset(out, 0.0), cost(n // 2)), sc_alt(out, T.ZZ[:, 0:n], n=n)], "ZZ", w)
 
     def digits(k):
         b = k % 2
+        if k in PELO:
+            ts(blk(T.TF, k, C), blk(T.TI, k, C), LIFT[k], A.add, "TI%d" % k, "TF%d" % k, n=C)
+            mm([(bk(b)[:, 0:C], T.I32[:], blk(T.TF, k, C), True, False)], "I32 TF%d" % k, "B%d" % b, 4 * C)
+            sc(blk(T.DG, 2 * k, C), blk(T.TF, k, C), "TF%d" % k, "DG%d" % (2 * k), n=C)
+            mm([(bk(b)[:, 0:C], T.NI[:], blk(T.DG, 2 * k, C), False, True)], "NI DG%d" % (2 * k), "B%d" % b, C)
+            sc(blk(T.DG, 2 * k + 1, C), bk(b)[:, 0:C], "B%d" % b, "DG%d" % (2 * k + 1), n=C)
+        else:
+            split(k, b)
+        for a in (2 * k, 2 * k + 1):
+            for at in (a, a + 8) if DUP else (a,):
+                dma(T.TB[at:128:16, :], blk(T.DG, a, C), "dR", 256 if DUP else 128, "DG%d TBb" % a, "+TBr", 96)
+
+    def split(k, b):
         ts(bk(b)[:, 0:C], blk(T.TI, k, C), LIFT[k], A.add, "TI%d" % k, "B%d" % b, n=C)
         sc(blk(T.DG, 2 * k, C), bk(b)[:, 0:C], "B%d" % b, "DG%d" % (2 * k), n=C)
         tt(blk(T.DG, 2 * k + 1, C), bk(b)[:, 0:C], blk(T.DG, 2 * k, C), A.subtract,
            "B%d DG%d" % (b, 2 * k), "DG%d" % (2 * k + 1), C)
-        for a in (2 * k, 2 * k + 1):
-            for at in (a, a + 8) if DUP else (a,):
-                dma(T.TB[at:128:16, :], blk(T.DG, a, C), "dR", 256 if DUP else 128, "DG%d TBb" % a, "+TBr", 96)
+
+    ts(T.NI[:], x128, cpp, A.is_equal, "XF cp", "NI", -1.0, A.mult)
+    if PELO:
+        scaled(T.I32[:], T.NI[:], -1.0, "NI", "I32", 256)
 
     ms(T.PH[:, 0:16], 128.0, "PHp")
     ms(T.L8[0:1, :], 1.0 / 128, "L8")
@@ -392,7 +415,6 @@ def rank_program(g, core, T, topo):
     select(T.S64[:], T.I64[:], [[1, 128]], A.is_equal, 0.0, -1, -1, "I64", "S64")
     select(T.Dp[:], T.S64[:], [[1, 128]], A.not_equal, 64.0, 0, -1, "S64", "Dp")
     select(T.D15[:], T.I64[:], [[1, 128]], A.is_equal, 0.0, 15, -1, "I64", "D15")
-    ts(T.NI[:], x128, cpp, A.is_equal, "XF cp", "NI", -1.0, A.mult)
     ts(T.LQ[:], T.D4[:], cm[7], A.is_equal, "D4 cm7", "LQ")
     ms(T.LC[0:32, :], -2.0 ** -9, "+LC")
     ms(T.LC[32:64, :], 15 * 2.0 ** -20, "+LC")
@@ -413,11 +435,11 @@ def rank_program(g, core, T, topo):
     src_of = {"G0": "TB oT", "GN1": "TB oN1", "GP1": "TB oP1", "GN2": "TB oN2", "X0": "XS oP2", "X1": "XS oP1",
               "X2": "XS oT", "X3": "XS oN1", "X4": "XS oN2", "VG": "VA oK"}
     also = {"TB": "TBr", "XS": "XS", "VA": "VA Vme0 Vme1"}
-    nch = len(CHUNKS)
-    hbank, ebank = (4, 5, 2)[:nch], (6, 7, 3)[:nch]
-    ecut = [0] + [hi // 2 - 2 for lo, hi in CHUNKS[:-1]] + [512]
-    parts = ((0, CUT), (CUT, C))
+    hbank, ebank = (4, 5, 2), (6, 7, 3)
     seen = {}
+
+    def span(name, lo, hi):
+        return " ".join(name + str(j) for j in range(lo // 256, hi // 256))
 
     def turn(k, n):
         seen[k] = seen.get(k, 0) + 1
@@ -426,69 +448,94 @@ def rank_program(g, core, T, topo):
     def upto(name, h):
         return " ".join(name + str(j) for j in range(h + 1))
 
-    def listed(b, k, src, name):
+    def listed(b, k, src, name, what):
         terms = [("EF", 144 * k, "EF%d" % k, "G0"), ("EN", 0, "EN", src)] if src == "GN1" else [("EF", 144 * k, "EF%d" % k, src)]
         for j, (m, at, mk, x) in enumerate(terms):
-            mm(group(bk(b)[:, 0:64], [(T[m][:, at + 15 - u:at + 143 - u], T[x][:, u:K:16]) for u in range(16)],
-                     j == 0, j == len(terms) - 1), upto(x, nch - 1) + " " + mk, "B%d" % b, 1024)
+            if what == "f":
+                mm(group(bk(b)[:, 0:64], [(T[m][:, at + 15 - u:at + 143 - u], T[x][:, u:K:16]) for u in range(16)],
+                         j == 0, j == len(terms) - 1), span(x, 0, K) + " " + mk, "B%d" % b, 1024)
+        if what == "f":
+            return
         if k:
             ts(T[name][:], bk(b)[:, 0:64], -1.0 if src == "GN1" else 1.0, A.mult, "B%d" % b, name, -LIFT[k], A.add)
         else:
             ts(T[name][:], bk(b)[:, 0:64], cq, A.add, "B%d cf" % b, name, float(V), A.mult)
 
-    def gather(name, h):
-        lo, hi = CHUNKS[h]
+    def gather(name, lo, hi, b=None):
         win, off = src_of[name].split()
         o, a, c = T[name][:, lo:hi], T[win][:].indirect(T[off][:, lo // 16:hi // 16]), GAT * CYC * (hi - lo)
+        r, w = also[win] + " " + off, span(name, lo, hi)
         if name in ("GN1", "GN2"):
             old = {"GN1": "G0", "GN2": "GN1"}[name]
-            return tt(o, a, T[old][:, lo:hi], A.add, also[win] + " " + off + " " + old + str(h), name + str(h), c / CYC + 25)
-        step([("V", lambda: vec.tensor_copy(o, a), 50 + c), ("S", lambda: act.activation(o, a, AF.Copy), 65 + c)],
-             also[win] + " " + off, name + str(h))
+            return tt(o, a, T[old][:, lo:hi], A.add, r + " " + span(old, lo, hi), w, c / CYC + 25)
+        step([("V", lambda: vec.tensor_copy(o, a), 50 + c), ("S", lambda: act.activation(o, a, AF.Copy), 65 + c)], r, w)
         if win == "XS":
-            d, b = int(name[1]), hbank[h]
+            d = int(name[1])
 
             def items():
                 first, last = turn(b, 5)
                 return [(bk(b)[:, q:hi - lo:8], blk(T.DI, 8 * d + q, 128), T[name][:, lo + q:hi:8], first and q == 0,
                          last and q == 7) for q in range(N)]
-            mm(items, name + str(h) + " DI%d" % d, "+B%d" % b, 512)
+            mm(items, w + " DI%d" % d, "+B%d" % b, 512)
 
-    def esum(name, h):
-        lo, hi, b, m = ecut[h], ecut[h + 1], ebank[h], "LE" if name == "PR" else "LR"
+    def ecol(k):
+        return min(max(k // 2 - 2, 0), 512) if k < K else 512
+
+    def esum(name, c, k0, k1):
+        lo, hi, b, m = ecol(k0), ecol(k1), ebank[c], "LE" if name == "PR" else "LR"
         mm(lambda: group(bk(b)[:, 0:hi - lo], [(blk(T[m], s, 128), T[name][:, 2 * lo + s:2 * hi + s:2]) for s in range(5)],
                          *turn(b + 10, 2)),
-           (upto(m, 4) if name == "PR" else m) + " " + upto(name, h) + " " + name + "p", "+B%d" % b, 5 * (hi - lo))
+           (upto(m, 4) if name == "PR" else m) + " " + span(name, 0, k1) + " " + name + "p", "+B%d" % b, 5 * (hi - lo))
+
+    def lay(rd, at):
+        for k, a in zip((1, 2, 3, 0), POS):
+            if rd == 0 and a == at:
+                digits(k)
+
+    def sample(rd, lo, hi, ab, bs, ba, bw):
+        n, base, of = hi - lo, 16 + ZONE * (1 - rd), T.OF[:, 48 * rd + lo // 8:48 * rd + hi // 8]
+        f, b = T.KK[:, 0, 16 + lo:16 + hi], T.KK[:, 0, 15 + lo:15 + hi]
+        ph, kk, kh, cc = [" ".join(t + x for x in ab) for t in ("PH", "KF", "KH", "CC")]
+        mm([(bk(bs)[:, 0:n], T.L8[0:1, :], T.NEG[0:1, 0:n], True, False)], "L8 NEG", "B%d" % bs, n)
+        for x in ab:
+            c0, c1 = (max(lo, CUT), hi) if x == "b" else (lo, CUT)
+            mm(group(bk(bs)[:, c0 - lo:c1 - lo], [(T.TRa[:], T.PH[:, 16 + c0:16 + c1]), (T.TRb[:], T.PH[:, 15 + c0:15 + c1])],
+                     False, x == ab[-1]), "TRa TRb PHa PHp PH" + x, "B%d" % bs, 2 * (c1 - c0))
+        lay(rd, 0)
+        mm(group(bk(ba)[:, 0:n], [(T.LB[0:1, :, :], T.NEG[0:1, 0:n]), (T.LS[0:1, :], T.RAMP[0:1, 0:n])], True, False),
+           "LB LS NEG RAMP", "B%d" % ba, 2 * n)
+        out, init = T.SF[:, 0:n] if hi < C else f, T.SF[:, lo - 1:lo] if lo else -2048.498046875
+        step([("V", lambda: vec.tensor_tensor_scan(out, bk(bs)[:, 0:n], T.NEG[:, 0:n], init, A.add, A.min), cost(n))],
+             "B%d NEG" % bs + " SF" * (lo > 0), "SF" if hi < C else kk)
+        if hi < C:
+            step([("V", lambda: vec.tensor_copy(f, out), cost(n)), sc_alt(f, out, n=n)], "SF", kk)
+        lay(rd, 1)
+        mm(group(bk(ba)[:, 0:n], [(T.LA1[:], f), (T.LA2[:], b)], False, True), "LA1 LA2 KFa KKp " + kk, "B%d" % ba, 2 * n)
+        ts(T.KK[:, 1, 16 + lo:16 + hi], f, 0.5, A.mult, kk, kh, -1024.25, A.add, n // 2)
+        mm(group(bk(bw)[:, 0:n // 8], [(T.EK[:, 15 - u:143 - u], T.KK[:, :, 15 + lo + u:15 + hi:16]) for u in range(16)],
+                 True, False), "EK KFa KHa KKp %s %s" % (kk, kh), "B%d" % bw, 1024)
+        ts(T.CC[:, lo:hi], bk(ba)[:, 0:n], 0.0, A.max, "B%d cm1" % ba, cc, cm[1], A.min, n)
+        lay(rd, 2)
+        mm(group(bk(bw)[:, 0:n // 16], [(T.EZ[:, 15 - u:143 - u], T.CC[:, lo + u:hi:16]) for u in range(16)], False, True),
+           "EZ " + cc, "B%d" % bw, 1024)
+        ts(of, bk(bw)[:, 0:n // 8], 2048.0, A.add, "B%d" % bw, "OF%d%s" % (rd, ab[0]))
+        tt(T.W[:, base:].indirect(T.OF[:, 48 * rd + lo // 8:48 * rd + lo // 8 + n // 16]), T.CC[:, lo:hi], T.CT[:, lo:hi],
+           A.mult, "CT OF%d%s %s" % (rd, ab[0], cc) + " Wz" * rd, "W", SCA * n)
+        lay(rd, 3)
 
     kf, kb, hb = T.KK[:, 0, 16:], T.KK[:, 0, 15:15 + C], T.KK[:, 1, 15:15 + C]
     for rd in range(2):
         base = 16 + ZONE * (1 - rd)
         early[0] = True
-        mm([(T.B4[:, 0:C], T.L8[0:1, :], T.NEG[0:1, :], True, False)], "L8 NEG", "B4", C)
-        mm(group(T.B4[:, 0:C], [(T.TRa[:], T.PH[:, 16:]), (T.TRb[:], T.PH[:, 15:15 + C])], False, True),
-           "TRa TRb PHa PHb PHp", "B4", 2 * C)
-        def lay(at):
-            for k, a in zip((1, 2, 3, 0), POS):
-                if rd == 0 and a == at:
-                    digits(k)
-        lay(0)
-        mm(group(T.B5[:, 0:C], [(T.LB[0:1, :, :], T.NEG[0:1, :]), (T.LS[0:1, :], T.RAMP[0:1, :])], True, False),
-           "LB LS NEG RAMP", "B5", 2 * C)
-        step([("V", lambda: vec.tensor_tensor_scan(kf, T.B4[:, 0:C], T.NEG[:], -2048.498046875, A.add, A.min), cost(C))],
-             "B4 NEG", "KF")
-        lay(1)
-        mm(group(T.B5[:, 0:C], [(T.LA1[:], kf), (T.LA2[:], kb)], False, True), "LA1 LA2 KF KKp", "B5", 2 * C)
-        ts(T.KK[:, 1, 16:], kf, 0.5, A.mult, "KF", "KH", -1024.25, A.add, C // 2)
-        mm(group(T.B2[:, 0:48], [(T.EK[:, 15 - u:143 - u], T.KK[:, :, 15 + u:15 + C:16]) for u in range(16)], True, False),
-           "EK KF KH KKp", "B2", 1024)
-        ts(T.CC[:], T.B5[:, 0:C], 0.0, A.max, "B5 cm1", "CC", cm[1], A.min, C)
-        lay(2)
-        mm(group(T.B2[:, 0:24], [(T.EZ[:, 15 - u:143 - u], T.CC[:, u:C:16]) for u in range(16)], False, True),
-           "EZ CC", "B2", 1024)
-        ts(T.OF[:], T.B2[:, 0:48], 2048.0, A.add, "B2", "OF")
-        tt(T.W[:, base:].indirect(T.OF[:, 0:24]), T.CC[:], T.CT[:], A.mult, "CC CT OF Wz" if rd else "CC CT OF", "W", SCA * C)
-        lay(3)
+        ech = ECH[rd]
+        parts = ((0, CUT), (CUT, C))
+        if rd == 1 and SPLIT:
+            sample(rd, CUT, C, "b", 4, 5, 2)
+        else:
+            sample(rd, 0, C, "ab", 4, 5, 2)
         if rd == 0:
+            if not XA:
+                dma(blk(T.XS, 0, F // 2), blk(T.x, 0, F // 2), "dX", 32, "gone", "+XS", 768)
             dma(blk(T.XS, 1, F // 2), blk(T.x, 1, F // 2), "dX", 32, "", "+XS", 768)
         pairs = [(T.ET[:, 15 - u:143 - u], T.W[:, base + u:base + K:16]) for u in range(13)]
         for s in range(3):
@@ -496,51 +543,61 @@ def rank_program(g, core, T, topo):
             pairs.append((blk(T.ES, 2 * s + 1, 128), T.W[:, base - 1 - s:base + K - 16:16]))
         mm(group(T.B3[:, 0:64], pairs), "ET ES W", "B3", 19 * 64)
         ts(T.oT[:], T.B3[:, 0:64], 3072.0, A.add, "B3", "oT")
-        for src, lists in (("G0", ((2, 1, "oN1"), (3, 2, "oP1"))), ("GN1", ((2, 1, "oN2"),)), ("GP1", ((3, 2, "oP2"),))):
-            for h in range(nch):
-                gather(src, h)
-            for b, k, name in lists:
-                listed(b, k, src, name)
-        listed(2, 0, "G0", "oK")
-        mm(group(T.B6[:, 0:C], [(T.SH[:], kf), (T.LE2[:], kb), (T.LE3[:], hb)]), "SH LE2 LE3 KF KH KKp", "B6", 3 * C)
-        sc(T.T1[:], T.B6[:, 0:C], "B6 cm8", "T1", -1.0, AF.Abs, cm[8], C)
-        mm(group(T.B7[:, 0:C], [(T.NI[:], T.PH[:, 16:]), (T.Dp[:], kf), (T.D15[:], kb)]), "NI Dp D15 PHa PHb KF KKp", "B7",
-           3 * C)
-        sc(T.Z1[:], T.B7[:, 0:C], "B7", "Z1", -1.0, AF.Relu, -129.0, C)
-        sc(T.CAP[:], T.T1[:], "T1", "CAP", -63.0, AF.Relu, 63.0, C)
-        step([ts_alt(T.ZO[:], T.Z1[:], 129.0, A.add, n=C // 2), sc_alt(T.ZO[:], T.Z1[:], 1.0, AF.Identity, 129.0, C)],
-             "Z1", "ZO")
-        for h, (lo, hi) in enumerate(parts):
-            mm(group(bk(h)[:, 0:hi - lo], [(T.LC[0:64, :], T.NEG[0:64, lo:hi]), (T.Dp[:], T.KK[:, 0, 16 + lo:16 + hi]),
-                                           (T.D15[:], T.KK[:, 0, 15 + lo:15 + hi])], True, False),
-               "LC NEG Dp D15 KF KKp", "B%d" % h, 3 * (hi - lo))
-        for c in range(nch if rd == 0 else 0):
-            for name in ("X2", "X3", "X1", "GN2", "X4", "X0"):
-                gather(name, c)
-            esum("GN2", c)
-        for c, (lo, hi) in enumerate(CHUNKS):
-            for name in ("VG",) if rd == 0 else ("X2", "X3", "X1", "GN2", "VG", "X4", "X0"):
-                gather(name, c)
-            if rd == 1:
-                esum("GN2", c)
-            tt(T.PR[:, lo:hi], bk(hbank[c])[:, 0:hi - lo], T.VG[:, lo:hi], A.mult, "B%d VG%d" % (hbank[c], c), "PR%d" % c,
-               hi - lo)
-            esum("PR", c)
-            n = ecut[c + 1] - ecut[c]
-            sc(T.AE[:, ecut[c]:ecut[c + 1]], bk(ebank[c])[:, 0:n], "B%d" % ebank[c], "AE%d" % c, 1.0 / 16, AF.Abs,
-               -3 * LIFT[3] / 16, n)
-            h = c - nch + 2
-            if h < 0:
-                continue
-            lo, hi = parts[h]
-            ab, win = "ab"[h], T.AE[:] if h else T.AE[:, 0:ecut[-2]]
-            tt(T.GG[:, lo:hi], win.indirect(T.OF[:, 24 + lo // 16:24 + hi // 16]), T.CAP[:, lo:hi], A.min,
-               upto("AE", c) + " OF CAP" + " AEp" * h, "GG" + ab, GAT * (hi - lo))
-            mm([(bk(h)[:, 0:hi - lo], T.LQ[:], T.GG[:, lo:hi], False, True)], "LQ GG" + ab, "B%d" % h, hi - lo)
-            tt(T.PH[:, 16 + lo:16 + hi], bk(h)[:, 0:hi - lo], T.ZO[:, lo:hi], A.max, "B%d ZO" % h, "PH" + ab, hi - lo)
-            if rd == 1:
-                sc(T.YO[:, lo:hi], T.PH[:, 16 + lo:16 + hi], "PH" + ab, "YO" + ab, 1.0, AF.Identity, -128.0, hi - lo)
-                dma(T.y[:, lo:hi], T.YO[:, lo:hi], "dY", 32, "YO" + ab, "y" + ab, 100)
+        lists = {"N1": (2, 1, "G0"), "P1": (3, 2, "G0"), "K": (3, 0, "G0"), "N2": (2, 1, "GN1"), "P2": (3, 2, "GP1")}
+        def marks():
+            mm(group(T.B6[:, 0:C], [(T.SH[:], kf), (T.LE2[:], kb), (T.LE3[:], hb)]), "SH LE2 LE3 KFa KFb KHa KHb KKp", "B6",
+               3 * C)
+            sc(T.T1[:], T.B6[:, 0:C], "B6 cm8", "T1", -1.0, AF.Abs, cm[8], C)
+            mm(group(T.B7[:, 0:C], [(T.NI[:], T.PH[:, 16:]), (T.Dp[:], kf), (T.D15[:], kb)]),
+               "NI Dp D15 PHa PHb KFa KFb KKp", "B7", 3 * C)
+            sc(T.Z1[:], T.B7[:, 0:C], "B7", "Z1", -1.0, AF.Relu, -129.0, C)
+            sc(T.CAP[:], T.T1[:], "T1", "CAP", -63.0, AF.Relu, 63.0, C)
+            sc(T.ZO[:], T.Z1[:], "Z1", "ZO", 1.0, AF.Identity, 129.0, C)
+            for h, (lo, hi) in enumerate(parts):
+                mm(group(bk(h)[:, 0:hi - lo], [(T.LC[0:64, :], T.NEG[0:64, lo:hi]), (T.Dp[:], T.KK[:, 0, 16 + lo:16 + hi]),
+                                               (T.D15[:], T.KK[:, 0, 15 + lo:15 + hi])], True, False),
+                   "LC NEG Dp D15 KFa KFb KKp", "B%d" % h, 3 * (hi - lo))
+
+        for it in ORDER[rd].split():
+            a, rest = it[0], it[1:]
+            pin[0] = a if a in "VS" else "V" if a in "tPN" and PIN[rd] else "S" if a == "A" and PIN[rd] else None
+            if a in "VS-":
+                lo, hi = {"a": (0, 512), "b": (512, K), "c": (512, 768), "d": (768, K)}[rest[-1]]
+                gather(rest[:-1], lo, hi, 4 + lo // 512)
+            elif a in "ft":
+                listed(*lists[rest], "o" + rest, a)
+            elif a == "M":
+                marks()
+            elif a in "EPA":
+                c = int(rest)
+                lo, hi = ech[c], ech[c + 1]
+                if a == "P":
+                    tt(T.PR[:, lo:hi], bk(4 + lo // 512)[:, lo % 512:lo % 512 + hi - lo], T.VG[:, lo:hi], A.mult,
+                       "B%d " % (4 + lo // 512) + span("VG", lo, hi), span("PR", lo, hi), hi - lo)
+                if a == "A":
+                    n = ecol(hi) - ecol(lo)
+                    sc(T.AE[:, ecol(lo):ecol(hi)], bk(ebank[c])[:, 0:n], "B%d" % ebank[c], "AE%d" % c, 1.0 / 16, AF.Abs,
+                       -3 * LIFT[3] / 16, n)
+                else:
+                    esum("GN2" if a == "E" else "PR", c, lo, hi)
+            else:
+                h = int(rest[1])
+                lo, hi = parts[h]
+                ab, win = "ab"[h], T.AE[:] if h else T.AE[:, 0:ecol(ech[-2])]
+                if rest[0] == "g":
+                    at = 48 + (hi + lo) // 16 if rd == 1 and SPLIT else 48 * rd + 24 + lo // 16
+                    tt(T.GG[:, lo:hi], win.indirect(T.OF[:, at:at + (hi - lo) // 16]), T.CAP[:, lo:hi], A.min,
+                       upto("AE", 1 + h) + " OF%da OF%db CAP" % (rd, rd) + " AEp" * h, "GG" + ab, GAT * (hi - lo))
+                    mm([(bk(h)[:, 0:hi - lo], T.LQ[:], T.GG[:, lo:hi], False, True)], "LQ GG" + ab, "B%d" % h, hi - lo)
+                    continue
+                tt(T.PH[:, 16 + lo:16 + hi], bk(h)[:, 0:hi - lo], T.ZO[:, lo:hi], A.max, "B%d ZO" % h, "PH" + ab, hi - lo)
+                pin[0] = None
+                if rd == 0 and h == 0 and SPLIT:
+                    sample(1, 0, CUT, "a", 0, 4, 6)
+                if rd == 1:
+                    sc(T.YO[:, lo:hi], T.PH[:, 16 + lo:16 + hi], "PH" + ab, "YO" + ab, 1.0, AF.Identity, -128.0, hi - lo)
+                    dma(T.y[:, lo:hi], T.YO[:, lo:hi], "dY", 32, "YO" + ab, "y" + ab, 100)
+        pin[0] = None
     cnt, wait = issue(steps, Q, T)
     wait("G", "loc", total[0])
     for e in "VSPG":

@@ -3,27 +3,29 @@ from concourse.mybir import AluOpType as A, ActivationFunctionType as AF
 
 N, F, C, K, V, NSIM = 8, 6144, 384, 1024, 2048, 64
 ZONE, GAP = 1040, 1152
+WIDE, PRI = ((512, 512), (656, 368)), 0
 GCH = ((0, 512, 1024), (0, 512, 768, 1024))
 ECH = ((0, 512, 768, 1024), (0, 512, 768, 1024))
 CUT, SPLIT, TOL, LAM, HOLD = 192, False, 70, 0, 2
-AHEAD, DUP, FILL, POS = 2, False, 10, (1, 1, 2, 2)
-PELO, XA, AFTER = (), True, "TI1"
-ORDER = ("-G0a -G0b fN1 fP1 tN1 -GN1a tP1 -GN1b -GP1a -GP1b fK fN2 tK tN2 fP2 tP2 M -X2a -X3a -X1a -GN2a -X4a -X0a E0 "
-         "-X2b -X3b -X1b -GN2b -X4b -X0b E1 E2 -VGa P0 A0 -VGc P1 A1 -VGd P2 A2 Ng0 Ng1 Nn0 Nn1",
-         "M VG0a SG0b fN1 fP1 VX2a SX2b tN1 SX3a VGN1a tP1 fK SGP1a VGN1b fN2 tK SGP1b VX3b fP2 tN2 SX1a VVGa tP2 SX4a "
-         "VGN2a E0 SX1b VX0a SX4b VGN2b SX0b P0 E1 E2 SVGc VVGd P1 A0 P2 A1 A2 Ng0 Ng1 Nn0 Nn1")
-PIN = (False, True)
+AHEAD, DUP, FILL, POS = 2, 2, 10, (1, 1, 2, 2)
+PELO, XA, AFTER, WG, POSA = (1, 2), False, "TI1", 4, (1, 1, 1, 1)
+ORDER = ("VG0a SG0b fN1 fP1 tN1 SX2a VGN1a tP1 fK SGP1a VGN1b fN2 tK SGP1b M fP2 tN2 SX3a VGN2a E0 tP2 SX1a VGN2b E1 E2 "
+         "SX4a VX0a SX2b VX3b VX1b SX4b VVGa SX0b P0 SVGc SVGd P1 A0 P2 A1 A2 Ng0 Ng1 Nn0 Nn1",
+         "M VG0a SG0b fN1 fP1 VX2a SX2b tN1 SX3a VGN1a tP1 fK SGP1a VGN1b fN2 tK SGP1b VX3b fP2 tN2 SX1a VGN2a E0 tP2 "
+         "SX4a VGN2b E1 E2 SX1b VX0a SX4b VVGa SX0b P0 SVGc VVGd P1 A0 P2 A1 A2 Ng0 Ng1 Nn0 Nn1")
+PIN = (True, True)
+MV, DS, LOOK, PREF, FIRST, GS, ZN = 0, (0, 1, 2, 3, 4), 1, 1, True, 1, 64
 LIFT = (0.0, 9216.0, 0.0, 3072.0)
 SCRATCH = {}
 for _dt, _bufs in (
-    ("bfloat16", dict(XS=F, TB=F, VA=N * V, HS=1024, HB=3072, DG=8 * C, WL=40, DI=40 * 128, CR=C, CT=C, B15=144,
+    ("bfloat16", dict(XS=F, TB=F, VA=N * V, DG=8 * C, WL=40, DI=40 * 128, CR=C, CT=C, B15=144,
                       EF=3 * 144, EZ=144, ET=160, ES=6 * 128, NI=128, LC=128, L8=128, LS=128, TRa=128, TRb=128,
                       BM=128, TG=128, NEG=C, RAMP=C, CC=C, T1=C, CAP=C, Z1=C, ZO=C, PH=16 + C, W=2 * ZONE + 17 * GAP,
-                      cf=8, XF=192, OB=128, D4=128, SM=128, ZZ=ZONE // 2,
+                      cf=8, XF=192, OB=128, D4=128, LB=128, ZZ=ZONE // 2,
                       G0=K, GP1=K, X0=K, X1=K, X2=K, X3=K, X4=K, VG=K)),
     ("float16", dict(EK=144, LE=5 * 128, QM=128, SH=128, LE2=128, LE3=128, LQ=128, I64=128, S64=128, Dp=128, D15=128,
-                     BH=128, PR=K + 16, GG=C, GN1=K, GN2=K + 16, LR=5 * 128, EN=144)),
-    ("float32", dict(OH=16, TF=4 * C, I32=128, WF=40, cm=16, cs=8, M4=4, Mle=4, Mgt=4, AE=520, YO=C, SF=C)),
+                     BH=128, BR=128, PR=K + 16, GG=C, GN1=K, GN2=K + 16, LR=5 * 128, EN=144)),
+    ("float32", dict(OH=16, TF=4 * C, I32=128, WF=40, cm=16, M4=8, Mle=4, Mgt=4, AE=520, YO=C, SF=C)),
     ("int32", dict(TI=4 * C, PI=C, ci=8)),
     ("uint16", dict(OF=96, oT=64, oN1=64, oP1=64, oN2=64, oP2=64, oK=64)),
 ):
@@ -32,15 +34,19 @@ for _dt, _bufs in (
 SCRATCH["KK"] = ("sbuf", [128, 2, 16 + C], "float16")
 for _n in ("R15", "LA1", "LA2"):
     SCRATCH[_n] = ("sbuf", [128, 8, 16], "float16")
-SCRATCH["LB"] = ("sbuf", [128, 8, 16], "bfloat16")
 for _k in range(8):
     SCRATCH["B%d" % _k] = ("psum", [128, 512], "float32")
-SEMAPHORES = ["cV", "cS", "cP", "cG", "dP", "dW", "dT0", "dT1", "dT2", "dT3", "dX", "dV0", "dV1", "dR", "dY",
-              "loc", "out", "aw", "av", "ah0", "ah1", "a0", "a1", "a2", "a3", "a4", "a5"]
+SEMAPHORES = ["cV", "cS", "cP", "cG", "dP", "dW", "dT0", "dT1", "dT2", "dT3", "dX", "dR", "dY", "loc", "out", "aw", "av"]
+SEMAPHORES += ["%s%d" % (_n, _k) for _n in ("dV", "ah") for _k in range(4)] + ["a%d" % _k for _k in range(12)]
 
 
 def blk(t, k, n, m=1):
     return t[:, n * k:n * (k + m)]
+
+
+def piece(t, r, i, h, n=1):
+    w = [x for pair in WIDE for x in pair]
+    return t[:, V * r + sum(w[:2 * i + h]):V * r + sum(w[:2 * i + h + n])]
 
 
 def plan(T, topo):
@@ -81,32 +87,32 @@ def helper_program(g, core, T, topo, pl):
         e_rest = [e for e in e_on if e not in e_off]
         both = [pl[q]["core"] for q in p["pair"]]
         src = [[q for q in range(N) if pl[q]["to"][j] == r][0] for j in range(3)]
-        if core in (p["E"], p["O"], p["F"]):
-            w = blk(T.WL, r, 5)
-            g.wait_ge(T.sem.aw, len(e_on))
-            send([(w, [w, w], [pl[q]["core"] for q in p["far"][(p["E"], p["O"], p["F"]).index(core)]], e_off, "aw")])
         if core in (p["E"], p["O"]):
             h = int(core == p["O"])
-            for i in range(2):
-                s = blk(T.HS, i, 512)
+            w = blk(T.WL, r, 5)
+            to = [pl[q]["core"] for q in p["far"][h] + p["far"][2][h:h + 1]]
+            g.wait_ge(T.sem.aw, len(e_on))
+            send([(w, [w] * 3, to, e_off, "aw")] + [(w, [w], [pl[p["sib"]]["core"]], e_rest, "aw")][h:])
+            for i in range(len(WIDE)):
+                s = piece(T.VA, r, i, h)
                 g.wait_ge(T.sem["ah%d" % i], len(e_on) // 2)
                 for j, q in enumerate(p["to"]):
-                    trs = [(s, [blk(T.HB, 3 * i + j, 512)], [pl[q]["M"][i] if h else pl[q]["F"]], e_off, "a%d" % (3 * i + j))]
+                    trs = [(s, [s], [pl[q]["M"][i % 2] if h else pl[q]["F"]], e_off, "a%d" % (3 * i + j))]
                     if j == 0:
-                        trs.append((s, [blk(T.VA, 4 * r + 2 * i + h, 512)], [pl[p["sib"]]["core"]], e_rest, "av"))
+                        trs.append((s, [s], [pl[p["sib"]]["core"]], e_rest, "av"))
                     send(trs)
-        if core in p["M"]:
-            i = p["M"].index(core)
+        for i in range(len(WIDE)):
             for j in range(3):
-                g.wait_ge(T.sem["a%d" % (3 * i + j)], len(e_off))
-                send([(blk(T.HB, 3 * i + j, 512), [blk(T.HB, j, 512)], [p["EO"[i]]], e_off, "a%d" % j)])
-        if core in (p["E"], p["O"], p["F"]):
-            h = int(core != p["F"])
-            for k in range(3 if h else 6):
-                i, j = int(core == p["O"]) if h else k // 3, k % 3
-                g.wait_ge(T.sem["a%d" % k], len(e_off))
-                d = blk(T.VA, 4 * src[j] + 2 * i + h, 512)
-                send([(blk(T.HB, k, 512), [d, d], both, e_rest if h else e_on, "av")])
+                sem = "a%d" % (3 * i + j)
+                if core == p["M"][i % 2]:
+                    s = piece(T.VA, src[j], i, 1)
+                    g.wait_ge(T.sem[sem], len(e_off))
+                    send([(s, [s], [p["EO"[i % 2]]], e_off, sem)])
+                if core in (p["EO"[i % 2]], p["F"]):
+                    h = int(core != p["F"])
+                    s = piece(T.VA, src[j], i, h)
+                    g.wait_ge(T.sem[sem], len(e_off))
+                    send([(s, [s, s], both, e_rest if h else e_on, "av")])
     if total[0]:
         g.wait_ge(T.sem.loc, total[0])
 
@@ -159,8 +165,15 @@ def issue(steps, Q, T):
                 t, e, c, fn = min(((start(i, a[0]) + a[2], a[0], a[2], a[1]) for a in s["alt"]), key=lambda x: x[0] + LAM * x[2])
                 cand.append((t - c, -s["chain"], i, e, c, fn))
         cand.sort(key=lambda x: x[:3])
+        soon, est = list(cand), {x[2]: x[0] + x[4] + steps[x[2]]["lat"] + 1200 * (x[3] == "Y") for x in cand}
+        for x in cand[:LOOK and len(cand)]:
+            for i in steps[x[2]]["post"]:
+                s = steps[i]
+                if i not in est and len(s["alt"]) == 1 and all(j in done or j in est for j in s["pre"]):
+                    t = max([free[s["alt"][0][0]]] + [(done[j][0] if j in done else est[j]) + HOP for j in s["pre"]])
+                    soon.append((t, -s["chain"], i, s["alt"][0][0]))
         for x in cand:
-            if all(y[3] != x[3] or y[1] >= x[1] or y[0] >= x[0] + x[4] - TOL for y in cand):
+            if all(y[3] != x[3] or y[1] >= x[1] or y[0] >= x[0] + x[4] - TOL for y in soon):
                 break
         else:
             x = min((y for y in cand if y[3] == cand[0][3]), key=lambda y: y[1])
@@ -253,10 +266,10 @@ def rank_program(g, core, T, topo):
         step([sc_alt(out, a, scale, func, bias, n)], r, w)
 
     def scaled(out, a, col, r, w, n=128):
-        step([ts_alt(out, a, col, A.mult, n=n // 2), sc_alt(out, a, col, n=n)], r, w)
+        step([ts_alt(out, a, col, A.mult, n=n // 2), sc_alt(out, a, col, n=n)][PREF:], r, w)
 
     def line(out, a, mul, add, r, w):
-        step([ts_alt(out, a, mul, A.mult, add, A.add), sc_alt(out, a, mul, AF.Identity, add)], r, w)
+        step([ts_alt(out, a, mul, A.mult, add, A.add), sc_alt(out, a, mul, AF.Identity, add)][PREF:], r, w)
 
     def iota(out, pat, base, cm, w, n):
         step([("G", lambda: g.iota(out, pat, base, cm, allow_small_or_imprecise_dtypes=True), 130 + 2 * CYC * n)], "", w)
@@ -274,9 +287,10 @@ def rank_program(g, core, T, topo):
 
     wme = blk(T.WL, me, 5)
     dma(wme, T.w[:], "dW", 16, "", "wme", 20)
-    dma(blk(T.VA, 2 * me, 1024), blk(T.val, 0, 1024), "dV0", 16, "", "Vme0", 256)
-    dma(T.PI[:], T.pri[:], "dP", 16, "", "PI", 192)
-    dma(blk(T.VA, 2 * me + 1, 1024), blk(T.val, 1, 1024), "dV1", 16, "", "Vme1", 256)
+    for i in range(len(WIDE)):
+        dma(piece(T.VA, me, i, 0, 2), piece(T.val, 0, i, 0, 2), "dV%d" % i, 16, "", "Vme%d" % i, sum(WIDE[i]) // 4)
+        if i == PRI:
+            dma(T.PI[:], T.pri[:], "dP", 16, "", "PI", 192)
 
     def table(k, r):
         dma(blk(T.TI, k, C), [T.key, T.nxt, T.prv, T.rw][k][:], "dT%d" % k, 16, r, "TI%d" % k, 192)
@@ -289,28 +303,47 @@ def rank_program(g, core, T, topo):
     iota(T.XF[:], [[1, 192]], -32, 0, "XF", 192)
     iota(T.cf[:, 6:7], [[1, 1]], 0, 1, "cp", 1)
     iota(T.D4[:], [[4, 32], [0, 4]], 0, 0, "D4", 128)
-    step([("G", lambda: send([(wme, [wme] * 4, [p["E"], p["O"], p["F"], pl[p["sib"]]["core"]], e_on, "aw")]), 1300)],
-         "wme", "WL", 4500, ("aw", n_on + 6 * n_off))
+    step([("G", lambda: send([(wme, [wme] * 2, [p["E"], p["O"]], e_on, "aw")]), 1300)],
+         "wme", "WL", 4500, ("aw", n_on + 5 * n_off))
 
     def hand_on(i):
-        send([(blk(T.VA, 4 * me + 2 * i + h, 512), [blk(T.HS, i, 512)], [p["EO"[h]]],
-               e_on[n_on // 2 * h:n_on // 2 * (h + 1)], "ah%d" % i) for h in range(2)])
-    step([("G", lambda: hand_on(0), 300)], "Vme0", "gone", 1500, ("loc", 3 * n_on))
-    step([("G", lambda: hand_on(1), 300)], "Vme1", "VA ord", 16000, ("av", 16 * (n_on - n_off) + 12 * n_on))
-    step([("G", lambda: g.sem_inc(T.sem.out, 1), 10)], "Vme0 Vme1 wme", "issued", 0, ("out", 1))
+        trs = [(piece(T.VA, me, i, h), [piece(T.VA, me, i, h)], [p["EO"[h]]], e_on[n_on // 2 * h:n_on // 2 * (h + 1)],
+                "ah%d" % i) for h in range(2)]
+        for call in [trs] if WIDE[i][0] == WIDE[i][1] else [trs[1:], trs[:1]]:
+            send(call)
+    nw = len(WIDE)
+    mine = " ".join("Vme%d" % i for i in range(nw))
+    for i in range(nw - 1):
+        step([("G", lambda i=i: hand_on(i), 300 + 300 * (WIDE[i][0] != WIDE[i][1]))], "Vme%d" % i, "+gone", 1500,
+             ("loc", (nw + 1) * n_on))
+    step([("G", lambda: hand_on(nw - 1), 600)], mine, "VA", 16000, ("av", nw * (8 * (n_on - n_off) + 6 * n_on)))
+    step([("G", lambda: g.sem_inc(T.sem.out, 1), 10)], mine + " wme", "issued", 0, ("out", 1))
     early[0] = False
     for k in (1, 2, 3, 0)[AHEAD:]:
         table(k, "issued")
+    for j, at in enumerate((8, 9, 12, 13, 14, 15) if DUP == 2 else ()):
+        dma(T.TB[at:128:16, :], T.VA[16 * j:16 * j + 24, V * me:V * me + V], "dR", 256, mine, "+TBr", 70)
     if XA:
         dma(blk(T.XS, 0, F // 2), blk(T.x, 0, F // 2), "dX", 32, "gone", "+XS", 768)
 
-    iota(T.LB[0:1, :, :], [[0, 32], [5, 4]], 0, 0, "LB", 128)
-    iota(T.LB[0:1, :, 1:4], [[0, 8], [4, 3]], 4, 0, "+LB", 24)
-    iota(T.LB[0:1, :, 6:8], [[0, 16]], 0, 0, "+LB", 16)
-    iota(T.RAMP[0:1, :], [[0, 24], [GAP, 16]], GAP, 0, "RAMP", C)
+    if GS & 1:
+        for lo, hi, a in ((0, 4, 4), (4, 6, 5), (6, 8, 0), (8, 12, 5), (12, 16, 5)):
+            scaled(T.LB[0:1, lo:hi], T.XF[0:1, 32:32 + hi - lo], a / 1024, "XF", "+LB", 64)
+        for n in (16, 32, 64):
+            scaled(T.LB[0:1, n:2 * n], T.LB[0:1, 0:n], 1.0, "LB", "LB", 64)
+    else:
+        iota(T.LB[0:1, :], [[0, 32], [5, 4]], 0, 0, "LB", 128)
+        for m in (1, 2, 3, 6, 7):
+            iota(T.LB[0:1, m:128:16], [[0, 8]], 4 * m * (m < 4), 0, "+LB", 8)
+        scaled(T.LB[0:1, :], T.LB[0:1, :], 1.0 / 1024, "LB", "LB")
+    if GS & 2:
+        scaled(T.RAMP[0:1, 0:16], T.XF[0:1, 33:49], float(GAP), "XF", "RAMP", 64)
+        for n in (16, 32, 64, 128, 256):
+            scaled(T.RAMP[0:1, n:min(2 * n, C)], T.RAMP[0:1, 0:min(n, C - n)], 1.0, "RAMP", "RAMP", min(n, 128))
+    else:
+        iota(T.RAMP[0:1, :], [[0, 24], [GAP, 16]], GAP, 0, "RAMP", C)
     iota(T.CR[:], [[4, C]], 4 - 768, 0, "CR", C)
-    iota(T.SM[:], [[16, 8], [0, 4], [1, 4]], 0, 0, "SM", 128)
-    iota(T.SM[:, 7:128:16], [[16, 8]], 4, 0, "SM", 8)
+    early[0] = FIRST
     for k, (m, s) in enumerate(((112, 0), (15, 0), (124, 0), (3, 0), (14, 1), (7, 0))):
         ts(T.ci[:, k:k + 1], pc, m, A.bitwise_and, "pc", "ci%d" % k, s, A.logical_shift_right)
     cp(T.cf[:, 0:1], T.ci[:, 0:1], "ci0", "cg")
@@ -320,11 +353,14 @@ def rank_program(g, core, T, topo):
     oh = [T.OH[:, k:k + 1] for k in range(16)]
     cm = [T.cm[:, k:k + 1] for k in range(16)]
     ts(T.OH[:], T.XF[:, 32:48], ca, A.is_equal, "XF cf", "OH")
+    ts(T.BH[:], T.OB[:], cgb, A.is_equal, "OB cg", "BH")
+    ts(T.B15[:], T.XF[:, 17:161], cgb, A.is_equal, "XF cg", "B15", n=72)
+    early[0] = False
     line(cm[0], oh[15], -1.0, 1.0, "OH", "cm0")
     ms(T.NEG[:], -1024.0, "NEG", 192)
 
     early[0] = True
-    ms(T.ZZ[:], 0.0, "ZZ", ZONE // 4)
+    ms(T.ZZ[:, 0:ZN], 0.0, "ZZ", ZN // 2)
     for k in range(0 if DUP else FILL):
         sc(blk(T.TB, k, 512), T.ZZ[:, 0:512], "ZZ", "+TBb", n=512)
     early[0] = False
@@ -337,7 +373,6 @@ def rank_program(g, core, T, topo):
     def digits(k):
         b = k % 2
         if k in PELO:
-            ts(blk(T.TF, k, C), blk(T.TI, k, C), LIFT[k], A.add, "TI%d" % k, "TF%d" % k, n=C)
             mm([(bk(b)[:, 0:C], T.I32[:], blk(T.TF, k, C), True, False)], "I32 TF%d" % k, "B%d" % b, 4 * C)
             sc(blk(T.DG, 2 * k, C), blk(T.TF, k, C), "TF%d" % k, "DG%d" % (2 * k), n=C)
             mm([(bk(b)[:, 0:C], T.NI[:], blk(T.DG, 2 * k, C), False, True)], "NI DG%d" % (2 * k), "B%d" % b, C)
@@ -345,8 +380,8 @@ def rank_program(g, core, T, topo):
         else:
             split(k, b)
         for a in (2 * k, 2 * k + 1):
-            for at in (a, a + 8) if DUP else (a,):
-                dma(T.TB[at:128:16, :], blk(T.DG, a, C), "dR", 256 if DUP else 128, "DG%d TBb" % a, "+TBr", 96)
+            for at in (a, a + 8) if DUP == 1 or k == 1 else (a,):
+                dma(T.TB[at:128:16, :], blk(T.DG, a, C), "dR", 256 if DUP else 160, "DG%d TBb" % a, "+TBr", 96)
 
     def split(k, b):
         ts(bk(b)[:, 0:C], blk(T.TI, k, C), LIFT[k], A.add, "TI%d" % k, "B%d" % b, n=C)
@@ -360,8 +395,7 @@ def rank_program(g, core, T, topo):
 
     ms(T.PH[:, 0:16], 128.0, "PHp")
     ms(T.L8[0:1, :], 1.0 / 128, "L8")
-    ts(T.BM[:], T.OB[:], cgb, A.is_equal, "OB cg", "BM0", 1.0 / 256, A.mult)
-    ts(T.BH[:], T.OB[:], cgb, A.is_equal, "OB cg", "BH")
+    scaled(T.BM[:], T.BH[:], 1.0 / 256, "BH", "BM0")
     ts(T.TG[:], x128, cpp, A.is_ge, "XF cp", "TG")
     tt(T.TRa[:], T.TG[:], T.BM[:], A.mult, "TG BM0", "TRa", 256)
     tt(T.TRb[:], T.BM[:], T.TRa[:], A.subtract, "TRa BM0", "TRb", 256)
@@ -369,11 +403,9 @@ def rank_program(g, core, T, topo):
 
     scaled(T.KK[:, :, 0:16], T.NEG[:, 0:32], 2.0, "NEG", "KKp", 64)
     scaled(T.R15[:], T.BH[:], oh[15], "BH OH", "R15")
-    scaled(T.LB[0:1, :, :], T.LB[0:1, :, :], 1.0 / 1024, "LB", "LB")
     ms(T.LS[0:1, :], 0.0, "LS")
     ms(T.LS[0:1, 7:128:16], 1.0, "LS")
     scaled(T.LA2[:], T.R15[:], -5.0, "R15", "LA2")
-    ts(T.B15[:], T.XF[:, 17:161], cgb, A.is_equal, "XF cg", "B15", n=72)
     line(cm[9], cpp, 1.0, 1.0, "cp", "cm9")
     ts(T.SH[:], T.D4[:], cm[9], A.is_equal, "D4 cm9 cm0", "SH", cm[0], A.mult)
     ts(T.QM[:], T.D4[:], cq4, A.is_equal, "D4 cf", "QM")
@@ -391,13 +423,17 @@ def rank_program(g, core, T, topo):
     ts(cm[4], cm[2], oh[7], A.add, "cm2 OH", "cm4", -1.0, A.add)
     line(cm[5], cm[3], 1.0, cgb, "cm3 cf", "cm5")
     for k in range(4):
-        zero(blk(T.W, k, ZONE // 2), ZONE // 2, "+W" if k > 1 else "+Wz")
+        if k < WG:
+            iota(blk(T.W, k, ZONE // 2), [[0, ZONE // 2]], 0, 0, "+W" if k > 1 else "+Wz", ZONE // 2)
+        else:
+            zero(blk(T.W, k, ZONE // 2), ZONE // 2, "+W" if k > 1 else "+Wz")
     sc(T.CT[:], T.CR[:], "CR cm2 cm4", "CT", cm[2], AF.Identity, cm[4], C)
 
     ts(T.Mle[:], x4, cm[3], A.is_ge, "XF cm3", "Mle")
     ts(T.Mgt[:], x4, cm[3], A.is_lt, "XF cm3", "Mgt")
     ts(T.ET[:], T.XF[:, 17:177], cm[5], A.is_equal, "XF cm5", "ET", n=80)
-    ts(T.M4[:], x4, ca2, A.is_equal, "XF cf", "M4")
+    ts(T.M4[:], T.XF[:, 32:40], ca2, A.is_equal, "XF cf", "M4")
+    ts(cm[10], ca, 7.5, A.is_lt, "cf", "cm10")
     for s in range(3):
         scaled(blk(T.ES, 2 * s, 128), T.ET[:, s:s + 128], T.Mle[:, s:s + 1], "ET Mle", "+ES")
         scaled(blk(T.ES, 2 * s + 1, 128), T.ET[:, 16 + s:144 + s], T.Mgt[:, s:s + 1], "ET Mgt", "+ES")
@@ -407,9 +443,8 @@ def rank_program(g, core, T, topo):
 
     line(cm[7], oh[7], 8.0, cq4, "OH cf", "cm7")
     ts(cm[8], oh[7], cr, A.add, "OH cf", "cm8", 2048.0, A.add)
-    line(T.cs[:, 0:5], T.XF[:, 32:37], 1.0, cgb, "XF cf", "cs")
     scaled(T.SH[:, 7:128:16], T.BH[:, 7:128:16], oh[11], "BH OH", "SH", 64)
-    ts(T.LE2[:], T.D4[:], T.cs[:, 0:1], A.is_equal, "D4 cs OH", "LE2", oh[15], A.mult)
+    select(T.LE2[:], T.R15[:], [[0, 8], [-1, 16]], A.is_ge, 0.0, 3, 0, "R15", "LE2")
     scaled(T.LE3[:], T.R15[:], -2.0, "R15", "LE3")
     scaled(T.I64[:], T.BH[:], -64.0, "BH", "I64")
     select(T.S64[:], T.I64[:], [[1, 128]], A.is_equal, 0.0, -1, -1, "I64", "S64")
@@ -418,23 +453,26 @@ def rank_program(g, core, T, topo):
     ts(T.LQ[:], T.D4[:], cm[7], A.is_equal, "D4 cm7", "LQ")
     ms(T.LC[0:32, :], -2.0 ** -9, "+LC")
     ms(T.LC[32:64, :], 15 * 2.0 ** -20, "+LC")
-    for s in range(5):
-        ts(blk(T.LE, s, 128), T.SM[:], T.cs[:, s:s + 1], A.is_equal, "SM cs", "LE%d" % s)
-        scaled(blk(T.LR, s, 128), blk(T.LE, s, 128), T.M4[:, 3:4], "LE%d M4" % s, "+LR")
+    scaled(T.BR[:], T.BH[:], T.M4[:, 3:4], "BH M4", "BR")
+    for m, src in (("LR", "BR"), ("LE", "BH")):
+        for s in range(5):
+            pat, at = ([[0, 32], [1, 4]], s) if s < 4 else ([[0, 8], [1, 16]], 7)
+            select(blk(T[m], s, 128), T[src][:], pat, A.is_equal, 0.0, -at, 0, src, m + str(s))
+        iota(T[m][:, 3 * 128 + 7:4 * 128:16], [[0, 8]], 0, 0, m + "3", 8)
     for t in ("GN2", "PR"):
         scaled(T[t][:, K:], T.ZZ[:, 0:16], 1.0, "ZZ", t + "p", 64)
-    scaled(T.EN[:], blk(T.EF, 1, 144), -1.0, "EF1", "EN", 144)
+    scaled(T.EN[:], T.B15[:], T.M4[:, 5:6], "B15 M4", "EN", 144)
     zero(T.AE[:, 512:], 8, "AEp")
     sc(T.WF[:], T.WL[:], "WL wme", "WF", -1.0)
     for d in (2, 3, 1, 4, 0):
         for q in range(N):
             o, j = blk(T.DI, 8 * d + q, 128), 5 * q + d
-            step([ts_alt(o, T.NI[:], T.WL[:, j:j + 1], A.mult, -1.0, A.mult), sc_alt(o, T.NI[:], T.WF[:, j:j + 1], n=128)],
+            step([ts_alt(o, T.NI[:], T.WL[:, j:j + 1], A.mult, -1.0, A.mult), sc_alt(o, T.NI[:], T.WF[:, j:j + 1], n=128)][:1 + (d in DS)],
                  "NI WF WL wme", "+DI%d" % d)
 
     src_of = {"G0": "TB oT", "GN1": "TB oN1", "GP1": "TB oP1", "GN2": "TB oN2", "X0": "XS oP2", "X1": "XS oP1",
               "X2": "XS oT", "X3": "XS oN1", "X4": "XS oN2", "VG": "VA oK"}
-    also = {"TB": "TBr", "XS": "XS", "VA": "VA Vme0 Vme1"}
+    also = {"TB": "TBr", "XS": "XS", "VA": "VA " + mine}
     hbank, ebank = (4, 5, 2), (6, 7, 3)
     seen = {}
 
@@ -449,7 +487,7 @@ def rank_program(g, core, T, topo):
         return " ".join(name + str(j) for j in range(h + 1))
 
     def listed(b, k, src, name, what):
-        terms = [("EF", 144 * k, "EF%d" % k, "G0"), ("EN", 0, "EN", src)] if src == "GN1" else [("EF", 144 * k, "EF%d" % k, src)]
+        terms = [("EN", 0, "EN", src)] if src == "GN1" else [("EF", 144 * k, "EF%d" % k, src)]
         for j, (m, at, mk, x) in enumerate(terms):
             if what == "f":
                 mm(group(bk(b)[:, 0:64], [(T[m][:, at + 15 - u:at + 143 - u], T[x][:, u:K:16]) for u in range(16)],
@@ -457,26 +495,31 @@ def rank_program(g, core, T, topo):
         if what == "f":
             return
         if k:
-            ts(T[name][:], bk(b)[:, 0:64], -1.0 if src == "GN1" else 1.0, A.mult, "B%d" % b, name, -LIFT[k], A.add)
+            ts(T[name][:], bk(b)[:, 0:64], -LIFT[k], A.add, "B%d" % b, name)
         else:
             ts(T[name][:], bk(b)[:, 0:64], cq, A.add, "B%d cf" % b, name, float(V), A.mult)
 
-    def gather(name, lo, hi, b=None):
+    def gather(name, lo, hi):
         win, off = src_of[name].split()
         o, a, c = T[name][:, lo:hi], T[win][:].indirect(T[off][:, lo // 16:hi // 16]), GAT * CYC * (hi - lo)
         r, w = also[win] + " " + off, span(name, lo, hi)
         if name in ("GN1", "GN2"):
             old = {"GN1": "G0", "GN2": "GN1"}[name]
             return tt(o, a, T[old][:, lo:hi], A.add, r + " " + span(old, lo, hi), w, c / CYC + 25)
+        if name == "G0":
+            return step([ts_alt(o, a, cm[10], A.mult, n=c / CYC + 25), sc_alt(o, a, cm[10], n=c / CYC + 40)], r + " cm10", w)
         step([("V", lambda: vec.tensor_copy(o, a), 50 + c), ("S", lambda: act.activation(o, a, AF.Copy), 65 + c)], r, w)
-        if win == "XS":
-            d = int(name[1])
+        for at in range(lo, hi, 512) if win == "XS" else ():
+            weigh(name, at)
 
-            def items():
-                first, last = turn(b, 5)
-                return [(bk(b)[:, q:hi - lo:8], blk(T.DI, 8 * d + q, 128), T[name][:, lo + q:hi:8], first and q == 0,
-                         last and q == 7) for q in range(N)]
-            mm(items, w + " DI%d" % d, "+B%d" % b, 512)
+    def weigh(name, lo):
+        d, b = int(name[1]), 4 + lo // 512
+
+        def items():
+            first, last = turn(b, 5)
+            return [(bk(b)[:, q:512:8], blk(T.DI, 8 * d + q, 128), T[name][:, lo + q:lo + 512:8], first and q == 0,
+                     last and q == 7) for q in range(N)]
+        mm(items, span(name, lo, lo + 512) + " DI%d" % d, "+B%d" % b, 512)
 
     def ecol(k):
         return min(max(k // 2 - 2, 0), 512) if k < K else 512
@@ -485,9 +528,12 @@ def rank_program(g, core, T, topo):
         lo, hi, b, m = ecol(k0), ecol(k1), ebank[c], "LE" if name == "PR" else "LR"
         mm(lambda: group(bk(b)[:, 0:hi - lo], [(blk(T[m], s, 128), T[name][:, 2 * lo + s:2 * hi + s:2]) for s in range(5)],
                          *turn(b + 10, 2)),
-           (upto(m, 4) if name == "PR" else m) + " " + span(name, 0, k1) + " " + name + "p", "+B%d" % b, 5 * (hi - lo))
+           upto(m, 4) + " " + span(name, 0, k1) + " " + name + "p", "+B%d" % b, 5 * (hi - lo))
 
     def lay(rd, at):
+        for k, a in zip((1, 2, 3, 0), POSA):
+            if rd == 0 and a == at and k in PELO:
+                ts(blk(T.TF, k, C), blk(T.TI, k, C), LIFT[k], A.add, "TI%d" % k, "TF%d" % k, n=C)
         for k, a in zip((1, 2, 3, 0), POS):
             if rd == 0 and a == at:
                 digits(k)
@@ -502,7 +548,7 @@ def rank_program(g, core, T, topo):
             mm(group(bk(bs)[:, c0 - lo:c1 - lo], [(T.TRa[:], T.PH[:, 16 + c0:16 + c1]), (T.TRb[:], T.PH[:, 15 + c0:15 + c1])],
                      False, x == ab[-1]), "TRa TRb PHa PHp PH" + x, "B%d" % bs, 2 * (c1 - c0))
         lay(rd, 0)
-        mm(group(bk(ba)[:, 0:n], [(T.LB[0:1, :, :], T.NEG[0:1, 0:n]), (T.LS[0:1, :], T.RAMP[0:1, 0:n])], True, False),
+        mm(group(bk(ba)[:, 0:n], [(T.LB[0:1, :], T.NEG[0:1, 0:n]), (T.LS[0:1, :], T.RAMP[0:1, 0:n])], True, False),
            "LB LS NEG RAMP", "B%d" % ba, 2 * n)
         out, init = T.SF[:, 0:n] if hi < C else f, T.SF[:, lo - 1:lo] if lo else -2048.498046875
         step([("V", lambda: vec.tensor_tensor_scan(out, bk(bs)[:, 0:n], T.NEG[:, 0:n], init, A.add, A.min), cost(n))],
@@ -547,12 +593,18 @@ def rank_program(g, core, T, topo):
         def marks():
             mm(group(T.B6[:, 0:C], [(T.SH[:], kf), (T.LE2[:], kb), (T.LE3[:], hb)]), "SH LE2 LE3 KFa KFb KHa KHb KKp", "B6",
                3 * C)
-            sc(T.T1[:], T.B6[:, 0:C], "B6 cm8", "T1", -1.0, AF.Abs, cm[8], C)
             mm(group(T.B7[:, 0:C], [(T.NI[:], T.PH[:, 16:]), (T.Dp[:], kf), (T.D15[:], kb)]),
                "NI Dp D15 PHa PHb KFa KFb KKp", "B7", 3 * C)
-            sc(T.Z1[:], T.B7[:, 0:C], "B7", "Z1", -1.0, AF.Relu, -129.0, C)
-            sc(T.CAP[:], T.T1[:], "T1", "CAP", -63.0, AF.Relu, 63.0, C)
-            sc(T.ZO[:], T.Z1[:], "Z1", "ZO", 1.0, AF.Identity, 129.0, C)
+            if rd == 0 and MV & 1:
+                ts(T.CAP[:], T.B6[:, 0:C], cm[8], A.is_equal, "B6 cm8", "CAP", 63.0, A.mult, C)
+            else:
+                sc(T.T1[:], T.B6[:, 0:C], "B6 cm8", "T1", -1.0, AF.Abs, cm[8], C)
+                sc(T.CAP[:], T.T1[:], "T1", "CAP", -63.0, AF.Relu, 63.0, C)
+            if rd == 0 and MV & 2:
+                ts(T.ZO[:], T.B7[:, 0:C], -1.0, A.mult, "B7", "ZO", 129.0, A.max, C)
+            else:
+                sc(T.Z1[:], T.B7[:, 0:C], "B7", "Z1", -1.0, AF.Relu, -129.0, C)
+                sc(T.ZO[:], T.Z1[:], "Z1", "ZO", 1.0, AF.Identity, 129.0, C)
             for h, (lo, hi) in enumerate(parts):
                 mm(group(bk(h)[:, 0:hi - lo], [(T.LC[0:64, :], T.NEG[0:64, lo:hi]), (T.Dp[:], T.KK[:, 0, 16 + lo:16 + hi]),
                                                (T.D15[:], T.KK[:, 0, 15 + lo:15 + hi])], True, False),
@@ -562,8 +614,8 @@ def rank_program(g, core, T, topo):
             a, rest = it[0], it[1:]
             pin[0] = a if a in "VS" else "V" if a in "tPN" and PIN[rd] else "S" if a == "A" and PIN[rd] else None
             if a in "VS-":
-                lo, hi = {"a": (0, 512), "b": (512, K), "c": (512, 768), "d": (768, K)}[rest[-1]]
-                gather(rest[:-1], lo, hi, 4 + lo // 512)
+                lo, hi = {"a": (0, 512), "b": (512, K), "c": (512, 768), "d": (768, K), "w": (0, K)}[rest[-1]]
+                gather(rest[:-1], lo, hi)
             elif a in "ft":
                 listed(*lists[rest], "o" + rest, a)
             elif a == "M":

from concourse.bass import DstId, RemoteDMATransfer
from concourse.mybir import AluOpType as A, ActivationFunctionType as AF

N, F, C, K, V, NSIM = 8, 6144, 384, 1024, 2048, 64
ZONE, GAP = 1040, 1152
WIDE, PRI = ((512, 512), (656, 368)), 0
GCH = ((0, 512, 1024), (0, 512, 768, 1024))
ECH = ((0, 512, 768, 1024), (0, 512, 768, 1024))
CUT, SPLIT, TOL, LAM, HOLD = 192, False, 70, 0, 2
AHEAD, DUP, FILL, POS = 2, 2, 10, (1, 1, 2, 2)
PELO, XA, AFTER, WG, POSA = (1, 2), False, "TI1", 4, (1, 1, 1, 1)
ORDER = ("VG0a SG0b fN1 fP1 tN1 SX2a VGN1a tP1 fK SGP1a VGN1b fN2 tK SGP1b M fP2 tN2 SX3a VGN2a E0 tP2 SX1a VGN2b E1 E2 "
         "SX4a VX0a SX2b VX3b VX1b SX4b VVGa SX0b P0 SVGc SVGd P1 A0 P2 A1 A2 Ng0 Ng1 Nn0 Nn1",
         "M VG0a SG0b fN1 fP1 VX2a SX2b tN1 SX3a VGN1a tP1 fK SGP1a VGN1b fN2 tK SGP1b VX3b fP2 tN2 SX1a VGN2a E0 tP2 "
         "SX4a VGN2b E1 E2 SX1b VX0a SX4b VVGa SX0b P0 SVGc VVGd P1 A0 P2 A1 A2 Ng0 Ng1 Nn0 Nn1")
PIN = (True, True)
MV, DS, LOOK, PREF, FIRST, GS, ZN = 0, (0, 1, 2, 3, 4), 1, 1, True, 1, 64
LIFT = (0.0, 9216.0, 0.0, 3072.0)
SCRATCH = {}
for _dt, _bufs in (
    ("bfloat16", dict(XS=F, TB=F, VA=N * V, DG=8 * C, WL=40, DI=40 * 128, CR=C, CT=C, B15=144,
                      EF=3 * 144, EZ=144, ET=160, ES=6 * 128, NI=128, LC=128, L8=128, LS=128, TRa=128, TRb=128,
                      BM=128, TG=128, NEG=C, RAMP=C, CC=C, T1=C, CAP=C, Z1=C, ZO=C, PH=16 + C, W=2 * ZONE + 17 * GAP,
                      cf=8, XF=192, OB=128, D4=128, LB=128, ZZ=ZONE // 2,
                      G0=K, GP1=K, X0=K, X1=K, X2=K, X3=K, X4=K, VG=K)),
    ("float16", dict(EK=144, LE=5 * 128, QM=128, SH=128, LE2=128, LE3=128, LQ=128, I64=128, S64=128, Dp=128, D15=128,
                     BH=128, BR=128, PR=K + 16, GG=C, GN1=K, GN2=K + 16, LR=5 * 128, EN=144)),
    ("float32", dict(OH=16, TF=4 * C, I32=128, WF=40, cm=16, M4=8, Mle=4, Mgt=4, AE=520, YO=C, SF=C)),
    ("int32", dict(TI=4 * C, PI=C, ci=8)),
    ("uint16", dict(OF=96, oT=64, oN1=64, oP1=64, oN2=64, oP2=64, oK=64)),
):
    for _n, _w in _bufs.items():
        SCRATCH[_n] = ("sbuf", [128, _w], _dt)
SCRATCH["KK"] = ("sbuf", [128, 2, 16 + C], "float16")
for _n in ("R15", "LA1", "LA2"):
    SCRATCH[_n] = ("sbuf", [128, 8, 16], "float16")
for _k in range(8):
    SCRATCH["B%d" % _k] = ("psum", [128, 512], "float32")
SEMAPHORES = ["cV", "cS", "cP", "cG", "dP", "dW", "dT0", "dT1", "dT2", "dT3", "dX", "dR", "dY", "loc", "out", "aw", "av"]
SEMAPHORES += ["%s%d" % (_n, _k) for _n in ("dV", "ah") for _k in range(4)] + ["a%d" % _k for _k in range(12)]


def blk(t, k, n, m=1):
    return t[:, n * k:n * (k + m)]


def piece(t, r, i, h, n=1):
    w = [x for pair in WIDE for x in pair]
    return t[:, V * r + sum(w[:2 * i + h]):V * r + sum(w[:2 * i + h + n])]


def plan(T, topo):
    cores, out = list(T.cores), []
    chips = sorted(set(topo.chip(c) for c in cores))
    for r, c in enumerate(cores):
        mate = [k for k in range(NSIM) if topo.mates(topo.chip(c), topo.chip(k)) and topo.die(k) == topo.die(c)]
        here = [k for k in topo.cores_of(c) if topo.die(k) == topo.die(c) and k != c]
        own = [k for k in here if topo.may_write(k, mate[0])]
        i = chips.index(topo.chip(c))
        sets = [[q for q in range(N) if topo.chip(cores[q]) == chips[(i + k) % len(chips)]] for k in range(len(chips))]
        out.append(dict(core=c, E=[k for k in here if k not in own][0], O=own[0], F=own[1],
                        M=[k for k in mate if topo.may_write(k, c)], pair=sets[0], far=sets[1:],
                        sib=[q for q in sets[0] if q != r][0],
                        to=[[q for q in s if topo.die(cores[q]) == topo.die(c)][0] for s in sets[1:]]))
    return out


def sender(g, core, T, topo):
    total = [0]

    def send(trs):
        out = []
        for s, ds, cs, es, sm in trs:
            ids = [DstId(rid=topo.addr(c)[0], pnc=topo.addr(c)[1]) for c in cs]
            out.append(RemoteDMATransfer(dst_ids=ids, dma_engine_mask=sum(1 << e for e in es), remote_sem=T.sem[sm],
                                         srcs=[s], dsts=ds))
            total[0] += len(es)
        g.remote_dma_fused(out, local_sem=T.sem.loc)
    return send, total


def helper_program(g, core, T, topo, pl):
    send, total = sender(g, core, T, topo)
    for r, p in enumerate(pl):
        e_on = topo.engines(core, [k for k in topo.cores_of(core) if k != core][0])
        e_off = topo.engines(core, pl[p["to"][0]]["core"])
        e_rest = [e for e in e_on if e not in e_off]
        both = [pl[q]["core"] for q in p["pair"]]
        src = [[q for q in range(N) if pl[q]["to"][j] == r][0] for j in range(3)]
        if core in (p["E"], p["O"]):
            h = int(core == p["O"])
            w = blk(T.WL, r, 5)
            to = [pl[q]["core"] for q in p["far"][h] + p["far"][2][h:h + 1]]
            g.wait_ge(T.sem.aw, len(e_on))
            send([(w, [w] * 3, to, e_off, "aw")] + [(w, [w], [pl[p["sib"]]["core"]], e_rest, "aw")][h:])
            for i in range(len(WIDE)):
                s = piece(T.VA, r, i, h)
                g.wait_ge(T.sem["ah%d" % i], len(e_on) // 2)
                for j, q in enumerate(p["to"]):
                    trs = [(s, [s], [pl[q]["M"][i % 2] if h else pl[q]["F"]], e_off, "a%d" % (3 * i + j))]
                    if j == 0:
                        trs.append((s, [s], [pl[p["sib"]]["core"]], e_rest, "av"))
                    send(trs)
        for i in range(len(WIDE)):
            for j in range(3):
                sem = "a%d" % (3 * i + j)
                if core == p["M"][i % 2]:
                    s = piece(T.VA, src[j], i, 1)
                    g.wait_ge(T.sem[sem], len(e_off))
                    send([(s, [s], [p["EO"[i % 2]]], e_off, sem)])
                if core in (p["EO"[i % 2]], p["F"]):
                    h = int(core != p["F"])
                    s = piece(T.VA, src[j], i, h)
                    g.wait_ge(T.sem[sem], len(e_off))
                    send([(s, [s, s], both, e_rest if h else e_on, "av")])
    if total[0]:
        g.wait_ge(T.sem.loc, total[0])


HOP, CYC, PEC, GAT, SCA = 70, 0.83, 0.45, 1.5, 3.5


def issue(steps, Q, T):
    wrote, pieces, read = {}, {}, {}
    last = {}
    for i, s in enumerate(steps):
        pre = set()
        for k in s["r"]:
            pre.update(wrote.get(k, []))
        for k in s["w"]:
            n = k.lstrip("+")
            if k[0] == "+" and n in pieces and not read.get(n):
                pre.update(pieces[n])
            else:
                old = wrote.get(n, []) + read.get(n, [])
                pre.update(old)
                wrote[n], read[n] = [], []
                pieces.pop(n, None)
                if k[0] == "+":
                    pieces[n] = old
            wrote[n].append(i)
        for k in s["r"]:
            read.setdefault(k, []).append(i)
        pre.discard(i)
        s["pre"], s["post"], s["behind"] = pre, [], last.get(s["row"])
        if s["row"]:
            last[s["row"]] = i
    for i, s in enumerate(steps):
        for j in s["pre"]:
            steps[j]["post"].append(i)
    for i in reversed(range(len(steps))):
        s = steps[i]
        s["chain"] = max([-i if s["early"] else -len(steps)] + [steps[j]["chain"] + 0.01 for j in s["post"]])
    free, done, order, pipe = {e: 0.0 for e in Q}, {}, [], [0.0]
    todo = set(range(len(steps)))

    def start(i, e):
        s = steps[i]
        return max([free[e]] + [done[j][0] + (0 if e == "P" == done[j][1] else HOP) for j in s["pre"]])
    while todo:
        cand = []
        for i in todo:
            s = steps[i]
            if all(j in done for j in s["pre"]) and (s["behind"] is None or s["behind"] in done):
                t, e, c, fn = min(((start(i, a[0]) + a[2], a[0], a[2], a[1]) for a in s["alt"]), key=lambda x: x[0] + LAM * x[2])
                cand.append((t - c, -s["chain"], i, e, c, fn))
        cand.sort(key=lambda x: x[:3])
        soon, est = list(cand), {x[2]: x[0] + x[4] + steps[x[2]]["lat"] + 1200 * (x[3] == "Y") for x in cand}
        for x in cand[:LOOK and len(cand)]:
            for i in steps[x[2]]["post"]:
                s = steps[i]
                if i not in est and len(s["alt"]) == 1 and all(j in done or j in est for j in s["pre"]):
                    t = max([free[s["alt"][0][0]]] + [(done[j][0] if j in done else est[j]) + HOP for j in s["pre"]])
                    soon.append((t, -s["chain"], i, s["alt"][0][0]))
        for x in cand:
            if all(y[3] != x[3] or y[1] >= x[1] or y[0] >= x[0] + x[4] - TOL for y in soon):
                break
        else:
            x = min((y for y in cand if y[3] == cand[0][3]), key=lambda y: y[1])
        t, _, i, e, c, fn = x
        free[e] = t + c
        end = t + c + steps[i]["lat"]
        if e == "Y":
            pipe[0] = max(pipe[0], t + 600) + steps[i]["lat"]
            end = pipe[0] + 600
        done[i] = (end, e)
        order.append((t, i, e, fn))
        todo.remove(i)
    cnt, tok, waited = {e: 0 for e in "VSPG"}, {}, {e: {} for e in Q}

    def wait(e, sem, v):
        if waited[e].get(sem, 0) < v:
            Q[e].wait_ge(T.sem[sem], v)
            waited[e][sem] = v
    for t, i, e, fn in order:
        need = {}
        for j in steps[i]["pre"]:
            if not e == "P" == done[j][1]:
                need[tok[j][0]] = max(need.get(tok[j][0], 0), tok[j][1])
        for sem, v in need.items():
            wait(e, sem, v)
        ins, tok[i] = fn(), steps[i]["tok"]
        if e == "Y":
            ins.then_inc(T.sem[tok[i][0]], 16)
        elif tok[i] is None:
            cnt[e] += 1
            ins.then_inc(T.sem["c" + e], 1)
            tok[i] = ("c" + e, cnt[e])
    return cnt, wait


def rank_program(g, core, T, topo):
    me, pl = T.rank_of(core), plan(T, topo)
    if me is None:
        return helper_program(g, core, T, topo, pl)
    Q = {"V": g.vector, "S": g.scalar, "P": g.tensor, "G": g, "Y": g.sync}
    vec, act = g.vector, g.scalar
    steps, early, pin = [], [0], [None]

    def step(alt, r, w, lat=0, tok=None):
        r, w = r.split(), w.split()
        banks = [k for k in r if len(k) == 2 and k[0] == "B" and k[1] in "01234567"]
        alt = [a for a in alt if a[0] == pin[0]] or alt
        steps.append(dict(alt=alt, row=alt[0][0] if alt[0][0] in ("Y", pin[0]) else None, r=[k for k in r if k not in banks], w=w + banks, lat=lat, tok=tok, early=early[0]))

    def cost(n):
        return 30 + CYC * max(64, n)

    def dma(out, in_, sem, val, r, w, kb):
        step([("Y", lambda: g.sync.dma_start(out, in_), 60)], r, w, 1.6 * kb, (sem, val))

    def mm(items, r, w, n):
        def fn():
            its = items if isinstance(items, list) else items()
            for it in its[:-1]:
                g.tensor.matmul(*it)
            return g.tensor.matmul(*its[-1])
        step([("P", fn, PEC * n)], r, w)

    def group(out, pairs, first=True, last=True):
        return [(out, l, x, first and i == 0, last and i == len(pairs) - 1) for i, (l, x) in enumerate(pairs)]

    def ts_alt(out, in0, s1, o0, s2=None, o1=None, n=64):
        if o1 is None:
            return ("V", lambda: vec.tensor_scalar(out, in0, s1, None, o0), cost(n))
        return ("V", lambda: vec.tensor_scalar(out, in0, s1, s2, o0, o1), cost(n))

    def sc_alt(out, a, scale=1.0, func=AF.Copy, bias=None, n=64):
        if bias is None:
            return ("S", lambda: act.activation(out, a, func, scale=scale), cost(n))
        return ("S", lambda: act.activation(out, a, func, bias=bias, scale=scale), cost(n))

    def ts(out, in0, s1, o0, r, w, s2=None, o1=None, n=64):
        step([ts_alt(out, in0, s1, o0, s2, o1, n)], r, w)

    def tt(out, a, b, o, r, w, n=64):
        step([("V", lambda: vec.tensor_tensor(out, a, b, o), cost(n))], r, w)

    def cp(out, a, r, w, n=64):
        step([("V", lambda: vec.tensor_copy(out, a), cost(n))], r, w)

    def ms(out, c, w, n=64):
        step([("V", lambda: vec.memset(out, c), cost(n))], "", w)

    def sc(out, a, r, w, scale=1.0, func=AF.Copy, bias=None, n=64):
        step([sc_alt(out, a, scale, func, bias, n)], r, w)

    def scaled(out, a, col, r, w, n=128):
        step([ts_alt(out, a, col, A.mult, n=n // 2), sc_alt(out, a, col, n=n)][PREF:], r, w)

    def line(out, a, mul, add, r, w):
        step([ts_alt(out, a, mul, A.mult, add, A.add), sc_alt(out, a, mul, AF.Identity, add)][PREF:], r, w)

    def iota(out, pat, base, cm, w, n):
        step([("G", lambda: g.iota(out, pat, base, cm, allow_small_or_imprecise_dtypes=True), 130 + 2 * CYC * n)], "", w)

    def select(out, a, pat, o, fill, base, cm, r, w, n=128):
        step([("G", lambda: g.affine_select(out, a, pat, o, fill, base, cm), 170 + 2 * CYC * n)], r, w)

    def bk(k):
        return T["B%d" % k]

    p = pl[me]
    send, total = sender(g, core, T, topo)
    e_on = topo.engines(core, p["E"])
    n_on, n_off = len(e_on), len(topo.engines(core, pl[p["to"][0]]["core"]))

    wme = blk(T.WL, me, 5)
    dma(wme, T.w[:], "dW", 16, "", "wme", 20)
    for i in range(len(WIDE)):
        dma(piece(T.VA, me, i, 0, 2), piece(T.val, 0, i, 0, 2), "dV%d" % i, 16, "", "Vme%d" % i, sum(WIDE[i]) // 4)
        if i == PRI:
            dma(T.PI[:], T.pri[:], "dP", 16, "", "PI", 192)

    def table(k, r):
        dma(blk(T.TI, k, C), [T.key, T.nxt, T.prv, T.rw][k][:], "dT%d" % k, 16, r, "TI%d" % k, 192)
    for k in (1, 2, 3, 0)[:AHEAD]:
        table(k, "")
    pc = T.ci[:, 7:8]
    early[0] = True
    iota(pc, [[0, 1]], 0, 1, "pc", 1)
    iota(T.OB[:], [[16, 8], [0, 16]], 0, 0, "OB", 128)
    iota(T.XF[:], [[1, 192]], -32, 0, "XF", 192)
    iota(T.cf[:, 6:7], [[1, 1]], 0, 1, "cp", 1)
    iota(T.D4[:], [[4, 32], [0, 4]], 0, 0, "D4", 128)
    step([("G", lambda: send([(wme, [wme] * 2, [p["E"], p["O"]], e_on, "aw")]), 1300)],
         "wme", "WL", 4500, ("aw", n_on + 5 * n_off))

    def hand_on(i):
        trs = [(piece(T.VA, me, i, h), [piece(T.VA, me, i, h)], [p["EO"[h]]], e_on[n_on // 2 * h:n_on // 2 * (h + 1)],
                "ah%d" % i) for h in range(2)]
        for call in [trs] if WIDE[i][0] == WIDE[i][1] else [trs[1:], trs[:1]]:
            send(call)
    nw = len(WIDE)
    mine = " ".join("Vme%d" % i for i in range(nw))
    for i in range(nw - 1):
        step([("G", lambda i=i: hand_on(i), 300 + 300 * (WIDE[i][0] != WIDE[i][1]))], "Vme%d" % i, "+gone", 1500,
             ("loc", (nw + 1) * n_on))
    step([("G", lambda: hand_on(nw - 1), 600)], mine, "VA", 16000, ("av", nw * (8 * (n_on - n_off) + 6 * n_on)))
    step([("G", lambda: g.sem_inc(T.sem.out, 1), 10)], mine + " wme", "issued", 0, ("out", 1))
    early[0] = False
    for k in (1, 2, 3, 0)[AHEAD:]:
        table(k, "issued")
    for j, at in enumerate((8, 9, 12, 13, 14, 15) if DUP == 2 else ()):
        dma(T.TB[at:128:16, :], T.VA[16 * j:16 * j + 24, V * me:V * me + V], "dR", 256, mine, "+TBr", 70)
    if XA:
        dma(blk(T.XS, 0, F // 2), blk(T.x, 0, F // 2), "dX", 32, "gone", "+XS", 768)

    if GS & 1:
        for lo, hi, a in ((0, 4, 4), (4, 6, 5), (6, 8, 0), (8, 12, 5), (12, 16, 5)):
            scaled(T.LB[0:1, lo:hi], T.XF[0:1, 32:32 + hi - lo], a / 1024, "XF", "+LB", 64)
        for n in (16, 32, 64):
            scaled(T.LB[0:1, n:2 * n], T.LB[0:1, 0:n], 1.0, "LB", "LB", 64)
    else:
        iota(T.LB[0:1, :], [[0, 32], [5, 4]], 0, 0, "LB", 128)
        for m in (1, 2, 3, 6, 7):
            iota(T.LB[0:1, m:128:16], [[0, 8]], 4 * m * (m < 4), 0, "+LB", 8)
        scaled(T.LB[0:1, :], T.LB[0:1, :], 1.0 / 1024, "LB", "LB")
    if GS & 2:
        scaled(T.RAMP[0:1, 0:16], T.XF[0:1, 33:49], float(GAP), "XF", "RAMP", 64)
        for n in (16, 32, 64, 128, 256):
            scaled(T.RAMP[0:1, n:min(2 * n, C)], T.RAMP[0:1, 0:min(n, C - n)], 1.0, "RAMP", "RAMP", min(n, 128))
    else:
        iota(T.RAMP[0:1, :], [[0, 24], [GAP, 16]], GAP, 0, "RAMP", C)
    iota(T.CR[:], [[4, C]], 4 - 768, 0, "CR", C)
    early[0] = FIRST
    for k, (m, s) in enumerate(((112, 0), (15, 0), (124, 0), (3, 0), (14, 1), (7, 0))):
        ts(T.ci[:, k:k + 1], pc, m, A.bitwise_and, "pc", "ci%d" % k, s, A.logical_shift_right)
    cp(T.cf[:, 0:1], T.ci[:, 0:1], "ci0", "cg")
    cp(T.cf[:, 1:6], T.ci[:, 1:6], "ci1 ci2 ci3 ci4 ci5 cg", "cf")
    cgb, ca, cq4, cr, ca2, cq, cpp, cp1 = [T.cf[:, k:k + 1] for k in range(8)]
    x4, x128 = T.XF[:, 32:36], T.XF[:, 32:160]
    oh = [T.OH[:, k:k + 1] for k in range(16)]
    cm = [T.cm[:, k:k + 1] for k in range(16)]
    ts(T.OH[:], T.XF[:, 32:48], ca, A.is_equal, "XF cf", "OH")
    ts(T.BH[:], T.OB[:], cgb, A.is_equal, "OB cg", "BH")
    ts(T.B15[:], T.XF[:, 17:161], cgb, A.is_equal, "XF cg", "B15", n=72)
    early[0] = False
    line(cm[0], oh[15], -1.0, 1.0, "OH", "cm0")
    ms(T.NEG[:], -1024.0, "NEG", 192)

    early[0] = True
    ms(T.ZZ[:, 0:ZN], 0.0, "ZZ", ZN // 2)
    for k in range(0 if DUP else FILL):
        sc(blk(T.TB, k, 512), T.ZZ[:, 0:512], "ZZ", "+TBb", n=512)
    early[0] = False
    for k in range(12 if DUP else FILL, 12):
        step([("V", lambda k=k: vec.memset(blk(T.TB, k, 512), 0.0), cost(256))], AFTER, "+TBb")

    def zero(out, n, w):
        step([("V", lambda: vec.memset(out, 0.0), cost(n // 2)), sc_alt(out, T.ZZ[:, 0:n], n=n)], "ZZ", w)

    def digits(k):
        b = k % 2
        if k in PELO:
            mm([(bk(b)[:, 0:C], T.I32[:], blk(T.TF, k, C), True, False)], "I32 TF%d" % k, "B%d" % b, 4 * C)
            sc(blk(T.DG, 2 * k, C), blk(T.TF, k, C), "TF%d" % k, "DG%d" % (2 * k), n=C)
            mm([(bk(b)[:, 0:C], T.NI[:], blk(T.DG, 2 * k, C), False, True)], "NI DG%d" % (2 * k), "B%d" % b, C)
            sc(blk(T.DG, 2 * k + 1, C), bk(b)[:, 0:C], "B%d" % b, "DG%d" % (2 * k + 1), n=C)
        else:
            split(k, b)
        for a in (2 * k, 2 * k + 1):
            for at in (a, a + 8) if DUP == 1 or k == 1 else (a,):
                dma(T.TB[at:128:16, :], blk(T.DG, a, C), "dR", 256 if DUP else 160, "DG%d TBb" % a, "+TBr", 96)

    def split(k, b):
        ts(bk(b)[:, 0:C], blk(T.TI, k, C), LIFT[k], A.add, "TI%d" % k, "B%d" % b, n=C)
        sc(blk(T.DG, 2 * k, C), bk(b)[:, 0:C], "B%d" % b, "DG%d" % (2 * k), n=C)
        tt(blk(T.DG, 2 * k + 1, C), bk(b)[:, 0:C], blk(T.DG, 2 * k, C), A.subtract,
           "B%d DG%d" % (b, 2 * k), "DG%d" % (2 * k + 1), C)

    ts(T.NI[:], x128, cpp, A.is_equal, "XF cp", "NI", -1.0, A.mult)
    if PELO:
        scaled(T.I32[:], T.NI[:], -1.0, "NI", "I32", 256)

    ms(T.PH[:, 0:16], 128.0, "PHp")
    ms(T.L8[0:1, :], 1.0 / 128, "L8")
    scaled(T.BM[:], T.BH[:], 1.0 / 256, "BH", "BM0")
    ts(T.TG[:], x128, cpp, A.is_ge, "XF cp", "TG")
    tt(T.TRa[:], T.TG[:], T.BM[:], A.mult, "TG BM0", "TRa", 256)
    tt(T.TRb[:], T.BM[:], T.TRa[:], A.subtract, "TRa BM0", "TRb", 256)
    ts(T.PH[:, 16:], T.PI[:], 128.0, A.add, "PI", "PHa PHb", n=C)

    scaled(T.KK[:, :, 0:16], T.NEG[:, 0:32], 2.0, "NEG", "KKp", 64)
    scaled(T.R15[:], T.BH[:], oh[15], "BH OH", "R15")
    ms(T.LS[0:1, :], 0.0, "LS")
    ms(T.LS[0:1, 7:128:16], 1.0, "LS")
    scaled(T.LA2[:], T.R15[:], -5.0, "R15", "LA2")
    line(cm[9], cpp, 1.0, 1.0, "cp", "cm9")
    ts(T.SH[:], T.D4[:], cm[9], A.is_equal, "D4 cm9 cm0", "SH", cm[0], A.mult)
    ts(T.QM[:], T.D4[:], cq4, A.is_equal, "D4 cf", "QM")
    tt(T.LA1[:], T.QM[:], T.SH[:], A.add, "QM SH", "LA1", 256)
    for lo, hi, a1, a2 in ((1, 4, 4.0, None), (0, 4, None, -4.0), (6, 7, 4.0, -4.0), (7, 8, -32768.0, 32768.0)):
        for t, a in (("LA1", a1), ("LA2", a2)):
            if a is not None:
                scaled(T[t][:, :, lo:hi], T.R15[:, :, lo:hi], a, "R15", "+" + t, 64)
    scaled(T.EK[:], T.B15[:], oh[15], "B15 OH", "EK", 144)
    scaled(T.EZ[:], T.B15[:], oh[7], "B15 OH", "EZ", 144)
    line(cm[1], oh[7], 32768.0, 4.0, "OH", "cm1")
    ts(cm[6], ca, 3.5, A.is_lt, "cf OH", "cm6", oh[0], A.subtract)
    line(cm[2], oh[6], 1.0, cm[6], "cm6 OH", "cm2")
    line(cm[3], oh[6], -2.0, cr, "OH cf", "cm3")
    ts(cm[4], cm[2], oh[7], A.add, "cm2 OH", "cm4", -1.0, A.add)
    line(cm[5], cm[3], 1.0, cgb, "cm3 cf", "cm5")
    for k in range(4):
        if k < WG:
            iota(blk(T.W, k, ZONE // 2), [[0, ZONE // 2]], 0, 0, "+W" if k > 1 else "+Wz", ZONE // 2)
        else:
            zero(blk(T.W, k, ZONE // 2), ZONE // 2, "+W" if k > 1 else "+Wz")
    sc(T.CT[:], T.CR[:], "CR cm2 cm4", "CT", cm[2], AF.Identity, cm[4], C)

    ts(T.Mle[:], x4, cm[3], A.is_ge, "XF cm3", "Mle")
    ts(T.Mgt[:], x4, cm[3], A.is_lt, "XF cm3", "Mgt")
    ts(T.ET[:], T.XF[:, 17:177], cm[5], A.is_equal, "XF cm5", "ET", n=80)
    ts(T.M4[:], T.XF[:, 32:40], ca2, A.is_equal, "XF cf", "M4")
    ts(cm[10], ca, 7.5, A.is_lt, "cf", "cm10")
    for s in range(3):
        scaled(blk(T.ES, 2 * s, 128), T.ET[:, s:s + 128], T.Mle[:, s:s + 1], "ET Mle", "+ES")
        scaled(blk(T.ES, 2 * s + 1, 128), T.ET[:, 16 + s:144 + s], T.Mgt[:, s:s + 1], "ET Mgt", "+ES")
    for k in (1, 2):
        scaled(blk(T.EF, k, 144), T.B15[:], T.M4[:, k:k + 1], "B15 M4", "EF%d" % k, 144)
    ts(blk(T.EF, 0, 144), T.B15[:], T.M4[:, 0:1], A.mult, "B15 M4", "EF0", 1.0 / V, A.mult, 72)

    line(cm[7], oh[7], 8.0, cq4, "OH cf", "cm7")
    ts(cm[8], oh[7], cr, A.add, "OH cf", "cm8", 2048.0, A.add)
    scaled(T.SH[:, 7:128:16], T.BH[:, 7:128:16], oh[11], "BH OH", "SH", 64)
    select(T.LE2[:], T.R15[:], [[0, 8], [-1, 16]], A.is_ge, 0.0, 3, 0, "R15", "LE2")
    scaled(T.LE3[:], T.R15[:], -2.0, "R15", "LE3")
    scaled(T.I64[:], T.BH[:], -64.0, "BH", "I64")
    select(T.S64[:], T.I64[:], [[1, 128]], A.is_equal, 0.0, -1, -1, "I64", "S64")
    select(T.Dp[:], T.S64[:], [[1, 128]], A.not_equal, 64.0, 0, -1, "S64", "Dp")
    select(T.D15[:], T.I64[:], [[1, 128]], A.is_equal, 0.0, 15, -1, "I64", "D15")
    ts(T.LQ[:], T.D4[:], cm[7], A.is_equal, "D4 cm7", "LQ")
    ms(T.LC[0:32, :], -2.0 ** -9, "+LC")
    ms(T.LC[32:64, :], 15 * 2.0 ** -20, "+LC")
    scaled(T.BR[:], T.BH[:], T.M4[:, 3:4], "BH M4", "BR")
    for m, src in (("LR", "BR"), ("LE", "BH")):
        for s in range(5):
            pat, at = ([[0, 32], [1, 4]], s) if s < 4 else ([[0, 8], [1, 16]], 7)
            select(blk(T[m], s, 128), T[src][:], pat, A.is_equal, 0.0, -at, 0, src, m + str(s))
        iota(T[m][:, 3 * 128 + 7:4 * 128:16], [[0, 8]], 0, 0, m + "3", 8)
    for t in ("GN2", "PR"):
        scaled(T[t][:, K:], T.ZZ[:, 0:16], 1.0, "ZZ", t + "p", 64)
    scaled(T.EN[:], T.B15[:], T.M4[:, 5:6], "B15 M4", "EN", 144)
    zero(T.AE[:, 512:], 8, "AEp")
    sc(T.WF[:], T.WL[:], "WL wme", "WF", -1.0)
    for d in (2, 3, 1, 4, 0):
        for q in range(N):
            o, j = blk(T.DI, 8 * d + q, 128), 5 * q + d
            step([ts_alt(o, T.NI[:], T.WL[:, j:j + 1], A.mult, -1.0, A.mult), sc_alt(o, T.NI[:], T.WF[:, j:j + 1], n=128)][:1 + (d in DS)],
                 "NI WF WL wme", "+DI%d" % d)

    src_of = {"G0": "TB oT", "GN1": "TB oN1", "GP1": "TB oP1", "GN2": "TB oN2", "X0": "XS oP2", "X1": "XS oP1",
              "X2": "XS oT", "X3": "XS oN1", "X4": "XS oN2", "VG": "VA oK"}
    also = {"TB": "TBr", "XS": "XS", "VA": "VA " + mine}
    hbank, ebank = (4, 5, 2), (6, 7, 3)
    seen = {}

    def span(name, lo, hi):
        return " ".join(name + str(j) for j in range(lo // 256, hi // 256))

    def turn(k, n):
        seen[k] = seen.get(k, 0) + 1
        return seen[k] % n == 1, seen[k] % n == 0

    def upto(name, h):
        return " ".join(name + str(j) for j in range(h + 1))

    def listed(b, k, src, name, what):
        terms = [("EN", 0, "EN", src)] if src == "GN1" else [("EF", 144 * k, "EF%d" % k, src)]
        for j, (m, at, mk, x) in enumerate(terms):
            if what == "f":
                mm(group(bk(b)[:, 0:64], [(T[m][:, at + 15 - u:at + 143 - u], T[x][:, u:K:16]) for u in range(16)],
                         j == 0, j == len(terms) - 1), span(x, 0, K) + " " + mk, "B%d" % b, 1024)
        if what == "f":
            return
        if k:
            ts(T[name][:], bk(b)[:, 0:64], -LIFT[k], A.add, "B%d" % b, name)
        else:
            ts(T[name][:], bk(b)[:, 0:64], cq, A.add, "B%d cf" % b, name, float(V), A.mult)

    def gather(name, lo, hi):
        win, off = src_of[name].split()
        o, a, c = T[name][:, lo:hi], T[win][:].indirect(T[off][:, lo // 16:hi // 16]), GAT * CYC * (hi - lo)
        r, w = also[win] + " " + off, span(name, lo, hi)
        if name in ("GN1", "GN2"):
            old = {"GN1": "G0", "GN2": "GN1"}[name]
            return tt(o, a, T[old][:, lo:hi], A.add, r + " " + span(old, lo, hi), w, c / CYC + 25)
        if name == "G0":
            return step([ts_alt(o, a, cm[10], A.mult, n=c / CYC + 25), sc_alt(o, a, cm[10], n=c / CYC + 40)], r + " cm10", w)
        step([("V", lambda: vec.tensor_copy(o, a), 50 + c), ("S", lambda: act.activation(o, a, AF.Copy), 65 + c)], r, w)
        for at in range(lo, hi, 512) if win == "XS" else ():
            weigh(name, at)

    def weigh(name, lo):
        d, b = int(name[1]), 4 + lo // 512

        def items():
            first, last = turn(b, 5)
            return [(bk(b)[:, q:512:8], blk(T.DI, 8 * d + q, 128), T[name][:, lo + q:lo + 512:8], first and q == 0,
                     last and q == 7) for q in range(N)]
        mm(items, span(name, lo, lo + 512) + " DI%d" % d, "+B%d" % b, 512)

    def ecol(k):
        return min(max(k // 2 - 2, 0), 512) if k < K else 512

    def esum(name, c, k0, k1):
        lo, hi, b, m = ecol(k0), ecol(k1), ebank[c], "LE" if name == "PR" else "LR"
        mm(lambda: group(bk(b)[:, 0:hi - lo], [(blk(T[m], s, 128), T[name][:, 2 * lo + s:2 * hi + s:2]) for s in range(5)],
                         *turn(b + 10, 2)),
           upto(m, 4) + " " + span(name, 0, k1) + " " + name + "p", "+B%d" % b, 5 * (hi - lo))

    def lay(rd, at):
        for k, a in zip((1, 2, 3, 0), POSA):
            if rd == 0 and a == at and k in PELO:
                ts(blk(T.TF, k, C), blk(T.TI, k, C), LIFT[k], A.add, "TI%d" % k, "TF%d" % k, n=C)
        for k, a in zip((1, 2, 3, 0), POS):
            if rd == 0 and a == at:
                digits(k)

    def sample(rd, lo, hi, ab, bs, ba, bw):
        n, base, of = hi - lo, 16 + ZONE * (1 - rd), T.OF[:, 48 * rd + lo // 8:48 * rd + hi // 8]
        f, b = T.KK[:, 0, 16 + lo:16 + hi], T.KK[:, 0, 15 + lo:15 + hi]
        ph, kk, kh, cc = [" ".join(t + x for x in ab) for t in ("PH", "KF", "KH", "CC")]
        mm([(bk(bs)[:, 0:n], T.L8[0:1, :], T.NEG[0:1, 0:n], True, False)], "L8 NEG", "B%d" % bs, n)
        for x in ab:
            c0, c1 = (max(lo, CUT), hi) if x == "b" else (lo, CUT)
            mm(group(bk(bs)[:, c0 - lo:c1 - lo], [(T.TRa[:], T.PH[:, 16 + c0:16 + c1]), (T.TRb[:], T.PH[:, 15 + c0:15 + c1])],
                     False, x == ab[-1]), "TRa TRb PHa PHp PH" + x, "B%d" % bs, 2 * (c1 - c0))
        lay(rd, 0)
        mm(group(bk(ba)[:, 0:n], [(T.LB[0:1, :], T.NEG[0:1, 0:n]), (T.LS[0:1, :], T.RAMP[0:1, 0:n])], True, False),
           "LB LS NEG RAMP", "B%d" % ba, 2 * n)
        out, init = T.SF[:, 0:n] if hi < C else f, T.SF[:, lo - 1:lo] if lo else -2048.498046875
        step([("V", lambda: vec.tensor_tensor_scan(out, bk(bs)[:, 0:n], T.NEG[:, 0:n], init, A.add, A.min), cost(n))],
             "B%d NEG" % bs + " SF" * (lo > 0), "SF" if hi < C else kk)
        if hi < C:
            step([("V", lambda: vec.tensor_copy(f, out), cost(n)), sc_alt(f, out, n=n)], "SF", kk)
        lay(rd, 1)
        mm(group(bk(ba)[:, 0:n], [(T.LA1[:], f), (T.LA2[:], b)], False, True), "LA1 LA2 KFa KKp " + kk, "B%d" % ba, 2 * n)
        ts(T.KK[:, 1, 16 + lo:16 + hi], f, 0.5, A.mult, kk, kh, -1024.25, A.add, n // 2)
        mm(group(bk(bw)[:, 0:n // 8], [(T.EK[:, 15 - u:143 - u], T.KK[:, :, 15 + lo + u:15 + hi:16]) for u in range(16)],
                 True, False), "EK KFa KHa KKp %s %s" % (kk, kh), "B%d" % bw, 1024)
        ts(T.CC[:, lo:hi], bk(ba)[:, 0:n], 0.0, A.max, "B%d cm1" % ba, cc, cm[1], A.min, n)
        lay(rd, 2)
        mm(group(bk(bw)[:, 0:n // 16], [(T.EZ[:, 15 - u:143 - u], T.CC[:, lo + u:hi:16]) for u in range(16)], False, True),
           "EZ " + cc, "B%d" % bw, 1024)
        ts(of, bk(bw)[:, 0:n // 8], 2048.0, A.add, "B%d" % bw, "OF%d%s" % (rd, ab[0]))
        tt(T.W[:, base:].indirect(T.OF[:, 48 * rd + lo // 8:48 * rd + lo // 8 + n // 16]), T.CC[:, lo:hi], T.CT[:, lo:hi],
           A.mult, "CT OF%d%s %s" % (rd, ab[0], cc) + " Wz" * rd, "W", SCA * n)
        lay(rd, 3)

    kf, kb, hb = T.KK[:, 0, 16:], T.KK[:, 0, 15:15 + C], T.KK[:, 1, 15:15 + C]
    for rd in range(2):
        base = 16 + ZONE * (1 - rd)
        early[0] = True
        ech = ECH[rd]
        parts = ((0, CUT), (CUT, C))
        if rd == 1 and SPLIT:
            sample(rd, CUT, C, "b", 4, 5, 2)
        else:
            sample(rd, 0, C, "ab", 4, 5, 2)
        if rd == 0:
            if not XA:
                dma(blk(T.XS, 0, F // 2), blk(T.x, 0, F // 2), "dX", 32, "gone", "+XS", 768)
            dma(blk(T.XS, 1, F // 2), blk(T.x, 1, F // 2), "dX", 32, "", "+XS", 768)
        pairs = [(T.ET[:, 15 - u:143 - u], T.W[:, base + u:base + K:16]) for u in range(13)]
        for s in range(3):
            pairs.append((blk(T.ES, 2 * s, 128), T.W[:, base + 15 - s:base + K:16]))
            pairs.append((blk(T.ES, 2 * s + 1, 128), T.W[:, base - 1 - s:base + K - 16:16]))
        mm(group(T.B3[:, 0:64], pairs), "ET ES W", "B3", 19 * 64)
        ts(T.oT[:], T.B3[:, 0:64], 3072.0, A.add, "B3", "oT")
        lists = {"N1": (2, 1, "G0"), "P1": (3, 2, "G0"), "K": (3, 0, "G0"), "N2": (2, 1, "GN1"), "P2": (3, 2, "GP1")}
        def marks():
            mm(group(T.B6[:, 0:C], [(T.SH[:], kf), (T.LE2[:], kb), (T.LE3[:], hb)]), "SH LE2 LE3 KFa KFb KHa KHb KKp", "B6",
               3 * C)
            mm(group(T.B7[:, 0:C], [(T.NI[:], T.PH[:, 16:]), (T.Dp[:], kf), (T.D15[:], kb)]),
               "NI Dp D15 PHa PHb KFa KFb KKp", "B7", 3 * C)
            if rd == 0 and MV & 1:
                ts(T.CAP[:], T.B6[:, 0:C], cm[8], A.is_equal, "B6 cm8", "CAP", 63.0, A.mult, C)
            else:
                sc(T.T1[:], T.B6[:, 0:C], "B6 cm8", "T1", -1.0, AF.Abs, cm[8], C)
                sc(T.CAP[:], T.T1[:], "T1", "CAP", -63.0, AF.Relu, 63.0, C)
            if rd == 0 and MV & 2:
                ts(T.ZO[:], T.B7[:, 0:C], -1.0, A.mult, "B7", "ZO", 129.0, A.max, C)
            else:
                sc(T.Z1[:], T.B7[:, 0:C], "B7", "Z1", -1.0, AF.Relu, -129.0, C)
                sc(T.ZO[:], T.Z1[:], "Z1", "ZO", 1.0, AF.Identity, 129.0, C)
            for h, (lo, hi) in enumerate(parts):
                mm(group(bk(h)[:, 0:hi - lo], [(T.LC[0:64, :], T.NEG[0:64, lo:hi]), (T.Dp[:], T.KK[:, 0, 16 + lo:16 + hi]),
                                               (T.D15[:], T.KK[:, 0, 15 + lo:15 + hi])], True, False),
                   "LC NEG Dp D15 KFa KFb KKp", "B%d" % h, 3 * (hi - lo))

        for it in ORDER[rd].split():
            a, rest = it[0], it[1:]
            pin[0] = a if a in "VS" else "V" if a in "tPN" and PIN[rd] else "S" if a == "A" and PIN[rd] else None
            if a in "VS-":
                lo, hi = {"a": (0, 512), "b": (512, K), "c": (512, 768), "d": (768, K), "w": (0, K)}[rest[-1]]
                gather(rest[:-1], lo, hi)
            elif a in "ft":
                listed(*lists[rest], "o" + rest, a)
            elif a == "M":
                marks()
            elif a in "EPA":
                c = int(rest)
                lo, hi = ech[c], ech[c + 1]
                if a == "P":
                    tt(T.PR[:, lo:hi], bk(4 + lo // 512)[:, lo % 512:lo % 512 + hi - lo], T.VG[:, lo:hi], A.mult,
                       "B%d " % (4 + lo // 512) + span("VG", lo, hi), span("PR", lo, hi), hi - lo)
                if a == "A":
                    n = ecol(hi) - ecol(lo)
                    sc(T.AE[:, ecol(lo):ecol(hi)], bk(ebank[c])[:, 0:n], "B%d" % ebank[c], "AE%d" % c, 1.0 / 16, AF.Abs,
                       -3 * LIFT[3] / 16, n)
                else:
                    esum("GN2" if a == "E" else "PR", c, lo, hi)
            else:
                h = int(rest[1])
                lo, hi = parts[h]
                ab, win = "ab"[h], T.AE[:] if h else T.AE[:, 0:ecol(ech[-2])]
                if rest[0] == "g":
                    at = 48 + (hi + lo) // 16 if rd == 1 and SPLIT else 48 * rd + 24 + lo // 16
                    tt(T.GG[:, lo:hi], win.indirect(T.OF[:, at:at + (hi - lo) // 16]), T.CAP[:, lo:hi], A.min,
                       upto("AE", 1 + h) + " OF%da OF%db CAP" % (rd, rd) + " AEp" * h, "GG" + ab, GAT * (hi - lo))
                    mm([(bk(h)[:, 0:hi - lo], T.LQ[:], T.GG[:, lo:hi], False, True)], "LQ GG" + ab, "B%d" % h, hi - lo)
                    continue
                tt(T.PH[:, 16 + lo:16 + hi], bk(h)[:, 0:hi - lo], T.ZO[:, lo:hi], A.max, "B%d ZO" % h, "PH" + ab, hi - lo)
                pin[0] = None
                if rd == 0 and h == 0 and SPLIT:
                    sample(1, 0, CUT, "a", 0, 4, 6)
                if rd == 1:
                    sc(T.YO[:, lo:hi], T.PH[:, 16 + lo:16 + hi], "PH" + ab, "YO" + ab, 1.0, AF.Identity, -128.0, hi - lo)
                    dma(T.y[:, lo:hi], T.YO[:, lo:hi], "dY", 32, "YO" + ab, "y" + ab, 100)
        pin[0] = None
    cnt, wait = issue(steps, Q, T)
    wait("G", "loc", total[0])
    for e in "VSPG":
        wait("Y", "c" + e, cnt[e])
    wait("Y", "dY", 32)
